import numpy as np, ml_dtypes
CORES = [2,3,42,43,82,83,122,123]
N = 8
BF = ml_dtypes.bfloat16
L, F, M, Q, S, R, C, P = 1024, 512, 512, 4, 3, 2, 128, 8
A, ND, W = L + F, Q * M, L + F + Q * M
def pull(y, ix):
    return np.take_along_axis(y, ix[:, :, None, :], 3)
def evaluate(y, kd, om):
    for l in range(Q):
        i = l * M
        a = pull(y, kd[:, :, i:i + M]); b = pull(y, kd[:, :, ND + i:ND + i + M])
        y[..., A + i:A + i + M] = np.where(om[:, :, None, i:i + M] == 1, np.maximum(a, b), np.minimum(a + b, 255))
def begin(v, kd, om):
    y = np.zeros((N, 8, 16, W), np.int64); y[..., :A] = v
    evaluate(y, kd, om)
    return y
def values(rng, lo, hi):
    return (rng.random((N, 8, 16, A)) * np.exp2(rng.integers(lo, hi + 1, (N, 8, 1, A)))).astype(np.int64)
def kids(rng, near, other):
    k = np.zeros((N, 8, 2, Q, M), np.int64); sh = (N, 8, 2, M)
    for l in range(Q):
        c = rng.random(sh)
        x = rng.integers(A + max(l - 1, 0) * M, A + max(l, 1) * M, sh); z = rng.integers(0, A + l * M, sh); e = rng.integers(0, A, sh)
        k[:, :, :, l] = np.where((c < near) & (l > 0), x, np.where(c < near + other, z, e))
    return k
def aims(rng, v, k, o, share):
    y = begin(v, k.reshape(N, 8, 2 * ND), o)[..., W - M:]
    e = rng.random((N, 8, 1, M)); close = np.clip(y + rng.integers(-20, 21, y.shape), 0, 255)
    far = (rng.random(y.shape) * np.exp2(rng.integers(4, 9, (N, 8, 1, M)))).astype(np.int64)
    return np.where(e < share, y, np.where(e < share + (1 - share) * 0.5, close, far))
def ops(rng, share):
    return (rng.random((N, 8, ND)) < share).astype(np.int64)
def weights(rng, share):
    return (rng.random((N, 8, 16, 2)) < share).astype(np.int64)
def pack(v, k, o, g, w):
    return {"lv": np.ascontiguousarray(v.reshape(N, 128, A)).astype(np.float32).astype(BF), "kid": np.ascontiguousarray(k.reshape(N, 8, 2 * ND)).astype(np.int32),
            "mx": np.ascontiguousarray(o).astype(np.int32), "tg": np.ascontiguousarray(g.reshape(N, 128, M)).astype(np.float32).astype(BF),
            "wt": np.ascontiguousarray(w.reshape(N, 128, 2)).astype(np.int32)}
def setup_inputs(rng):
    v = values(rng, 4, 8); k = kids(rng, 0.5, 0.25); o = ops(rng, 0.4)
    return pack(v, k, o, aims(rng, v, k, o, rng.choice(np.array([0.2, 0.5, 0.8, 0.97]), (N, 8, 1, 1))), weights(rng, 0.6))
def setup_inputs_room(rng):
    v = rng.integers(1, 128, (N, 8, 16, A)); v[..., L:L + 2] = 0; v[:, :, 0, L + 1] = 1
    k = kids(rng, 0.5, 0.25); o = ops(rng, 0.4); w = weights(rng, 0.6)
    k[:, :, :, Q - 1] = rng.integers(0, A, (N, 8, 2, M)); o[:, :, ND - M:] = 0
    g = pull(v, k[:, :, 0, Q - 1]) + pull(v, k[:, :, 1, Q - 1])
    for q in range(N):
        for j in range(8):
            n = int(rng.choice(np.array([0, 1, C - 1, C, C + 1, M])))
            if q == 0: n = (C, C + 1, M, C - 1, 1, 0, C, C + 1)[j]
            at = np.arange(M - n, M) if q == 0 and j < 4 else rng.permutation(M)[:n]
            k[q, j, :, Q - 1, at] = L; g[q, j, :, at] = rng.integers(128, 256, (n, 16))
    k[0, 0:4:3, 1, Q - 1, M - 1] = L + 1; o[0, 0:4:3, ND - 1] = 1
    return pack(v, k, o, g, w)
def setup_inputs_ties(rng):
    few = np.array([0, 1, 2, 127, 128, 254, 255]); pal = rng.choice(few, (N, 8, 16, 6)).astype(np.int64)
    v = pull(pal, rng.integers(0, 6, (N, 8, A))); k = kids(rng, 0.4, 0.2)
    k[:, :, 1] = np.where(rng.random((N, 8, Q, M)) < 0.3, k[:, :, 0], k[:, :, 1])
    g = np.where(rng.random((N, 8, 1, M)) < 0.5, pull(pal, rng.integers(0, 6, (N, 8, M))), rng.choice(few, (N, 8, 16, M)))
    return pack(v, k, ops(rng, 0.5), g, weights(rng, 0.5))
def setup_inputs_meet(rng):
    v = values(rng, 3, 6); k = kids(rng, 0.5, 0.25)
    for l in range(1, Q):
        some = rng.integers(0, M, (N, 8, 8))
        k[:, :, :, l] = A + (l - 1) * M + np.take_along_axis(some, rng.integers(0, 8, (N, 8, 2 * M)), 2).reshape(N, 8, 2, M)
    k[:, 1::2, :, Q - 1] = k[:, 1::2, :, Q - 1, :1]
    return pack(v, k, ops(rng, 0.7), rng.integers(0, 256, (N, 8, 16, M)), weights(rng, 0.6))
def setup_inputs_ends(rng):
    v = np.where(rng.random((N, 8, 16, A)) < rng.random((N, 8, 1, A)), 255, 0)
    k = kids(rng, 1.0, 0.0); o = ops(rng, 0.5); w = weights(rng, 0.6); w[:, 0::4] = 1; w[:, 1::4] = 0
    for l in range(Q):
        c = [0, L - 1, L, A - 1] + ([A, A + (l - 1) * M, A + l * M - 1] if l else [])
        k[:, 0::2, :, l] = rng.choice(np.array(c), (N, 4, 2, M))
    g = np.where(rng.random((N, 8, 16, M)) < rng.random((N, 8, 1, M)), 255, 0)
    g[..., 0] = 255; g[..., M - 1] = 255; g[..., 1] = 0
    o[..., ND - M] = 1
    for j in (0, 4, 6):
        k[:, j, :, Q - 1, 0] = 0; v[:, j, :, 0] = 0; v[:, j, 0, 1:L] = 255
    w[:, 4] = 1; w[:, 4, 15, 0] = 0; g[:, 4, 15, 0] = 111
    w[:, 6] = 1; w[:, 6, 15, 0] = 0; v[:, 6, :, 1:L] = rng.integers(0, 5, (N, 16, L - 1)); v[:, 6, 0, 1:L] = rng.integers(1, 5, (N, L - 1))
    return pack(v, k, o, g, w)
def setup_inputs_spread(rng):
    v = (rng.random((N, 8, 16, A)) * np.exp2(8 * rng.random((N, 8, 1, A)))).astype(np.int64) * (rng.random((N, 8, 1, A)) > 0.0625)
    near = rng.random((N, 8, 1, 1)); k = kids(rng, near, (1 - near) * rng.random((N, 8, 1, 1))); o = ops(rng, rng.random((N, 8, 1)))
    return pack(v, k, o, aims(rng, v, k, o, rng.random((N, 8, 1, 1))), weights(rng, rng.random((N, 8, 1, 2))))
def check_inputs(d):
    bad = []
    for nm in ("lv", "tg"):
        x = d[nm].astype(np.float32)
        if not (np.min(x) >= 0 and np.max(x) <= 255): bad.append("range of " + nm)
        if np.any(x != np.floor(x)): bad.append("whole numbers in " + nm)
    for nm in ("mx", "wt"):
        if np.min(d[nm]) < 0 or np.max(d[nm]) > 1: bad.append("range of " + nm)
    k = d["kid"].reshape(N, 8, 2, Q, M)
    for l in range(Q):
        if np.min(k[:, :, :, l]) < 0 or np.max(k[:, :, :, l]) >= A + l * M: bad.append("range of kid in level " + str(l))
    return bad
def reference(lv, kid, mx, tg, wt):
    kd = kid.astype(np.int64); om = mx.astype(np.int64)
    y = begin(lv.astype(np.float32).astype(np.int64).reshape(N, 8, 16, A), kd, om)
    goal = tg.astype(np.float32).astype(np.int64).reshape(N, 8, 16, M); w = wt.astype(np.int64).reshape(N, 8, 16, 2)
    for rnd in range(R):
        node = np.tile(ND - M + np.arange(M), (N, 8, 1)); live = np.ones((N, 8, M), bool); want = goal
        par = np.zeros((N, 8, M), np.int64); side = np.zeros((N, 8, M), np.int64); child = np.zeros((N, 8, M), np.int64); err = np.zeros((N, 8, M), np.int64)
        for step in range(S):
            ka = np.take_along_axis(kd, node, 2); kb = np.take_along_axis(kd, node + ND, 2); o = np.take_along_axis(om, node, 2)[:, :, None, :] == 1
            ya = pull(y, ka); yb = pull(y, kb)
            wa = np.where(o, np.where(want >= yb, want, 0), np.maximum(want - yb, 0))
            wb = np.where(o, np.where(want >= ya, want, 0), np.maximum(want - ya, 0))
            ea = np.add.reduce(np.abs(wa - ya), axis=2); eb = np.add.reduce(np.abs(wb - yb), axis=2)
            tob = eb < ea
            par = np.where(live, node, par); side = np.where(live, tob, side); child = np.where(live, np.where(tob, kb, ka), child); err = np.where(live, np.where(tob, eb, ea), err)
            want = np.where(live[:, :, None, :], np.where(tob[:, :, None, :], wb, wa), want)
            live = live & (child >= A); node = np.where(live, child - A, 0)
        u1 = np.add.reduce(w[..., 0:1] * want, axis=2); u2 = np.add.reduce(w[..., 1:2] * want, axis=2)
        h = ((u1 * u2) >> 5) + u2; stride = 2 * (u1 & 127) + 1
        cand = (h[:, :, None, :] + np.arange(P)[None, None, :, None] * stride[:, :, None, :]) & (L - 1)
        off = np.abs(pull(y, cand.reshape(N, 8, P * M)).reshape(N, 8, 16, P, M) - want[:, :, :, None, :])
        ce = np.add.reduce(off, axis=2); m = np.argmin(ce, axis=2)
        donor = np.take_along_axis(cand, m[:, :, None, :], 2)[:, :, 0]
        hit = np.min(ce, axis=2) < err; one = hit.astype(np.int64)
        counts = hit & (np.add.accumulate(one, axis=2) - one < C)
        go = {}
        for q in range(N):
            for g in range(8):
                i = np.flatnonzero(counts[q, g]); go[q, g] = y[q, g][:, child[q, g, i]]
                key, first = np.unique(side[q, g, i] * ND + par[q, g, i], return_index=True)
                kd[q, g, key] = donor[q, g, i[first]]
        for q in range(N):
            for g in range(8):
                v = go[q, g]; y[(q + 1) % N, g, :, rnd * C:rnd * C + v.shape[1]] = v
        evaluate(y, kd, om)
    return {"yo": y.reshape(N, 128, W).astype(np.float32).astype(BF), "ko": kd.astype(np.float32)}

@@ -1,0 +1,602 @@
+from concourse.mybir import AluOpType as A, ActivationFunctionType as F
+
+H = 16
+LIB = 1024
+SENT = -1048576.0
+
+SCRATCH, PLACE = {}, {}
+
+
+def declare(dtype, text, packed=False):
+    o = 0
+    for item in text.split():
+        name, w = item.split(":")
+        if packed:
+            PLACE[name] = ("SM" + dtype, o)
+            o += (int(w) + 7) // 8 * 8
+        else:
+            SCRATCH[name] = ("sbuf", [128, int(w)], dtype)
+    if packed:
+        SCRATCH["SM" + dtype] = ("sbuf", [128, o], dtype)
+
+
+declare("bfloat16", "YT:3616 YAB:4096 YAP:4096 TG:512 WAB0:1536 WAB1:1536 Y2:1024 Y2P:1024 SB:1024 AB:1024 WT:512 MT:512 DF:4096 GV:1024 "
+        "YC:512 LF:128 LT2:128 HIT:32 INC:32 EQ:1024 QH:1024 QD:1024 ONE:128 IB:128 NI:128 BD:128 BD1:128 O256:2048 BQ:2048 KQ0:2048 KQ1:2048 MQ:2048 "
+        "W1:2048 W2:2048 AQ:2048 L00:128 L01:128 L10:128 L11:128 UP:128 DN:128 MLB:128 MLT:128 LB:128 LT:128 TRI:128 I5:128 IO1:128 IOC:256 "
+        "MCI:256 MC:256")
+declare("float16", "KLH:256 WF:256 KTG:512 XH:32 DNH:32 DG:1024 CHM:2048")
+declare("uint16", "UL:512 SEL:32 NL:32 KEYU:32 CU:256 SLOT:32")
+declare("int32", "KLD:256 MLD:128 WTI:2")
+declare("float32", "KT:1536 PAY:512 SL0:640 SL1:640 LAND0:128 LAND1:128 KLF:256 KLT:256 KOF:256 KOT:256 WTF:2")
+declare("float32", "WK:256 NW:128 NKB:256 ES:64 TOB:32 DK:32 QC:32 Q0:32 Q1:32 S1:32 S2:32 S3:32 CHI:32 ST:64 NS:64 DS:64 LV:64 NB:32 XG:32 US:64 B1:128 B2:64 "
+        "B3:64 BEST:32 CT:32 RD:32 RE:32 RF:32 XF:16 DX:8 XN:8 XK:8 QF:8 CF:8 WIN:8 DD:8 ZU:256 ZT:256 STR:32 SR2:64 SR4:128 SELC:16 LANE:32 LQ:32 LQ2:32 "
+        "TC:32 TM:32 NB0:32 ONEF:8 XC:8 NX:8 G16:8", True)
+declare("int32", "LI:128 LY:128 U1I:32 PRI:32 SHI:32 UMI:32 CA:256 CI:256 B8:32 MI:32 MTT:32 HD:32 DNI:32 XI:16 XS:16 KI:8 QI:8 CQ:8 KPI:32 KAI:32 KBI:32 "
+        "XI1:32 LI0:32 LI1:32 LI2:32", True)
+for _k in range(8):
+    SCRATCH["P%d" % _k] = ("psum", [128, 512], "float32")
+
+SEMAPHORES = ["cV", "cS", "cP", "cG", "arr0", "arr1", "snt0", "snt1"] + ["d%d" % k for k in range(16)]
+
+
+def rank_program(g, core, T, topo):
+    rank = T.rank_of(core)
+    if rank is None:
+        return
+    n_ranks = len(T.cores)
+    ENG = {"V": g.vector, "S": g.scalar, "P": g.tensor, "G": g, "Y": g.sync}
+    cnt = {s: 0 for s in SEMAPHORES}
+    seen = {q: {} for q in ENG}
+    clocks = {}
+    acc = {}
+    dmas = [0]
+
+    def ap(r):
+        if r[0] == "ind":
+            return ap(r[1]).indirect(ap(r[2]))
+        b, lo, hi, st, p0, p1 = r
+        if b in PLACE:
+            b, o = PLACE[b]
+            lo, hi = lo + o, hi + o
+        return T[b][p0:p1, lo:hi] if st == 1 else T[b][p0:p1, lo:hi:st]
+
+    def R(b, lo, hi, st=1, p0=0, p1=128):
+        return (b, lo, hi, st, p0, p1)
+
+    def is_psum(b):
+        return b[0] == "P" and len(b) == 2
+
+    def wait(q, sem, n):
+        if seen[q].get(sem, 0) >= n:
+            return
+        ENG[q].wait_ge(T.sem[sem], n)
+        s = seen[q]
+        for k, v in list(clocks.get((sem, n), {}).items()) + [(sem, n)]:
+            s[k] = max(s.get(k, 0), v)
+
+    def sync_for(q, reads, writes):
+        need = {}
+        for rs, w in ((reads, False), (writes, True)):
+            for (b, lo, hi, st, p0, p1) in rs:
+                ps = is_psum(b)
+                if ps:
+                    lo, hi, p0, p1 = 0, 512, 0, 128
+                for (q2, sem, n, lo2, hi2, a0, a1, w2) in acc.get(b, ()):
+                    if lo2 >= hi or hi2 <= lo or a0 >= p1 or a1 <= p0:
+                        continue
+                    if ps and q2 == q and (q == "P" or not (w or w2)):
+                        continue
+                    if not ps and not (w or w2):
+                        continue
+                    need[sem] = max(need.get(sem, 0), cnt[sem] if sem[0] == "d" else n)
+        for sem in sorted(need, key=lambda s: -sum(clocks.get((s, need[s]), {}).values())):
+            wait(q, sem, need[sem])
+
+    def note(q, sem, n, reads, writes):
+        for rs, w in ((writes, True), (reads, False)):
+            for (b, lo, hi, st, p0, p1) in rs:
+                if is_psum(b):
+                    lo, hi, p0, p1 = 0, 512, 0, 128
+                L = acc.setdefault(b, [])
+                if w and st == 1:
+                    L[:] = [e for e in L if not (lo <= e[3] and e[4] <= hi and p0 <= e[5] and e[6] <= p1)]
+                elif not w:
+                    L[:] = [e for e in L if not (e[0] == q and not e[7] and lo <= e[3] and e[4] <= hi and p0 <= e[5] and e[6] <= p1)]
+                L.append((q, sem, n, lo, hi, p0, p1, w))
+
+    def emit(q, fn, reads, writes):
+        sync_for(q, reads, writes)
+        sem = "c" + q
+        cnt[sem] += 1
+        fn().then_inc(T.sem[sem], 1)
+        clocks[(sem, cnt[sem])] = dict(seen[q], **{sem: cnt[sem]})
+        note(q, sem, cnt[sem], reads, writes)
+
+    def newd():
+        dmas[0] += 1
+        return "d%d" % (dmas[0] - 1)
+
+    def dma(q, sem, out, in_, reads, writes):
+        sync_for(q, reads, writes)
+        cnt[sem] += 16
+        ENG[q].dma_start(out, in_).then_inc(T.sem[sem], 16)
+        c = dict(seen[q])
+        for k, v in clocks.get((sem, cnt[sem] - 16), {}).items():
+            c[k] = max(c.get(k, 0), v)
+        clocks[(sem, cnt[sem])] = c
+        note(q, sem, cnt[sem], reads, writes)
+
+    def IND(win, off):
+        return ("ind", win, off)
+
+    def rd(*xs):
+        r = []
+        for x in xs:
+            if isinstance(x, tuple):
+                r += [x[1], x[2]] if x[0] == "ind" else [x]
+        return r
+
+    def num(x):
+        return ap(x) if isinstance(x, tuple) else x
+
+    def tt(out, a, b, op):
+        emit("V", lambda: g.vector.tensor_tensor(ap(out), ap(a), ap(b), op), rd(a, b), [out])
+
+    def ts(out, a, s1, op0, s2=None, op1=None):
+        if op1 is None:
+            emit("V", lambda: g.vector.tensor_scalar(ap(out), ap(a), num(s1), None, op0), rd(a, s1), [out])
+        else:
+            emit("V", lambda: g.vector.tensor_scalar(ap(out), ap(a), num(s1), num(s2), op0, op1), rd(a, s1, s2), [out])
+
+    def cp(out, a):
+        if out[0] == "ind":
+            emit("V", lambda: g.vector.tensor_copy(ap(out), ap(a)), rd(a) + [out[2]], [out[1]])
+        else:
+            emit("V", lambda: g.vector.tensor_copy(ap(out), ap(a)), rd(a), [out])
+
+    def ms(out, v):
+        emit("V", lambda: g.vector.memset(ap(out), v), [], [out])
+
+    def vtr(out, a):
+        emit("V", lambda: g.vector.transpose(ap(out), ap(a)), [a], [out])
+
+    def act(out, a, func=F.Identity, scale=1.0, bias=0.0):
+        emit("S", lambda: g.scalar.activation(ap(out), ap(a), func, bias=num(bias), scale=num(scale)), rd(a, scale, bias), [out])
+
+    def mm(out, lhsT, rhs, start, stop):
+        emit("P", lambda: g.tensor.matmul(ap(out), ap(lhsT), ap(rhs), start, stop), [lhsT, rhs], [out])
+
+    def iota(out, pat, chm, small):
+        if small:
+            emit("G", lambda: g.iota(ap(out), pat, 0, chm, allow_small_or_imprecise_dtypes=True), [], [out])
+        else:
+            emit("G", lambda: g.iota(ap(out), pat, 0, chm), [], [out])
+
+    def asel(out, in_, pat, op, base, chm):
+        emit("G", lambda: g.affine_select(ap(out), ap(in_), pat, op, 0.0, base, chm), [in_], [out])
+
+    def phases(out_b, lo, n, W, src, s0, first, last):
+        for q in range(16):
+            mm(R(out_b, lo, lo + n), R(W, 128 * q, 128 * q + 128), R(src, s0 + q, s0 + 16 * n, 16), first and q == 0, last and q == 15)
+
+    def to_rows(P, W, src):
+        for q in range(16):
+            yield R(P, q, 512, 16), R(W, 128 * q, 128 * q + 128), src
+
+    a128 = lambda b: R(b, 0, 128)
+    c32 = lambda b, k=0: R(b, 32 * k, 32 * k + 32)
+
+    dK, dM, dL, dT, dW = [newd() for _ in range(5)]
+    dma("S", dK, ap(R("KLD", 0, 256)), T.kid[:, :], [], [R("KLD", 0, 256)])
+    dma("Y", dM, ap(R("MLD", 0, 128)), T.mx[:, :], [], [R("MLD", 0, 128)])
+    dma("Y", dL, ap(R("YT", H, H + 1536)), T.lv[:, :], [], [R("YT", H, H + 1536)])
+    dma("Y", dT, ap(R("TG", 0, 512)), T.tg[:, :], [], [R("TG", 0, 512)])
+    dma("Y", dW, ap(R("WTI", 0, 2)), T.wt[:, :], [], [R("WTI", 0, 2)])
+
+    ms(a128("ONE"), 1.0)
+    ms(R("YT", 0, H), 0.0)
+    ms(R("O256", 0, 2048), 256.0)
+    asel(a128("IB"), a128("ONE"), [[-1, 128]], A.is_equal, 0, 1)
+    iota(R("LI1", 0, 32), [[0, 32]], 1, False)
+    asel(a128("UP"), a128("ONE"), [[1, 128]], A.is_equal, -16, -1)
+    asel(a128("DN"), a128("ONE"), [[1, 128]], A.is_equal, 16, -1)
+    asel(a128("BD1"), a128("ONE"), [[-16, 8], [0, 16]], A.is_ge, 0, 1)
+    asel(a128("BD"), a128("BD1"), [[16, 8], [0, 16]], A.is_ge, 15, -1)
+    asel(R("BQ", 0, 2048), R("O256", 0, 2048), [[-1, 16], [-16, 8], [0, 16]], A.is_equal, 0, 1)
+    iota(R("LI0", 0, 32), [[16, 32]], 0, False)
+    for k in range(2):
+        act(R("KQ%d" % k, 0, 2048), R("O256", 0, 2048), scale=0.0)
+    asel(a128("LT"), a128("BD"), [[1, 128]], A.is_gt, 0, -1)
+    asel(a128("TRI"), a128("ONE"), [[-1, 128]], A.is_gt, 0, 1)
+    iota(R("MCI", 0, 256), [[1, 8], [0, 32]], 0, True)
+    iota(R("IO1", 0, 128), [[1, 128]], 0, True)
+    iota(R("IOC", 0, 256), [[1, 256]], 0, True)
+    iota(R("G16", 0, 8), [[-16, 8]], 0, True)
+    ts(c32("XI1"), c32("LI1"), 4, A.arith_shift_right, 1, A.bitwise_and)
+    cp(R("XC", 0, 8), R("XI1", 0, 8))
+    ts(R("NX", 0, 8), R("XC", 0, 8), -1.0, A.mult, 1.0, A.add)
+    for u, v, b in ((0, 0, "IB"), (0, 1, "UP"), (1, 0, "DN"), (1, 1, "IB")):
+        ts(a128("L%d%d" % (u, v)), a128(b), R("XC" if u else "NX", 0, 1), A.mult)
+
+    def constants_0():
+        ts(a128("NI"), a128("IB"), -1.0, A.mult)
+        ms(R("MQ", 0, 2048), 0.0)
+        for gr in range(8):
+            cp(R("MQ", 16 * gr, 2048, 129), R("BD", 16 * gr, 16 * gr + 16))
+
+    def constants_1():
+        ts(c32("LI2"), c32("LI1"), 15, A.bitwise_and)
+        ts(c32("Q0"), c32("LI2"), 0.0, A.is_equal)
+        ts(c32("Q1"), c32("LI2"), 1.0, A.is_equal, 4096.0, A.mult)
+        tt(c32("LANE"), c32("LI2"), c32("LI0"), A.add)
+        tt(c32("QC"), c32("Q0"), c32("Q1"), A.add)
+        ts(c32("LQ"), c32("LANE"), 1.0 / 512, A.mult)
+        act(R("AQ", 0, 2048), R("MQ", 0, 2048), scale=R("QC", 0, 1))
+        ts(c32("LQ2"), c32("LQ"), 2.0, A.add)
+        ms(R("ONEF", 0, 8), 1.0)
+        ts(c32("NB0"), c32("LANE"), 1536.0, A.add)
+        cp(R("WTF", 0, 2), R("WTI", 0, 2))
+
+    def weighted(k):
+        act(R("W%d" % (k + 1), 0, 2048), R("MQ", 0, 2048), scale=R("WTF", k, k + 1))
+
+    def constants_2():
+        ts(c32("TC"), c32("LANE"), 128.0, A.add)
+        ts(c32("TM"), c32("LANE"), -383.0, A.add)
+        ts(R("MC", 0, 256), R("MCI", 0, 256), 0.125, A.mult)
+        for s in range(2):
+            ts(R("SELC", 8 * s, 8 * s + 8), R("BQ", 128 * s, 128 * s + 128, 16), 1.0 / 256, A.mult)
+        ts(a128("I5"), a128("IB"), -512.0, A.mult)
+        tt(a128("LB"), a128("LT"), a128("BD"), A.subtract)
+        tt(a128("LB"), a128("LB"), a128("IB"), A.add)
+        tt(a128("LT"), a128("LB"), a128("I5"), A.add)
+
+    def unscramble(P, src, nb):
+        for k in range(nb):
+            for c2 in range(2):
+                for x in range(2):
+                    mm(R(P, 2 * k + c2, 32 * nb, 2 * nb), a128("L%d%d" % (c2, x)), R(src, 32 * k + 16 * x, 32 * k + 16 * x + 16), x == 0, x == 1)
+
+    def load_lists():
+        ts(a128("MLB"), a128("MLD"), -1.0, A.mult, 1.0, A.add)
+        vtr(a128("MLT"), a128("MLB"))
+        unscramble("P6", "MLT", 4)
+        ts(R("KLF", 0, 256), R("KLD", 0, 256), -1792.0, A.add)
+        vtr(R("KLT", 0, 256), R("KLF", 0, 256))
+        cp(R("KLH", 0, 256), R("KLT", 0, 256))
+        unscramble("P7", "KLH", 8)
+        constants_0()
+        cp(R("NW", 0, 128), R("P6", 0, 128))
+        ts(R("WK", 0, 256), R("P7", 0, 256), 1792.0 + H, A.add)
+
+    def lists():
+        tt(R("NKB", 0, 128), R("WK", 128, 256), R("NW", 0, 128), A.mult)
+        cp(R("UL", 0, 256), R("WK", 0, 256))
+        cp(R("UL", 256, 384), R("NKB", 0, 128))
+
+    def wf():
+        ts(R("WF", 0, 256), R("WK", 0, 256), -1792.0 - H, A.add)
+
+    def lists_2():
+        tt(R("NKB", 128, 256), R("WK", 0, 128), R("NW", 0, 128), A.mult)
+        wf()
+        cp(R("UL", 384, 512), R("NKB", 128, 256))
+
+    ul = lambda k, l, a=0, b=32: R("UL", 128 * k + 32 * l + a, 128 * k + 32 * l + b)
+    below = lambda l: R("YT", 0, H + 1536 + 512 * l)
+
+    def table(k, l):
+        n, lo, which = (("YAB", 0, 0), ("YAB", 2048, 1), ("YAP", 0, 3))["abp".index(k)]
+        act(R(n, lo + 512 * l, lo + 512 * l + 512), IND(below(l), ul(which, l)))
+
+    def level(l, tables="", between=None):
+        W = below(l)
+        cut = ((0, 8), (8, 32))
+        bp = lambda a, b: R("YAP", 2048 + 512 * l + 16 * a, 2048 + 512 * l + 16 * b)
+        cp(bp(*cut[0]), IND(W, ul(2, l, *cut[0])))
+        act(bp(*cut[1]), IND(W, ul(2, l, *cut[1])))
+        for k in tables.split():
+            table(k[0], int(k[1]))
+        if between:
+            between()
+        for a, b in cut:
+            c = (16 * a, 16 * b)
+            tt(R("WT", *c), IND(W, ul(0, l, a, b)), bp(a, b), A.add)
+            tt(R("MT", *c), IND(W, ul(1, l, a, b)), R("WT", *c), A.max)
+        o = H + 1536 + 512 * l
+        ts(R("YT", o, o + 512), R("MT", 0, 512), 255.0, A.min)
+
+    def levels():
+        level(0, "b0 a0", lists_2)
+        level(1, "p0 b1")
+        for l in (2, 0, 1):
+            kt(l)
+        level(2, "a1 p1")
+        level(3, "b3 p3", lambda: kt_copy(2))
+        cp(R("YAB", 1536, 2048), IND(below(3), ul(0, 3)))
+        for k in "bap":
+            table(k, 2)
+
+    def kt(l):
+        P = "P%d" % (7 - l)
+        for q in range(16):
+            for k in range(2):
+                mm(R(P, q, 512, 16), R("KQ%d" % k, 128 * q, 128 * q + 128), R("WF", 128 * k + 32 * l, 128 * k + 32 * l + 32), k == 0, k == 1)
+
+    def kt_copy(l):
+        ts(R("KT", 512 * l, 512 * l + 512), R("P%d" % (7 - l), 0, 512), 1.0 / 256, A.mult)
+
+    def step(st, fill):
+        Wc, Wn = "WAB%d" % (st % 2), "WAB%d" % ((st + 1) % 2)
+        if st == 0:
+            D = R("TG", 0, 512)
+            y = (R("YAB", 1536, 2048), R("YAB", 3584, 4096))
+            yn = (R("YAP", 1536, 2048), R("YAP", 3584, 4096))
+            ka, kb = R("WK", 96, 128), R("WK", 224, 256)
+        else:
+            D = R(Wc, 1024, 1536)
+            y = (R("Y2", 0, 512), R("Y2", 512, 1024))
+            yn = (R("Y2P", 0, 512), R("Y2P", 512, 1024))
+            cp(y[1], IND(R("YAB", 2048, 3584), c32("NL")))
+            act(yn[1], IND(R("YAP", 2048, 3584), c32("NL")))
+            act(y[0], IND(R("YAB", 0, 1536), c32("NL")))
+            act(yn[0], IND(R("YAP", 0, 1536), c32("NL")))
+            if st == 1:
+                act(R("KTG", 0, 512), IND(R("KT", 0, 1536), c32("NL")))
+            ka, kb = c32("KAI"), c32("KBI")
+        parts = ((0, 0, 512, "P4"), (1, 0, 256, "P5"), (1, 256, 512, "P1"))
+        mm(R("P0", 0, 512), a128("IB"), D, True, True)
+        for s in range(2):
+            mm(R("P%d" % (2 + s), 0, 512), a128("IB"), D, True, False)
+        mm(R("P2", 0, 512), a128("NI"), yn[1], False, True)
+        for s, a, b, P in parts[1:] + parts[:1]:
+            mm(R(P, 0, b - a), a128("NI"), R(y[s][0], y[s][1] + a, y[s][1] + b), True, False)
+        mm(R("P3", 0, 512), a128("NI"), yn[0], False, True)
+        for s in range(2):
+            tt(R("SB", 512 * s, 512 * s + 512), y[1 - s], R("P0", 0, 512), A.is_le)
+        for s, a, b, P in parts:
+            c = (512 * s + a, 512 * s + b)
+            tt(R(Wc, *c), R("SB", *c), R("P%d" % (2 + s), a, b), A.mult)
+            mm(R(P, 0, b - a), a128("IB"), R(Wc, *c), False, True)
+            act(R("AB", *c), R(P, 0, b - a), F.Abs)
+        if st == 1:
+            phases("P7", 0, 32, "AQ", "KTG", 0, True, True)
+        fill()
+        if st == 1:
+            ts(c32("KPI"), c32("P7"), (1792.0 + H) * 4097.0, A.add)
+            ts(c32("KAI"), c32("KPI"), 4095, A.bitwise_and)
+            ts(c32("KBI"), c32("KPI"), 12, A.arith_shift_right)
+        if st < 2:
+            tt(c32("DK"), kb, ka, A.subtract)
+        phases("P6", 0, 64, "MQ", "AB", 0, True, True)
+        cp(R("ES", 0, 64), R("P6", 0, 64))
+        tt(c32("TOB"), c32("ES", 1), c32("ES"), A.is_lt)
+        if st == 0:
+            tt(c32("S1"), c32("TOB"), c32("LQ"), A.add)
+        else:
+            ts(c32("S1"), c32("TOB"), -2.0, A.add)
+            tt(c32("S3"), c32("S1"), c32("LV"), A.mult)
+            tt(c32("S1"), c32("S3"), c32("LQ2"), A.add)
+        if st < 2:
+            tt(c32("S2"), c32("TOB"), c32("DK"), A.mult)
+        ts(c32("SEL"), c32("S1"), 512.0, A.mult)
+        win = R(Wc, 0, 1024 if st == 0 else 1536)
+        act(R(Wn, 1024, 1280), IND(win, R("SEL", 0, 16)))
+        if st < 2:
+            tt(c32("CHI"), c32("S2"), ka, A.add)
+            ts(c32("NL"), c32("CHI"), -1536.0 - H, A.add, 0.0, A.max)
+        cp(R(Wn, 1280, 1536), IND(win, R("SEL", 16, 32)))
+
+        def rest():
+            X = "ST" if st == 0 else "NS"
+            ts(c32("S3"), c32("TOB"), 2048.0, A.mult)
+            tt(c32(X, 1), c32("ES", 1), c32("ES"), A.min)
+            tt(c32(X), c32("S3"), c32("NB" if st else "NB0"), A.add)
+            if st:
+                tt(R("DS", 0, 64), R("NS", 0, 64), R("ST", 0, 64), A.subtract)
+                tt(R("DS", 0, 64), R("DS", 0, 64), R("LV", 0, 64), A.mult)
+                tt(R("ST", 0, 64), R("DS", 0, 64), R("ST", 0, 64), A.add)
+            if st == 0:
+                for k in range(2):
+                    ts(c32("LV", k), c32("CHI"), 1536.0 + H, A.is_ge)
+            elif st == 1:
+                ts(c32("S3"), c32("CHI"), 1536.0 + H, A.is_ge)
+                for k in range(2):
+                    tt(c32("LV", k), c32("LV", k), c32("S3"), A.mult)
+            if st < 2:
+                ts(c32("NB"), c32("CHI"), -1536.0 - H, A.add, 0.0, A.max)
+        return rest
+
+    def donors(t, rest):
+        D = R("WAB1", 1024, 1536)
+        SL = "SL%d" % t
+        phases("P6", 0, 32, "W1", "WAB1", 1024, True, True)
+        phases("P6", 32, 32, "W2", "WAB1", 1024, True, True)
+        rest()
+        cp(c32("KEYU"), c32("ST"))
+        act(R("YC", 0, 512), IND(R("YAB", 0, 4096), c32("KEYU")))
+        ts(c32("XG"), c32("ST"), 2048.0, A.is_ge)
+        tt(c32("S3"), c32("XG"), c32("ST"), A.add)
+        ts(c32("XH"), c32("S3"), -2048.0, A.add)
+        ms(R(SL, 0, 128), SENT)
+        cp(R("US", 0, 64), R("P6", 0, 64))
+        cp(c32("U1I"), c32("US"))
+        tt(c32("PRI"), c32("US"), c32("US", 1), A.mult)
+        ts(c32("UMI"), c32("U1I"), 127, A.bitwise_and)
+        ts(c32("SHI"), c32("PRI"), 5, A.arith_shift_right)
+        ts(c32("STR"), c32("UMI"), 2.0, A.mult, 1.0, A.add)
+        for k in range(4):
+            act(c32("SR4", k), c32("STR"), scale=4.0)
+        tt(c32("CA"), c32("SHI"), c32("US", 1), A.add)
+        for k in range(2):
+            ts(c32("SR2", k), c32("UMI"), 4.0, A.mult, 2.0, A.add)
+        tt(c32("CA", 1), c32("CA"), c32("STR"), A.add)
+        tt(R("CA", 64, 128), R("CA", 0, 64), R("SR2", 0, 64), A.add)
+        ts(R("CI", 0, 128), R("CA", 0, 128), 1023, A.bitwise_and)
+        cp(R("CU", 0, 128), R("CI", 0, 128))
+        LW = R("YT", H, H + LIB)
+        for k, m in enumerate((1, 3)):
+            act(R("GV", 512 * k, 512 * k + 512), IND(LW, c32("CU", m)))
+            mm(R("P%d" % (4 + 3 * k), 0, 512), a128("IB"), R("GV", 512 * k, 512 * k + 512), True, False)
+            mm(R("P%d" % (4 + 3 * k), 0, 512), a128("NI"), D, False, True)
+        for h in range(2):
+            mm(R("P%d" % (2 + h), 0, 128), a128("IB"), R("MC", 128 * h, 128 * h + 128), True, False)
+
+        def cand(m):
+            c = (512 * m, 512 * m + 512)
+            if m in (1, 3):
+                act(R("DF", *c), R("P4" if m == 1 else "P7", 0, 512), F.Abs)
+            else:
+                tt(R("DF", *c), IND(LW, c32("CU", m)), D, A.subtract)
+                act(R("DF", *c), R("DF", *c), F.Abs)
+        cand(0)
+        cand(1)
+        tt(R("CA", 128, 256), R("CA", 0, 128), R("SR4", 0, 128), A.add)
+        cand(2)
+        ts(R("CI", 128, 256), R("CA", 128, 256), 1023, A.bitwise_and)
+        cp(R("CU", 128, 256), R("CI", 128, 256))
+        cand(3)
+        phases("P2", 0, 64, "MQ", "DF", 0, False, False)
+        phases("P2", 64, 64, "MQ", "DF", 1024, False, True)
+        mm(R("P5", 0, 512), a128("IB"), R("YC", 0, 512), True, False)
+        for o, w, x in to_rows("P5", "KQ0", c32("XH")):
+            mm(o, w, x, False, False)
+        cand(4)
+        cand(5)
+        phases("P3", 0, 64, "MQ", "DF", 2048, False, False)
+        cand(6)
+        cp(R("B1", 0, 128), R("P2", 0, 128))
+        cand(7)
+        tt(R("B3", 0, 64), R("B1", 0, 64), R("B1", 64, 128), A.min)
+        phases("P3", 64, 64, "MQ", "DF", 3072, False, True)
+        tt(R("B2", 0, 64), R("B3", 0, 64), R("P3", 0, 64), A.min)
+        tt(R("B1", 0, 64), R("B2", 0, 64), R("P3", 64, 128), A.min)
+        tt(c32("BEST"), c32("B1"), c32("B1", 1), A.min)
+        tt(c32("HIT"), c32("BEST"), c32("ST", 1), A.is_lt)
+        ts(c32("B8"), c32("BEST"), 8.0, A.mult)
+        emit("V", lambda: g.vector.tensor_tensor_scan(ap(c32("INC")), ap(R("ONE", 0, 32)), ap(c32("HIT")), 0.0, A.mult, A.add),
+             [R("ONE", 0, 32), c32("HIT")], [c32("INC")])
+        ts(c32("MI"), c32("B8"), 7, A.bitwise_and)
+        mm(R("P6", 0, 32), a128("LT"), c32("HIT"), True, False)
+        mm(R("P6", 0, 32), a128("BD"), c32("INC"), False, True)
+        tt(c32("MTT"), c32("MI"), c32("STR"), A.mult)
+        tt(c32("HD"), c32("MTT"), c32("CA"), A.add)
+        ts(c32("DNI"), c32("HD"), 1023, A.bitwise_and)
+        ts(c32("DNH"), c32("DNI"), float(H), A.add)
+        for k, (o, w, x) in enumerate(to_rows("P5", "KQ1", c32("DNH"))):
+            mm(o, w, x, False, k == 15)
+        act(R("PAY", 0, 512), R("P5", 0, 512))
+        ts(c32("CT"), c32("P6"), -383.0, A.is_lt)
+        tt(c32("RD"), c32("P6"), c32("TM"), A.subtract)
+        tt(c32("RE"), c32("RD"), c32("CT"), A.mult)
+        tt(c32("RF"), c32("RE"), c32("TC"), A.add)
+        cp(c32("SLOT"), c32("RF"))
+        cp(IND(R(SL, 0, 640), c32("SLOT")), R("PAY", 0, 512))
+
+    def send(t):
+        dst = T.cores[(rank + 1) % n_ranks]
+        rid, pid, _ = topo.addr(dst)
+        sl = R("SL%d" % t, 0, 128)
+        sync_for("G", [sl], [])
+        g.remote_dma(T["LAND%d" % t][:, :], ap(sl), T.sem["arr%d" % t], T.sem["snt%d" % t], pid, rid, topo.mask(core, dst))
+
+    def grafts(t):
+        g8 = lambda b: R(b, 0, 8)
+        at = lambda gr, w=128: (w * gr, w * gr + w)
+        mm(R("P6", 0, 16), R("SL%d" % t, 0, 128), R("SELC", 0, 16), True, True)
+        cp(R("XI", 0, 16), R("P6", 0, 16))
+        ts(R("XS", 0, 16), R("XI", 0, 16), 8, A.arith_shift_right)
+        cp(R("XF", 0, 16), R("XS", 0, 16))
+        for gr in range(8):
+            if gr > 2:
+                act(R("DG", *at(gr)), a128("IB"), scale=R("XF", gr, gr + 1))
+            else:
+                ts(R("DG", *at(gr)), a128("IB"), R("XF", gr, gr + 1), A.mult)
+            mm(R("P%d" % (gr // 4), *at(gr % 4)), a128("TRI"), R("DG", *at(gr)), True, True)
+        ts(g8("XN"), g8("XF"), 0.0, A.is_lt)
+        ts(g8("DX"), R("XF", 8, 16), 0.0, A.max)
+        tt(g8("XK"), g8("XN"), g8("XF"), A.add)
+        ts(g8("KI"), g8("XK"), 2047.0, A.add)
+        ts(g8("QI"), g8("KI"), 15, A.bitwise_and)
+        ts(g8("CQ"), g8("KI"), 4, A.arith_shift_right)
+        tt(g8("QF"), g8("G16"), g8("QI"), A.subtract)
+        cp(g8("CF"), g8("CQ"))
+        for gr in range(8):
+            act(R("QD", *at(gr)), R("IO1", 0, 128), F.Abs, bias=R("QF", gr, gr + 1))
+        for h in range(2):
+            act(R("QH", *at(h, 512)), R("QD", *at(h, 512)), F.Relu, scale=-1.0, bias=R("ONEF", 0, 1))
+        for gr in range(8):
+            ts(R("EQ", *at(gr)), R("P%d" % (gr // 4), *at(gr % 4)), R("XF", gr, gr + 1), A.is_equal)
+            mm(R("P4", gr, gr + 1), R("EQ", *at(gr)), R("ONE", 0, 1), True, True)
+        ts(g8("WIN"), R("P4", 0, 8), 0.0, A.is_equal)
+        tt(g8("DD"), g8("WIN"), g8("DX"), A.mult)
+        for gr in range(8):
+            ts(R("CHM", *at(gr, 256)), R("IOC", 0, 256), R("CF", gr, gr + 1), A.is_equal, R("DD", gr, gr + 1), A.mult)
+            mm(R("P5", 0, 256), R("QH", *at(gr)), R("CHM", *at(gr, 256)), gr == 0, gr == 7)
+        c = (0, 256)
+        ts(R("ZU", *c), R("P5", *c), 0.0, A.is_equal)
+        tt(R("ZT", *c), R("WK", *c), R("ZU", *c), A.mult)
+        tt(R("WK", *c), R("ZT", *c), R("P5", *c), A.add)
+        lists()
+
+    def receive(t):
+        lib = R("YT", H + 128 * t, H + 128 * t + 128)
+        src = T.cores[(rank - 1) % n_ranks]
+        L = "LAND%d" % t
+        g.vector.wait_ge(T.sem["arr%d" % t], len(topo.engines(src, core)))
+        ts(a128("LF"), a128(L), -700000.0, A.is_lt)
+        cp(a128("LI"), a128(L))
+        tt(a128("LT2"), lib, a128("LF"), A.mult)
+        ts(a128("LY"), a128("LI"), 255, A.bitwise_and)
+        tt(lib, a128("LT2"), a128("LY"), A.add)
+
+    do, dko = newd(), newd()
+
+    def out(lo, hi):
+        src = R("YT", H + lo, H + hi)
+        dma("Y", do, T.yo[:, lo:hi], ap(src), [src], [])
+
+    def kids_out_1():
+        for k in range(8):
+            for x in range(2):
+                for c2 in range(2):
+                    mm(R("P0", 32 * k + 16 * x, 32 * k + 16 * x + 16), a128("L%d%d" % (x, c2)), R("WF", 2 * k + c2, 256, 16), c2 == 0, c2 == 1)
+
+    def kids_out_2():
+        ts(R("KOF", 0, 256), R("P0", 0, 256), 1792.0, A.add)
+        vtr(R("KOT", 0, 256), R("KOF", 0, 256))
+        dma("Y", dko, T.ko[:, :], ap(R("KOT", 0, 256)), [R("KOT", 0, 256)], [])
+
+    load_lists()
+    lists()
+    for k in range(2):
+        act(R("KQ%d" % k, k, 2048, 16), R("BQ", k, 2048, 16))
+    levels()
+
+    for t in range(2):
+        first = t == 0
+        r0 = step(0, lambda: (constants_1() if first else None, kt_copy(0), kt_copy(1)))
+        r1 = step(1, lambda: (r0(), (constants_2(), weighted(0), weighted(1)) if first else None))
+        r2 = step(2, lambda: r1())
+        donors(t, r2)
+        send(t)
+        grafts(t)
+        receive(t)
+        if first:
+            levels()
+        else:
+            out(0, 1536)
+            level(0, "", wf)
+            out(1536, 2048)
+            level(1, "", kids_out_1)
+            out(2048, 2560)
+            level(2, "", kids_out_2)
+            out(2560, 3072)
+            level(3)
+            out(3072, 3584)
+
+    for s in ["cV", "cS", "cP", "cG"] + ["d%d" % k for k in range(dmas[0])]:
+        wait("G", s, cnt[s])
+    dst = T.cores[(rank + 1) % n_ranks]
+    for t in range(2):
+        g.wait_ge(T.sem["snt%d" % t], len(topo.engines(core, dst)))

@@ -13,26 +13,26 @@ def declare(dtype, text, packed=False):
         name, w = item.split(":")
         if packed:
             PLACE[name] = ("SM" + dtype, o)
-            o += (int(w) + 7) // 8 * 8
+            o += (int(w) + 15) // 16 * 16
         else:
             SCRATCH[name] = ("sbuf", [128, int(w)], dtype)
     if packed:
         SCRATCH["SM" + dtype] = ("sbuf", [128, o], dtype)
 
 
-declare("bfloat16", "YT:3616 YAB:4096 YAP:4096 TG:512 WAB0:1536 WAB1:1536 Y2:1024 Y2P:1024 SB:1024 AB:1024 WT:512 MT:512 DF:4096 GV:1024 "
-        "YC:512 LF:128 LT2:128 HIT:32 INC:32 EQ:1024 QH:1024 QD:1024 ONE:128 IB:128 NI:128 BD:128 BD1:128 O256:2048 BQ:2048 KQ0:2048 KQ1:2048 MQ:2048 "
-        "W1:2048 W2:2048 AQ:2048 L00:128 L01:128 L10:128 L11:128 UP:128 DN:128 MLB:128 MLT:128 LB:128 LT:128 TRI:128 I5:128 IO1:128 IOC:256 "
-        "MCI:256 MC:256")
-declare("float16", "KLH:256 WF:256 KTG:512 XH:32 DNH:32 DG:1024 CHM:2048")
-declare("uint16", "UL:512 SEL:32 NL:32 KEYU:32 CU:256 SLOT:32")
+declare("bfloat16", "YT:3616 ZAB:4096 BP:2048 SG:2048 TG:512 WAB0:1536 WAB1:1536 Y2:1024 Y2P:512 MN:512 UU:512 CB:512 SA:512 AB:1024 DF:4096 DD:2048 "
+        "GV:2048 YO:2048 YR:512 YC:512 EQ:1024 O256:512 BQ:2048 KQ:2064 BC0:1024 BC:1024 NBC:1024 WZ:1920")
+declare("bfloat16", "LF:128 LT2:128 HIT:32 INC:32 ONE:128 IB:128 NI:128 N256:128 I2:128 BD:128 BD1:128 L00:128 L01:128 L10:128 L11:128 UP:128 DN:128 "
+        "MLB:128 MLT:128 SGB:128 LB:128 LT:128 TRI:128 MCI:256 MC:256 ZM:144 ZM2:144 ZMN:144 ZW1:144 ZW2:144 ZA0:144 ZAD:144 SEL2:16 RQ:128 S16:16 "
+        "DEAD:64", True)
+declare("float16", "KLF:256 KLH:256 WF:256 NXF:256 KTG:512 CHM:2048")
+declare("float16", "QCH:64 DNH:32 XH:128 IQN:128 IOC:256 L512:32 HL:32", True)
+declare("uint16", "UL:384 SEL:32 NL:32 KEYU:32 CU:256 SLOT:32")
 declare("int32", "KLD:256 MLD:128 WTI:2")
-declare("float32", "KT:1536 PAY:512 SL0:640 SL1:640 LAND0:128 LAND1:128 KLF:256 KLT:256 KOF:256 KOT:256 WTF:2")
-declare("float32", "WK:256 NW:128 NKB:256 ES:64 TOB:32 DK:32 QC:32 Q0:32 Q1:32 S1:32 S2:32 S3:32 CHI:32 ST:64 NS:64 DS:64 LV:64 NB:32 XG:32 US:64 B1:128 B2:64 "
-        "B3:64 BEST:32 CT:32 RD:32 RE:32 RF:32 XF:16 DX:8 XN:8 XK:8 QF:8 CF:8 WIN:8 DD:8 ZU:256 ZT:256 STR:32 SR2:64 SR4:128 SELC:16 LANE:32 LQ:32 LQ2:32 "
-        "TC:32 TM:32 NB0:32 ONEF:8 XC:8 NX:8 G16:8", True)
-declare("int32", "LI:128 LY:128 U1I:32 PRI:32 SHI:32 UMI:32 CA:256 CI:256 B8:32 MI:32 MTT:32 HD:32 DNI:32 XI:16 XS:16 KI:8 QI:8 CQ:8 KPI:32 KAI:32 KBI:32 "
-        "XI1:32 LI0:32 LI1:32 LI2:32", True)
+declare("float32", "KT:1536 PAY:512 SL0:1536 SL1:1536 LAND0:128 LAND1:128 KOF:256 KOT:256 WTF:2")
+declare("float32", "WK:256 NW:128 NKB:128 TOB:32 DK:32 ES:64 Q0:32 Q1:32 QD:32 S1:32 S2:32 S3:32 LQ:32 CHI:32 ST:64 NS:64 DS:64 LV:64 NB:32 SB:32 B1:128 B2:64 "
+        "B3:64 B4:32 B5:32 BEST:32 XF:16 ZU:256 ZT:256 STR:32 SR2:64 SR4:128 LANE:32 NL512:32 NB0:32 XC:8 NX:8 IQF:128 IOF:256 C255:8 CNX:8", True)
+declare("int32", "LI:128 LY:128 U1I:32 PRI:32 SHI:32 UMI:32 CA:256 CI:256 B8:32 MI:32 MTT:32 HD:32 DNI:32 KI:32 QCI:64 XI1:32 LI0:32 LI1:32 LI2:32", True)
 for _k in range(8):
     SCRATCH["P%d" % _k] = ("psum", [128, 512], "float32")
 
@@ -62,6 +62,9 @@ def rank_program(g, core, T, topo):
 
     def R(b, lo, hi, st=1, p0=0, p1=128):
         return (b, lo, hi, st, p0, p1)
+
+    def sub(r, a, b):
+        return R(r[0], r[1] + a, r[1] + b)
 
     def is_psum(b):
         return b[0] == "P" and len(b) == 2
@@ -166,25 +169,27 @@ def rank_program(g, core, T, topo):
     def mm(out, lhsT, rhs, start, stop):
         emit("P", lambda: g.tensor.matmul(ap(out), ap(lhsT), ap(rhs), start, stop), [lhsT, rhs], [out])
 
-    def iota(out, pat, chm, small):
+    def iota(out, pat, base, chm, small=True):
         if small:
-            emit("G", lambda: g.iota(ap(out), pat, 0, chm, allow_small_or_imprecise_dtypes=True), [], [out])
+            emit("G", lambda: g.iota(ap(out), pat, base, chm, allow_small_or_imprecise_dtypes=True), [], [out])
         else:
-            emit("G", lambda: g.iota(ap(out), pat, 0, chm), [], [out])
+            emit("G", lambda: g.iota(ap(out), pat, base, chm), [], [out])
 
     def asel(out, in_, pat, op, base, chm):
         emit("G", lambda: g.affine_select(ap(out), ap(in_), pat, op, 0.0, base, chm), [in_], [out])
 
-    def phases(out_b, lo, n, W, src, s0, first, last):
+    def phases(out_b, lo, n, Z, src, s0, first, last):
         for q in range(16):
-            mm(R(out_b, lo, lo + n), R(W, 128 * q, 128 * q + 128), R(src, s0 + q, s0 + 16 * n, 16), first and q == 0, last and q == 15)
+            mm(R(out_b, lo, lo + n), R(Z, 15 - q, 143 - q), R(src, s0 + q, s0 + 16 * n, 16), first and q == 0, last and q == 15)
 
-    def to_rows(P, W, src):
+    def to_row(P, r, src, first, last):
         for q in range(16):
-            yield R(P, q, 512, 16), R(W, 128 * q, 128 * q + 128), src
+            mm(R(P, q, 512, 16), R("KQ", 16 + 128 * q - r, 144 + 128 * q - r), src, first and q == 0, last and q == 15)
 
     a128 = lambda b: R(b, 0, 128)
     c32 = lambda b, k=0: R(b, 32 * k, 32 * k + 32)
+    col = lambda b, k=0: R(b, k, k + 1)
+    HALF = ((0, 256), (256, 512))
 
     dK, dM, dL, dT, dW = [newd() for _ in range(5)]
     dma("S", dK, ap(R("KLD", 0, 256)), T.kid[:, :], [], [R("KLD", 0, 256)])
@@ -193,63 +198,81 @@ def rank_program(g, core, T, topo):
     dma("Y", dT, ap(R("TG", 0, 512)), T.tg[:, :], [], [R("TG", 0, 512)])
     dma("Y", dW, ap(R("WTI", 0, 2)), T.wt[:, :], [], [R("WTI", 0, 2)])
 
+    O256 = R("O256", 0, 512)
     ms(a128("ONE"), 1.0)
+    ms(O256, 256.0)
     ms(R("YT", 0, H), 0.0)
-    ms(R("O256", 0, 2048), 256.0)
+    ms(R("KQ", 0, 16), 0.0)
+    ms(R("ZM", 0, 144), 0.0)
+    ms(R("C255", 0, 8), 255.0)
+    ms(R("CNX", 0, 8), -1535.0 - H)
+    ms(R("S16", 0, 16), 16.0)
+    ms(c32("DEAD", 1), 0.0)
+    ms(R("KT", 0, 512), 0.0)
     asel(a128("IB"), a128("ONE"), [[-1, 128]], A.is_equal, 0, 1)
-    iota(R("LI1", 0, 32), [[0, 32]], 1, False)
+    iota(c32("LI1"), [[0, 32]], 0, 1, False)
     asel(a128("UP"), a128("ONE"), [[1, 128]], A.is_equal, -16, -1)
     asel(a128("DN"), a128("ONE"), [[1, 128]], A.is_equal, 16, -1)
+    for j in range(4):
+        asel(R("BQ", 512 * j, 512 * j + 512), O256, [[-1, 4], [-16, 8], [0, 16]], A.is_equal, -4 * j, 1)
     asel(a128("BD1"), a128("ONE"), [[-16, 8], [0, 16]], A.is_ge, 0, 1)
     asel(a128("BD"), a128("BD1"), [[16, 8], [0, 16]], A.is_ge, 15, -1)
-    asel(R("BQ", 0, 2048), R("O256", 0, 2048), [[-1, 16], [-16, 8], [0, 16]], A.is_equal, 0, 1)
-    iota(R("LI0", 0, 32), [[16, 32]], 0, False)
-    for k in range(2):
-        act(R("KQ%d" % k, 0, 2048), R("O256", 0, 2048), scale=0.0)
+    iota(c32("LI0"), [[16, 32]], 0, 0, False)
+    for j in range(4):
+        asel(R("KQ", 16 + 512 * j, 528 + 512 * j), O256, [[-1, 4], [-16, 8], [1000, 16]], A.is_equal, -4 * j, 1)
     asel(a128("LT"), a128("BD"), [[1, 128]], A.is_gt, 0, -1)
-    asel(a128("TRI"), a128("ONE"), [[-1, 128]], A.is_gt, 0, 1)
-    iota(R("MCI", 0, 256), [[1, 8], [0, 32]], 0, True)
-    iota(R("IO1", 0, 128), [[1, 128]], 0, True)
-    iota(R("IOC", 0, 256), [[1, 256]], 0, True)
-    iota(R("G16", 0, 8), [[-16, 8]], 0, True)
+    iota(R("MCI", 0, 256), [[1, 8], [0, 32]], 0, 0)
+    iota(a128("IQF"), [[-1, 16], [0, 8]], -1025, 0)
+    iota(R("IOF", 0, 256), [[1, 256]], H, 0)
+    asel(a128("TRI"), a128("O256"), [[-1, 128]], A.is_ge, 0, 1)
+    asel(R("SEL2", 0, 16), R("ONE", 0, 16), [[-1, 2], [-16, 8]], A.is_equal, -1, 1)
+    asel(a128("RQ"), a128("ONE"), [[0, 16], [-16, 8]], A.is_equal, 0, 1)
+    iota(R("BC0", 0, 1024), [[-240, 8], [0, 128]], 1, 15)
+    asel(R("BC", 0, 1024), R("BC0", 0, 1024), [[-16, 8], [0, 128]], A.is_ge, 0, 1)
+    asel(R("BC", 0, 1024), R("BC", 0, 1024), [[16, 8], [0, 128]], A.is_ge, 1, -1)
+    for lo, hi in ((0, 448), (448, 896), (1024, 1472), (1472, 1920)):
+        asel(R("WZ", lo, hi), R("O256", 0, hi - lo), [[0, hi - lo]], A.is_ge, -1, 0)
     ts(c32("XI1"), c32("LI1"), 4, A.arith_shift_right, 1, A.bitwise_and)
+    ts(a128("NI"), a128("IB"), -1.0, A.mult)
     cp(R("XC", 0, 8), R("XI1", 0, 8))
+    ts(c32("LI2"), c32("LI1"), 15, A.bitwise_and)
     ts(R("NX", 0, 8), R("XC", 0, 8), -1.0, A.mult, 1.0, A.add)
-    for u, v, b in ((0, 0, "IB"), (0, 1, "UP"), (1, 0, "DN"), (1, 1, "IB")):
-        ts(a128("L%d%d" % (u, v)), a128(b), R("XC" if u else "NX", 0, 1), A.mult)
+    for u, v, b in ((0, 0, "IB"), (1, 1, "IB"), (0, 1, "UP"), (1, 0, "DN")):
+        ts(a128("L%d%d" % (u, v)), a128(b), col("XC" if u else "NX"), A.mult)
+
+    def strip(Z, w):
+        ts(R(Z, 0, 144), R("ZM", 0, 144), w, A.mult)
 
     def constants_0():
-        ts(a128("NI"), a128("IB"), -1.0, A.mult)
-        ms(R("MQ", 0, 2048), 0.0)
-        for gr in range(8):
-            cp(R("MQ", 16 * gr, 2048, 129), R("BD", 16 * gr, 16 * gr + 16))
+        ts(a128("N256"), a128("IB"), -256.0, A.mult)
+        ts(a128("I2"), a128("IB"), 2.0, A.mult)
+        ts(c32("Q0"), c32("LI2"), 0.0, A.is_equal)
+        ts(c32("Q1"), c32("LI2"), 1.0, A.is_equal)
 
     def constants_1():
-        ts(c32("LI2"), c32("LI1"), 15, A.bitwise_and)
-        ts(c32("Q0"), c32("LI2"), 0.0, A.is_equal)
-        ts(c32("Q1"), c32("LI2"), 1.0, A.is_equal, 4096.0, A.mult)
+        cp(R("ZM", 15, 128, 16), R("BD", 0, 128, 16))
         tt(c32("LANE"), c32("LI2"), c32("LI0"), A.add)
-        tt(c32("QC"), c32("Q0"), c32("Q1"), A.add)
+        tt(c32("QD"), c32("Q1"), c32("Q0"), A.subtract)
+        strip("ZA0", col("Q0"))
+        ts(c32("NB0"), c32("LANE"), 1536.0, A.add, 1.0 / 2048, A.mult)
         ts(c32("LQ"), c32("LANE"), 1.0 / 512, A.mult)
-        act(R("AQ", 0, 2048), R("MQ", 0, 2048), scale=R("QC", 0, 1))
-        ts(c32("LQ2"), c32("LQ"), 2.0, A.add)
-        ms(R("ONEF", 0, 8), 1.0)
-        ts(c32("NB0"), c32("LANE"), 1536.0, A.add)
-        cp(R("WTF", 0, 2), R("WTI", 0, 2))
-
-    def weighted(k):
-        act(R("W%d" % (k + 1), 0, 2048), R("MQ", 0, 2048), scale=R("WTF", k, k + 1))
+        strip("ZAD", col("QD"))
 
     def constants_2():
-        ts(c32("TC"), c32("LANE"), 128.0, A.add)
-        ts(c32("TM"), c32("LANE"), -383.0, A.add)
+        cp(R("WTF", 0, 2), R("WTI", 0, 2))
+        strip("ZMN", -1.0)
+        strip("ZM2", 2.0)
         ts(R("MC", 0, 256), R("MCI", 0, 256), 0.125, A.mult)
-        for s in range(2):
-            ts(R("SELC", 8 * s, 8 * s + 8), R("BQ", 128 * s, 128 * s + 128, 16), 1.0 / 256, A.mult)
-        ts(a128("I5"), a128("IB"), -512.0, A.mult)
+        strip("ZW1", col("WTF", 0))
+        strip("ZW2", col("WTF", 1))
+
+    def constants_3():
+        ts(c32("L512"), c32("LANE"), 512.0, A.add)
+        ts(c32("NL512"), c32("LANE"), -1.0, A.mult, -512.0, A.add)
         tt(a128("LB"), a128("LT"), a128("BD"), A.subtract)
-        tt(a128("LB"), a128("LB"), a128("IB"), A.add)
-        tt(a128("LT"), a128("LB"), a128("I5"), A.add)
+        cp(a128("IQN"), a128("IQF"))
+        cp(R("IOC", 0, 256), R("IOF", 0, 256))
+        act(R("NBC", 0, 1024), R("BC", 0, 1024), scale=-1.0)
 
     def unscramble(P, src, nb):
         for k in range(nb):
@@ -257,241 +280,303 @@ def rank_program(g, core, T, topo):
                 for x in range(2):
                     mm(R(P, 2 * k + c2, 32 * nb, 2 * nb), a128("L%d%d" % (c2, x)), R(src, 32 * k + 16 * x, 32 * k + 16 * x + 16), x == 0, x == 1)
 
+    def signs(l):
+        P = "P%d" % (2 + l)
+        for r in range(4):
+            mm(R(P, 128 * r, 128 * r + 128), R("BQ", 512 * l + 128 * r, 512 * l + 128 * r + 128), a128("SGB"), True, True)
+        act(R("SG", 512 * l, 512 * l + 512), R(P, 0, 512), scale=1.0 / 256)
+
     def load_lists():
+        ts(a128("SGB"), a128("MLD"), 2.0, A.mult, -1.0, A.add)
+        ts(R("KLF", 0, 256), R("KLD", 0, 256), -1792.0, A.add)
+        signs(0)
         ts(a128("MLB"), a128("MLD"), -1.0, A.mult, 1.0, A.add)
+        vtr(R("KLH", 0, 256), R("KLF", 0, 256))
+        unscramble("P7", "KLH", 8)
         vtr(a128("MLT"), a128("MLB"))
         unscramble("P6", "MLT", 4)
-        ts(R("KLF", 0, 256), R("KLD", 0, 256), -1792.0, A.add)
-        vtr(R("KLT", 0, 256), R("KLF", 0, 256))
-        cp(R("KLH", 0, 256), R("KLT", 0, 256))
-        unscramble("P7", "KLH", 8)
         constants_0()
-        cp(R("NW", 0, 128), R("P6", 0, 128))
-        ts(R("WK", 0, 256), R("P7", 0, 256), 1792.0 + H, A.add)
+        ts(R("UL", 0, 256), R("P7", 0, 256), 1792.0 + H, A.add)
 
-    def lists():
+    def load_lists_2():
+        ts(R("WK", 0, 256), R("P7", 0, 256), 1792.0 + H, A.add)
+        cp(R("NW", 0, 128), R("P6", 0, 128))
+
+    def lists_2():
         tt(R("NKB", 0, 128), R("WK", 128, 256), R("NW", 0, 128), A.mult)
-        cp(R("UL", 0, 256), R("WK", 0, 256))
+        act(R("NXF", 0, 256), R("WK", 0, 256), F.Relu, bias=col("CNX"))
         cp(R("UL", 256, 384), R("NKB", 0, 128))
 
     def wf():
         ts(R("WF", 0, 256), R("WK", 0, 256), -1792.0 - H, A.add)
 
-    def lists_2():
-        tt(R("NKB", 128, 256), R("WK", 0, 128), R("NW", 0, 128), A.mult)
-        wf()
-        cp(R("UL", 384, 512), R("NKB", 128, 256))
-
-    ul = lambda k, l, a=0, b=32: R("UL", 128 * k + 32 * l + a, 128 * k + 32 * l + b)
+    ul = lambda k, l, a=0, b=512: R("UL", 128 * k + 32 * l + a // 16, 128 * k + 32 * l + b // 16)
     below = lambda l: R("YT", 0, H + 1536 + 512 * l)
 
-    def table(k, l):
-        n, lo, which = (("YAB", 0, 0), ("YAB", 2048, 1), ("YAP", 0, 3))["abp".index(k)]
-        act(R(n, lo + 512 * l, lo + 512 * l + 512), IND(below(l), ul(which, l)))
+    def table_p(l, a=0, b=512, q="S"):
+        (act if q == "S" else cp)(R("BP", 512 * l + a, 512 * l + b), IND(below(l), ul(2, l, a, b)))
 
-    def level(l, tables="", between=None):
-        W = below(l)
-        cut = ((0, 8), (8, 32))
-        bp = lambda a, b: R("YAP", 2048 + 512 * l + 16 * a, 2048 + 512 * l + 16 * b)
-        cp(bp(*cut[0]), IND(W, ul(2, l, *cut[0])))
-        act(bp(*cut[1]), IND(W, ul(2, l, *cut[1])))
-        for k in tables.split():
-            table(k[0], int(k[1]))
-        if between:
-            between()
-        for a, b in cut:
-            c = (16 * a, 16 * b)
-            tt(R("WT", *c), IND(W, ul(0, l, a, b)), bp(a, b), A.add)
-            tt(R("MT", *c), IND(W, ul(1, l, a, b)), R("WT", *c), A.max)
+    def level(l, out, first=None, behind=None):
+        za, yb = R("ZAB", 512 * l, 512 * l + 512), R("ZAB", 2048 + 512 * l, 2560 + 512 * l)
+        for h, (a, b) in enumerate(HALF):
+            tt(sub(za, a, b), IND(below(l), ul(0, l, a, b)), R("SG", 512 * l + a, 512 * l + b), A.mult)
+            act(sub(yb, a, b), IND(below(l), ul(1, l, a, b)))
+            if h == 0 and first:
+                first()
+            ts(R("MN", a, b), sub(za, a, b), 0.0, A.min)
+            if out:
+                mm(R("P%d" % h, 0, 256), a128("IB"), sub(yb, a, b), True, False)
+                mm(R("P%d" % h, 0, 256), a128("NI"), R("MN", a, b), False, True)
+        if behind:
+            behind()
+        if out:
+            for h, (a, b) in enumerate(HALF):
+                tt(sub(out, a, b), R("P%d" % h, 0, 256), sub(za, a, b), A.max)
+
+    def clamp(l):
         o = H + 1536 + 512 * l
-        ts(R("YT", o, o + 512), R("MT", 0, 512), 255.0, A.min)
-
-    def levels():
-        level(0, "b0 a0", lists_2)
-        level(1, "p0 b1")
-        for l in (2, 0, 1):
-            kt(l)
-        level(2, "a1 p1")
-        level(3, "b3 p3", lambda: kt_copy(2))
-        cp(R("YAB", 1536, 2048), IND(below(3), ul(0, 3)))
-        for k in "bap":
-            table(k, 2)
+        for a, b in HALF:
+            ts(R("YT", o + a, o + b), R("UU", a, b), 255.0, A.min)
 
     def kt(l):
-        P = "P%d" % (7 - l)
-        for q in range(16):
-            for k in range(2):
-                mm(R(P, q, 512, 16), R("KQ%d" % k, 128 * q, 128 * q + 128), R("WF", 128 * k + 32 * l, 128 * k + 32 * l + 32), k == 0, k == 1)
+        P = "P%d" % (5 + l)
+        for k in range(2):
+            to_row(P, k, R("NXF", 128 * k + 32 * l, 128 * k + 32 * l + 32), k == 0, k == 1)
 
     def kt_copy(l):
-        ts(R("KT", 512 * l, 512 * l + 512), R("P%d" % (7 - l), 0, 512), 1.0 / 256, A.mult)
+        act(R("KT", 512 * l, 512 * l + 512), R("P%d" % (5 + l), 0, 512), scale=1.0 / 256)
 
-    def step(st, fill):
+    def levels(first):
+        UU = R("UU", 0, 512)
+        sg = signs if first else lambda l: None
+        level(0, UU, load_lists_2 if first else None, lambda: (lists_2(), sg(1), table_p(0)))
+        clamp(0)
+        level(1, UU, None, lambda: (sg(2), table_p(1)))
+        clamp(1)
+        level(2, UU, None, lambda: (sg(3), table_p(2), kt(1)))
+        clamp(2)
+        level(3, None)
+        kt(2)
+        table_p(3, 0, 256)
+        table_p(3, 256, 512, "V")
+        kt_copy(1)
+        kt_copy(2)
+
+    def step(st, fill, fill2):
         Wc, Wn = "WAB%d" % (st % 2), "WAB%d" % ((st + 1) % 2)
+        I, NI = a128("IB"), a128("NI")
+        mn = R("MN", 0, 512)
         if st == 0:
             D = R("TG", 0, 512)
-            y = (R("YAB", 1536, 2048), R("YAB", 3584, 4096))
-            yn = (R("YAP", 1536, 2048), R("YAP", 3584, 4096))
-            ka, kb = R("WK", 96, 128), R("WK", 224, 256)
+            za, yb, bp = R("ZAB", 1536, 2048), R("ZAB", 3584, 4096), R("BP", 1536, 2048)
         else:
             D = R(Wc, 1024, 1536)
-            y = (R("Y2", 0, 512), R("Y2", 512, 1024))
-            yn = (R("Y2P", 0, 512), R("Y2P", 512, 1024))
-            cp(y[1], IND(R("YAB", 2048, 3584), c32("NL")))
-            act(yn[1], IND(R("YAP", 2048, 3584), c32("NL")))
-            act(y[0], IND(R("YAB", 0, 1536), c32("NL")))
-            act(yn[0], IND(R("YAP", 0, 1536), c32("NL")))
+            za, yb, bp = R("Y2", 0, 512), R("Y2", 512, 1024), R("Y2P", 0, 512)
+            nl = lambda a, b: R("NL", a // 16, b // 16)
+            cut = 256 if st == 1 else 512
+            act(yb, IND(R("ZAB", 2048, 3584), c32("NL")))
+            act(sub(bp, 0, cut), IND(R("BP", 0, 1536), nl(0, cut)))
+            for a, b in HALF:
+                cp(sub(za, a, b), IND(R("ZAB", 0, 1536), nl(a, b)))
+                ts(sub(mn, a, b), sub(za, a, b), 0.0, A.min)
             if st == 1:
                 act(R("KTG", 0, 512), IND(R("KT", 0, 1536), c32("NL")))
-            ka, kb = c32("KAI"), c32("KBI")
-        parts = ((0, 0, 512, "P4"), (1, 0, 256, "P5"), (1, 256, 512, "P1"))
-        mm(R("P0", 0, 512), a128("IB"), D, True, True)
-        for s in range(2):
-            mm(R("P%d" % (2 + s), 0, 512), a128("IB"), D, True, False)
-        mm(R("P2", 0, 512), a128("NI"), yn[1], False, True)
-        for s, a, b, P in parts[1:] + parts[:1]:
-            mm(R(P, 0, b - a), a128("NI"), R(y[s][0], y[s][1] + a, y[s][1] + b), True, False)
-        mm(R("P3", 0, 512), a128("NI"), yn[0], False, True)
-        for s in range(2):
-            tt(R("SB", 512 * s, 512 * s + 512), y[1 - s], R("P0", 0, 512), A.is_le)
-        for s, a, b, P in parts:
-            c = (512 * s + a, 512 * s + b)
-            tt(R(Wc, *c), R("SB", *c), R("P%d" % (2 + s), a, b), A.mult)
-            mm(R(P, 0, b - a), a128("IB"), R(Wc, *c), False, True)
-            act(R("AB", *c), R(P, 0, b - a), F.Abs)
+        PB = lambda h: R("P%d" % (2 + h), 0, 256)
+        EB = lambda h: R("P%d" % (2 + h), 256, 512)
+        EA = lambda h: R("P%d" % (4 + h), 0, 256)
+        mm(R("P0", 0, 512), I, D, True, True)
+        for h, c in enumerate(HALF):
+            mm(PB(h), I, sub(D, *c), True, False)
+        mm(R("P1", 0, 512), I, D, True, False)
+
+        def less_a(h):
+            mm(EA(h), NI, sub(za, *HALF[h]), True, False)
+            mm(EA(h), a128("I2"), sub(mn, *HALF[h]), False, False)
+
+        for h, (a, b) in enumerate(HALF):
+            mm(PB(h), I, sub(mn, a, b), False, False)
+            if h == 0:
+                less_a(0)
+            tt(R("CB", a, b), sub(za, a, b), R("P0", a, b), A.is_gt)
+            mm(PB(h), a128("N256"), R("CB", a, b), False, True)
+            act(R(Wc, 512 + a, 512 + b), PB(h), F.Relu)
         if st == 1:
-            phases("P7", 0, 32, "AQ", "KTG", 0, True, True)
+            cp(sub(bp, 256, 512), IND(R("BP", 0, 1536), nl(256, 512)))
+        mm(R("P1", 0, 256), NI, sub(bp, 0, 256), False, False)
+        for h, (a, b) in enumerate(HALF):
+            mm(EB(h), NI, sub(yb, a, b), True, False)
+            mm(EB(h), I, R(Wc, 512 + a, 512 + b), False, True)
+            act(R("AB", 512 + a, 512 + b), EB(h), F.Abs)
+            tt(R("SA", a, b), sub(yb, a, b), R("P0", a, b), A.is_le)
+            if h == 0:
+                mm(R("P1", 256, 512), NI, sub(bp, 256, 512), False, True)
+        less_a(1)
+        for h, (a, b) in enumerate(HALF):
+            tt(R(Wc, a, b), R("SA", a, b), R("P1", a, b), A.mult)
+            mm(EA(h), I, R(Wc, a, b), False, True)
+            act(R("AB", a, b), EA(h), F.Abs)
         fill()
-        if st == 1:
-            ts(c32("KPI"), c32("P7"), (1792.0 + H) * 4097.0, A.add)
-            ts(c32("KAI"), c32("KPI"), 4095, A.bitwise_and)
-            ts(c32("KBI"), c32("KPI"), 12, A.arith_shift_right)
-        if st < 2:
-            tt(c32("DK"), kb, ka, A.subtract)
-        phases("P6", 0, 64, "MQ", "AB", 0, True, True)
+        if st == 0:
+            tt(c32("DK"), R("NXF", 224, 256), R("NXF", 96, 128), A.subtract)
+            na, dk = R("NXF", 96, 128), c32("DK")
+        elif st == 1:
+            phases("P7", 0, 32, "ZA0", "KTG", 0, True, True)
+            phases("P7", 32, 32, "ZAD", "KTG", 0, True, True)
+            na, dk = c32("P7"), c32("P7", 1)
+        if st:
+            mm(R("P6", 0, 64), a128("N256"), R("DEAD", 0, 64), True, False)
+        phases("P6", 0, 64, "ZM", "AB", 0, st == 0, True)
+        fill2()
         cp(R("ES", 0, 64), R("P6", 0, 64))
         tt(c32("TOB"), c32("ES", 1), c32("ES"), A.is_lt)
-        if st == 0:
-            tt(c32("S1"), c32("TOB"), c32("LQ"), A.add)
-        else:
-            ts(c32("S1"), c32("TOB"), -2.0, A.add)
-            tt(c32("S3"), c32("S1"), c32("LV"), A.mult)
-            tt(c32("S1"), c32("S3"), c32("LQ2"), A.add)
         if st < 2:
-            tt(c32("S2"), c32("TOB"), c32("DK"), A.mult)
+            tt(c32("S2"), c32("TOB"), dk, A.mult)
+        tt(c32("S1"), c32("TOB"), c32("SB" if st else "LQ"), A.add)
+        if st < 2:
+            tt(c32("CHI"), c32("S2"), na, A.add)
         ts(c32("SEL"), c32("S1"), 512.0, A.mult)
         win = R(Wc, 0, 1024 if st == 0 else 1536)
         act(R(Wn, 1024, 1280), IND(win, R("SEL", 0, 16)))
         if st < 2:
-            tt(c32("CHI"), c32("S2"), ka, A.add)
-            ts(c32("NL"), c32("CHI"), -1536.0 - H, A.add, 0.0, A.max)
+            ts(c32("NL"), c32("CHI"), -1.0, A.add, 0.0, A.max)
+        X = "ST" if st == 0 else "NS"
         cp(R(Wn, 1280, 1536), IND(win, R("SEL", 16, 32)))
 
         def rest():
-            X = "ST" if st == 0 else "NS"
-            ts(c32("S3"), c32("TOB"), 2048.0, A.mult)
-            tt(c32(X, 1), c32("ES", 1), c32("ES"), A.min)
-            tt(c32(X), c32("S3"), c32("NB" if st else "NB0"), A.add)
+            tt(c32(X), c32("TOB"), c32("NB" if st else "NB0"), A.add)
+            tt(c32(X, 1), c32("ES"), c32("ES", 1), A.min)
+            if st < 2:
+                ts(c32("NB"), c32("CHI"), -1.0, A.add, 1.0 / 2048, A.mult)
             if st:
                 tt(R("DS", 0, 64), R("NS", 0, 64), R("ST", 0, 64), A.subtract)
+            if st:
                 tt(R("DS", 0, 64), R("DS", 0, 64), R("LV", 0, 64), A.mult)
+            if st == 1:
+                ts(c32("S3"), c32("CHI"), 1.0, A.is_ge)
+            if st:
                 tt(R("ST", 0, 64), R("DS", 0, 64), R("ST", 0, 64), A.add)
-            if st == 0:
-                for k in range(2):
-                    ts(c32("LV", k), c32("CHI"), 1536.0 + H, A.is_ge)
-            elif st == 1:
-                ts(c32("S3"), c32("CHI"), 1536.0 + H, A.is_ge)
-                for k in range(2):
+            for k in range(2 if st < 2 else 0):
+                if st == 0:
+                    ts(c32("LV", k), c32("CHI"), 1.0, A.is_ge)
+                else:
                     tt(c32("LV", k), c32("LV", k), c32("S3"), A.mult)
             if st < 2:
-                ts(c32("NB"), c32("CHI"), -1536.0 - H, A.add, 0.0, A.max)
+                ts(c32("DEAD"), c32("LV"), -16.0, A.mult, 16.0, A.add)
+                ts(c32("S3"), c32("LV"), -2.0, A.mult, 2.0, A.add)
+                tt(c32("SB"), c32("S3"), c32("LQ"), A.add)
         return rest
+
+    BY_S, RELU = (1, 2, 3), (4, 5, 6, 7)
 
     def donors(t, rest):
         D = R("WAB1", 1024, 1536)
         SL = "SL%d" % t
-        phases("P6", 0, 32, "W1", "WAB1", 1024, True, True)
-        phases("P6", 32, 32, "W2", "WAB1", 1024, True, True)
+        I, NI = a128("IB"), a128("NI")
+        phases("P6", 0, 32, "ZW1", "WAB1", 1024, True, True)
+        phases("P6", 32, 32, "ZW2", "WAB1", 1024, True, True)
         rest()
-        cp(c32("KEYU"), c32("ST"))
-        act(R("YC", 0, 512), IND(R("YAB", 0, 4096), c32("KEYU")))
-        ts(c32("XG"), c32("ST"), 2048.0, A.is_ge)
-        tt(c32("S3"), c32("XG"), c32("ST"), A.add)
-        ts(c32("XH"), c32("S3"), -2048.0, A.add)
-        ms(R(SL, 0, 128), SENT)
-        cp(R("US", 0, 64), R("P6", 0, 64))
-        cp(c32("U1I"), c32("US"))
-        tt(c32("PRI"), c32("US"), c32("US", 1), A.mult)
+        ts(c32("KEYU"), c32("ST"), 2048.0, A.mult)
+        ts(c32("KI"), c32("ST"), 2048.0, A.mult)
+        act(R("YC", 0, 512), IND(R("ZAB", 0, 4096), c32("KEYU")), F.Abs)
+        ts(c32("QCI"), c32("KI"), 15, A.bitwise_and)
+        ts(c32("QCI", 1), c32("KI"), 4, A.arith_shift_right)
+        cp(c32("U1I"), c32("P6"))
+        cp(R("QCH", 0, 64), R("QCI", 0, 64))
+        tt(c32("PRI"), c32("U1I"), c32("P6", 1), A.mult)
         ts(c32("UMI"), c32("U1I"), 127, A.bitwise_and)
         ts(c32("SHI"), c32("PRI"), 5, A.arith_shift_right)
         ts(c32("STR"), c32("UMI"), 2.0, A.mult, 1.0, A.add)
+        tt(c32("CA"), c32("SHI"), c32("P6", 1), A.add)
+        for k in range(2):
+            act(c32("SR2", k), c32("STR"), scale=2.0)
         for k in range(4):
             act(c32("SR4", k), c32("STR"), scale=4.0)
-        tt(c32("CA"), c32("SHI"), c32("US", 1), A.add)
-        for k in range(2):
-            ts(c32("SR2", k), c32("UMI"), 4.0, A.mult, 2.0, A.add)
         tt(c32("CA", 1), c32("CA"), c32("STR"), A.add)
+        ms(R(SL, 0, 128), SENT)
+        ts(R("CI", 0, 64), R("CA", 0, 64), 1023, A.bitwise_and)
         tt(R("CA", 64, 128), R("CA", 0, 64), R("SR2", 0, 64), A.add)
-        ts(R("CI", 0, 128), R("CA", 0, 128), 1023, A.bitwise_and)
-        cp(R("CU", 0, 128), R("CI", 0, 128))
+        cp(R("CU", 0, 64), R("CI", 0, 64))
+        ts(R("CI", 64, 128), R("CA", 64, 128), 1023, A.bitwise_and)
         LW = R("YT", H, H + LIB)
-        for k, m in enumerate((1, 3)):
-            act(R("GV", 512 * k, 512 * k + 512), IND(LW, c32("CU", m)))
-            mm(R("P%d" % (4 + 3 * k), 0, 512), a128("IB"), R("GV", 512 * k, 512 * k + 512), True, False)
-            mm(R("P%d" % (4 + 3 * k), 0, 512), a128("NI"), D, False, True)
-        for h in range(2):
-            mm(R("P%d" % (2 + h), 0, 128), a128("IB"), R("MC", 128 * h, 128 * h + 128), True, False)
+        df = lambda m, b="DF": R(b, 512 * m, 512 * m + 512)
+        banks = {1: "P0", 2: "P1", 3: "P4"}
 
-        def cand(m):
-            c = (512 * m, 512 * m + 512)
-            if m in (1, 3):
-                act(R("DF", *c), R("P4" if m == 1 else "P7", 0, 512), F.Abs)
+        def fetch(m):
+            if m in BY_S:
+                k = BY_S.index(m)
+                act(df(k, "GV"), IND(LW, c32("CU", m)))
+                mm(R(banks[m], 0, 512), NI, D, True, False)
+                mm(R(banks[m], 0, 512), I, df(k, "GV"), False, True)
             else:
-                tt(R("DF", *c), IND(LW, c32("CU", m)), D, A.subtract)
-                act(R("DF", *c), R("DF", *c), F.Abs)
-        cand(0)
-        cand(1)
+                tt(df(RELU.index(m), "DD") if m in RELU else df(m), IND(LW, c32("CU", m)), D, A.subtract)
+
+        def size(m):
+            if m in RELU:
+                ts(df(m), df(RELU.index(m), "DD"), 0.0, A.max)
+            else:
+                act(df(m), R(banks[m], 0, 512) if m in BY_S else df(m), F.Abs, scale=0.5)
+
+        def sums(P, lo, m, last):
+            phases(P, lo, 64, "ZM2", "DF", 512 * m, False, last)
+
+        mm(R("P5", 0, 512), I, R("YC", 0, 512), True, False)
+        to_row("P5", 0, c32("QCH"), False, False)
+        to_row("P5", 1, c32("QCH", 1), False, False)
+        for P, lo, n in (("P2", 0, 128), ("P3", 128, 64), ("P7", 192, 64)):
+            mm(R(P, 0, n), I, R("MC", lo, lo + n), True, False)
+        fetch(1)
         tt(R("CA", 128, 256), R("CA", 0, 128), R("SR4", 0, 128), A.add)
-        cand(2)
+        cp(R("CU", 64, 128), R("CI", 64, 128))
+        fetch(0)
         ts(R("CI", 128, 256), R("CA", 128, 256), 1023, A.bitwise_and)
+        fetch(2)
         cp(R("CU", 128, 256), R("CI", 128, 256))
-        cand(3)
-        phases("P2", 0, 64, "MQ", "DF", 0, False, False)
-        phases("P2", 64, 64, "MQ", "DF", 1024, False, True)
-        mm(R("P5", 0, 512), a128("IB"), R("YC", 0, 512), True, False)
-        for o, w, x in to_rows("P5", "KQ0", c32("XH")):
-            mm(o, w, x, False, False)
-        cand(4)
-        cand(5)
-        phases("P3", 0, 64, "MQ", "DF", 2048, False, False)
-        cand(6)
+        size(1)
+        fetch(4)
+        size(0)
+        fetch(3)
+        fetch(5)
+        sums("P2", 0, 0, False)
+        size(4)
+        size(5)
+        phases("P3", 0, 64, "ZMN", "DD", 0, False, False)
+        size(2)
+        fetch(6)
+        sums("P3", 0, 4, True)
+        size(3)
+        fetch(7)
+        sums("P2", 64, 2, True)
+        mm(c32("P6"), I, c32("L512"), True, False)
+        phases("P7", 0, 64, "ZMN", "DD", 1024, False, False)
+        size(6)
+        size(7)
+        sums("P7", 0, 6, True)
         cp(R("B1", 0, 128), R("P2", 0, 128))
-        cand(7)
         tt(R("B3", 0, 64), R("B1", 0, 64), R("B1", 64, 128), A.min)
-        phases("P3", 64, 64, "MQ", "DF", 3072, False, True)
         tt(R("B2", 0, 64), R("B3", 0, 64), R("P3", 0, 64), A.min)
-        tt(R("B1", 0, 64), R("B2", 0, 64), R("P3", 64, 128), A.min)
-        tt(c32("BEST"), c32("B1"), c32("B1", 1), A.min)
-        tt(c32("HIT"), c32("BEST"), c32("ST", 1), A.is_lt)
+        tt(c32("B4"), c32("B2"), c32("B2", 1), A.min)
+        tt(c32("B5"), c32("B4"), c32("P7"), A.min)
+        tt(c32("BEST"), c32("B5"), c32("P7", 1), A.min)
         ts(c32("B8"), c32("BEST"), 8.0, A.mult)
+        tt(c32("HIT"), c32("BEST"), c32("ST", 1), A.is_lt)
+        ts(c32("MI"), c32("B8"), 7, A.bitwise_and)
         emit("V", lambda: g.vector.tensor_tensor_scan(ap(c32("INC")), ap(R("ONE", 0, 32)), ap(c32("HIT")), 0.0, A.mult, A.add),
              [R("ONE", 0, 32), c32("HIT")], [c32("INC")])
-        ts(c32("MI"), c32("B8"), 7, A.bitwise_and)
-        mm(R("P6", 0, 32), a128("LT"), c32("HIT"), True, False)
-        mm(R("P6", 0, 32), a128("BD"), c32("INC"), False, True)
         tt(c32("MTT"), c32("MI"), c32("STR"), A.mult)
+        tt(c32("HL"), c32("HIT"), c32("NL512"), A.mult)
         tt(c32("HD"), c32("MTT"), c32("CA"), A.add)
+        mm(c32("P6"), a128("LB"), c32("HIT"), False, False)
+        mm(c32("P6"), a128("BD"), c32("INC"), False, False)
+        mm(c32("P6"), I, c32("HL"), False, True)
         ts(c32("DNI"), c32("HD"), 1023, A.bitwise_and)
-        ts(c32("DNH"), c32("DNI"), float(H), A.add)
-        for k, (o, w, x) in enumerate(to_rows("P5", "KQ1", c32("DNH"))):
-            mm(o, w, x, False, k == 15)
+        cp(c32("DNH"), c32("DNI"))
+        to_row("P5", 2, c32("DNH"), False, True)
+        cp(c32("SLOT"), c32("P6"))
         act(R("PAY", 0, 512), R("P5", 0, 512))
-        ts(c32("CT"), c32("P6"), -383.0, A.is_lt)
-        tt(c32("RD"), c32("P6"), c32("TM"), A.subtract)
-        tt(c32("RE"), c32("RD"), c32("CT"), A.mult)
-        tt(c32("RF"), c32("RE"), c32("TC"), A.add)
-        cp(c32("SLOT"), c32("RF"))
-        cp(IND(R(SL, 0, 640), c32("SLOT")), R("PAY", 0, 512))
+        for h in range(8):
+            mm(R("P%d" % (h // 4), 128 * (h % 4), 128 * (h % 4) + 128), a128("N256"), a128("TRI"), h % 4 == 0, False)
+        mm(a128("P4"), I, a128("IQN"), True, False)
+        cp(IND(R(SL, 0, 1536), c32("SLOT")), R("PAY", 0, 512))
 
     def send(t):
         dst = T.cores[(rank + 1) % n_ranks]
@@ -501,43 +586,38 @@ def rank_program(g, core, T, topo):
         g.remote_dma(T["LAND%d" % t][:, :], ap(sl), T.sem["arr%d" % t], T.sem["snt%d" % t], pid, rid, topo.mask(core, dst))
 
     def grafts(t):
-        g8 = lambda b: R(b, 0, 8)
         at = lambda gr, w=128: (w * gr, w * gr + w)
-        mm(R("P6", 0, 16), R("SL%d" % t, 0, 128), R("SELC", 0, 16), True, True)
-        cp(R("XI", 0, 16), R("P6", 0, 16))
-        ts(R("XS", 0, 16), R("XI", 0, 16), 8, A.arith_shift_right)
-        cp(R("XF", 0, 16), R("XS", 0, 16))
-        for gr in range(8):
-            if gr > 2:
-                act(R("DG", *at(gr)), a128("IB"), scale=R("XF", gr, gr + 1))
-            else:
-                ts(R("DG", *at(gr)), a128("IB"), R("XF", gr, gr + 1), A.mult)
-            mm(R("P%d" % (gr // 4), *at(gr % 4)), a128("TRI"), R("DG", *at(gr)), True, True)
-        ts(g8("XN"), g8("XF"), 0.0, A.is_lt)
-        ts(g8("DX"), R("XF", 8, 16), 0.0, A.max)
-        tt(g8("XK"), g8("XN"), g8("XF"), A.add)
-        ts(g8("KI"), g8("XK"), 2047.0, A.add)
-        ts(g8("QI"), g8("KI"), 15, A.bitwise_and)
-        ts(g8("CQ"), g8("KI"), 4, A.arith_shift_right)
-        tt(g8("QF"), g8("G16"), g8("QI"), A.subtract)
-        cp(g8("CF"), g8("CQ"))
-        for gr in range(8):
-            act(R("QD", *at(gr)), R("IO1", 0, 128), F.Abs, bias=R("QF", gr, gr + 1))
+        XH = a128("XH")
+        ts(XH, R("SL%d" % t, 0, 128), 1.0 / 256, A.mult, 1024.5 + 1.0 / 512, A.add)
+        mm(R("P6", 0, 16), XH, R("SEL2", 0, 16), True, True)
         for h in range(2):
-            act(R("QH", *at(h, 512)), R("QD", *at(h, 512)), F.Relu, scale=-1.0, bias=R("ONEF", 0, 1))
+            mm(R("P%d" % h, 0, 512), XH, R("NBC", *at(h, 512)), False, False)
+            for gr in range(4 * h, 4 * h + 4):
+                mm(R("P%d" % h, *at(gr % 4)), R("BC", *at(gr)), XH, False, gr % 4 == 3)
+        mm(a128("P4"), XH, a128("RQ"), False, False)
+        ts(R("XF", 0, 16), R("P6", 0, 16), H - 1025.0, A.add)
+
+        def one_hot(gr):
+            ts(R("CHM", *at(gr, 256)), R("IOC", 0, 256), col("XF", gr), A.is_equal, col("XF", 8 + gr), A.mult)
+        one_hot(0)
+        for h in range(2):
+            ts(R("EQ", *at(h, 512)), R("P%d" % h, 0, 512), 0.0, A.is_equal)
+            for gr in range(4 * h, 4 * h + 4):
+                mm(R("P4", gr, 128, 8), R("EQ", *at(gr)), R("S16", 0, 16), False, gr == 7)
+        for gr in (1, 2, 3):
+            one_hot(gr)
+        ts(R("WZ", 896, 1024), a128("P4"), 0.0, A.is_equal)
         for gr in range(8):
-            ts(R("EQ", *at(gr)), R("P%d" % (gr // 4), *at(gr % 4)), R("XF", gr, gr + 1), A.is_equal)
-            mm(R("P4", gr, gr + 1), R("EQ", *at(gr)), R("ONE", 0, 1), True, True)
-        ts(g8("WIN"), R("P4", 0, 8), 0.0, A.is_equal)
-        tt(g8("DD"), g8("WIN"), g8("DX"), A.mult)
-        for gr in range(8):
-            ts(R("CHM", *at(gr, 256)), R("IOC", 0, 256), R("CF", gr, gr + 1), A.is_equal, R("DD", gr, gr + 1), A.mult)
-            mm(R("P5", 0, 256), R("QH", *at(gr)), R("CHM", *at(gr, 256)), gr == 0, gr == 7)
-        c = (0, 256)
-        ts(R("ZU", *c), R("P5", *c), 0.0, A.is_equal)
-        tt(R("ZT", *c), R("WK", *c), R("ZU", *c), A.mult)
-        tt(R("WK", *c), R("ZT", *c), R("P5", *c), A.add)
-        lists()
+            if gr > 3:
+                one_hot(gr)
+            o = 896 - 127 * gr
+            mm(R("P5", 0, 256), R("WZ", o, o + 1017, 8), R("CHM", *at(gr, 256)), gr == 0, gr == 7)
+
+    def merge(a, b):
+        ts(R("ZU", a, b), R("P5", a, b), 0.0, A.is_equal)
+        tt(R("ZT", a, b), R("WK", a, b), R("ZU", a, b), A.mult)
+        tt(R("WK", a, b), R("ZT", a, b), R("P5", a, b), A.add)
+        cp(R("UL", a, b), R("WK", a, b))
 
     def receive(t):
         lib = R("YT", H + 128 * t, H + 128 * t + 128)
@@ -552,48 +632,54 @@ def rank_program(g, core, T, topo):
 
     do, dko = newd(), newd()
 
-    def out(lo, hi):
-        src = R("YT", H + lo, H + hi)
+    def out(lo, hi, src):
         dma("Y", do, T.yo[:, lo:hi], ap(src), [src], [])
 
     def kids_out_1():
         for k in range(8):
             for x in range(2):
                 for c2 in range(2):
-                    mm(R("P0", 32 * k + 16 * x, 32 * k + 16 * x + 16), a128("L%d%d" % (x, c2)), R("WF", 2 * k + c2, 256, 16), c2 == 0, c2 == 1)
+                    mm(R("P2", 32 * k + 16 * x, 32 * k + 16 * x + 16), a128("L%d%d" % (x, c2)), R("WF", 2 * k + c2, 256, 16), c2 == 0, c2 == 1)
 
     def kids_out_2():
-        ts(R("KOF", 0, 256), R("P0", 0, 256), 1792.0, A.add)
+        act(R("KOF", 0, 256), R("P2", 0, 256), bias=col("CNX", 1))
         vtr(R("KOT", 0, 256), R("KOF", 0, 256))
         dma("Y", dko, T.ko[:, :], ap(R("KOT", 0, 256)), [R("KOT", 0, 256)], [])
 
-    load_lists()
-    lists()
-    for k in range(2):
-        act(R("KQ%d" % k, k, 2048, 16), R("BQ", k, 2048, 16))
-    levels()
+    def last_levels():
+        yt = lambda l: R("YT", H + 1536 + 512 * l, H + 2048 + 512 * l)
+        yo = lambda l: R("YO", 512 * l, 512 * l + 512)
 
+        def cut(l):
+            act(R("YR", 0, 512), yt(l), F.Relu, scale=-1.0, bias=col("C255"))
+            act(yo(l), R("YR", 0, 512), scale=-1.0, bias=col("C255"))
+            out(1536 + 512 * l, 2048 + 512 * l, yo(l))
+        out(0, 1536, R("YT", H, H + 1536))
+        level(0, yt(0), None, lambda: (wf(), ms(col("CNX", 1), 1792.0), kids_out_1()))
+        level(1, yt(1), None, lambda: (cut(0), kids_out_2()))
+        level(2, yt(2), None, lambda: cut(1))
+        level(3, R("UU", 0, 512), None, lambda: cut(2))
+        ts(yo(3), R("UU", 0, 512), 255.0, A.min)
+        out(3072, 3584, yo(3))
+
+    load_lists()
+    levels(True)
+
+    none = lambda: None
     for t in range(2):
         first = t == 0
-        r0 = step(0, lambda: (constants_1() if first else None, kt_copy(0), kt_copy(1)))
-        r1 = step(1, lambda: (r0(), (constants_2(), weighted(0), weighted(1)) if first else None))
-        r2 = step(2, lambda: r1())
+        r0 = step(0, constants_1 if first else none, none)
+        r1 = step(1, r0, constants_2 if first else none)
+        r2 = step(2, r1, constants_3 if first else none)
         donors(t, r2)
         send(t)
         grafts(t)
+        merge(0, 256)
         receive(t)
         if first:
-            levels()
+            levels(False)
         else:
-            out(0, 1536)
-            level(0, "", wf)
-            out(1536, 2048)
-            level(1, "", kids_out_1)
-            out(2048, 2560)
-            level(2, "", kids_out_2)
-            out(2560, 3072)
-            level(3)
-            out(3072, 3584)
+            last_levels()
 
     for s in ["cV", "cS", "cP", "cG"] + ["d%d" % k for k in range(dmas[0])]:
         wait("G", s, cnt[s])

@@ -2,6 +2,8 @@ from concourse.mybir import AluOpType as A, ActivationFunctionType as F
 
 H = 16
 LIB = 1024
+MID = 1792.0
+SIDE = 2064
 SENT = -1048576.0
 
 SCRATCH, PLACE = {}, {}
@@ -20,23 +22,137 @@ def declare(dtype, text, packed=False):
         SCRATCH["SM" + dtype] = ("sbuf", [128, o], dtype)
 
 
-declare("bfloat16", "YT:3616 ZAB:4096 BP:2048 SG:2048 TG:512 WAB0:1536 WAB1:1536 Y2:1024 Y2P:512 MN:512 UU:512 CB:512 SA:512 AB:1024 DF:4096 DD:2048 "
-        "GV:2048 YO:2048 YR:512 YC:512 EQ:1024 O256:512 BQ:2048 KQ:2064 BC0:1024 BC:1024 NBC:1024 WZ:1920")
-declare("bfloat16", "LF:128 LT2:128 HIT:32 INC:32 ONE:128 IB:128 NI:128 N256:128 I2:128 BD:128 BD1:128 L00:128 L01:128 L10:128 L11:128 UP:128 DN:128 "
-        "MLB:128 MLT:128 SGB:128 LB:128 LT:128 TRI:128 MCI:256 MC:256 ZM:144 ZM2:144 ZMN:144 ZW1:144 ZW2:144 ZA0:144 ZAD:144 SEL2:16 RQ:128 S16:16 "
-        "DEAD:64", True)
-declare("float16", "KLF:256 KLH:256 WF:256 NXF:256 KTG:512 CHM:2048")
-declare("float16", "QCH:64 DNH:32 XH:128 IQN:128 IOC:256 L512:32 HL:32", True)
-declare("uint16", "UL:384 SEL:32 NL:32 KEYU:32 CU:256 SLOT:32")
+declare("bfloat16", "YT:3616 ZAB:4128 SG:2064 TG:512 WAB:1024 DA:512 DB:512 Y2:1024 ZB:512 MN:1024 UU:512 CB:512 SA:512 AB:1024 DF:4096 DD:2048 "
+        "GV:2048 LT7:7168 YO:2048 YR:512 YC:512 EQ:1024 O256:512 BQ:2048 KQ:2064 BC0:1024 BC:1024 NBC:1024")
+declare("bfloat16", "LF:128 LT2:128 HIT:32 INC:32 ONE:128 IB:128 NI:128 N256:128 I2:128 IH:128 NH:128 BD:128 BD1:128 L00:128 L01:128 L10:128 L11:128 "
+        "UP:128 DN:128 SGB:128 LB:128 LT:128 TRI:128 MCI:256 MC:256 ZM:144 ZM2:144 ZMN:144 ZW1:144 ZW2:144 ZA0:144 ZAD:144 ZR2:144 SEL1:16 RQ:128 "
+        "S16:16 WW:256", True)
+declare("float16", "KLF:256 KLH:256 WF:256 NXF:256 KTG:512 CHM:2048 WZ0:1920 WZ1:1920 ZU:256 ZT:256")
+declare("float16", "QCH:64 DNH:32 XH:128 IQN:128 IOC:256 L512:32 HL:32 DG:128", True)
+declare("uint16", "UL:256 SEL:32 NL:32 KEYU:32 CU:256 SLOT:32 LL:8")
 declare("int32", "KLD:256 MLD:128 WTI:2")
-declare("float32", "KT:1536 PAY:512 SL0:1536 SL1:1536 LAND0:128 LAND1:128 KOF:256 KOT:256 WTF:2")
-declare("float32", "WK:256 NW:128 NKB:128 TOB:32 DK:32 ES:64 Q0:32 Q1:32 QD:32 S1:32 S2:32 S3:32 LQ:32 CHI:32 ST:64 NS:64 DS:64 LV:64 NB:32 SB:32 B1:128 B2:64 "
-        "B3:64 B4:32 B5:32 BEST:32 XF:16 ZU:256 ZT:256 STR:32 SR2:64 SR4:128 LANE:32 NL512:32 NB0:32 XC:8 NX:8 IQF:128 IOF:256 C255:8 CNX:8", True)
-declare("int32", "LI:128 LY:128 U1I:32 PRI:32 SHI:32 UMI:32 CA:256 CI:256 B8:32 MI:32 MTT:32 HD:32 DNI:32 KI:32 QCI:64 XI1:32 LI0:32 LI1:32 LI2:32", True)
+declare("float32", "KT:1552 PAY:512 DR:512 SL0:1536 SL1:1536 LAND0:128 LAND1:128 KOF:256 KOT:256 WTF:2")
+declare("float32", "TOB0:32 TOB1:32 TOB2:32 T2:32 DK:32 ES0:64 ES1:64 ES2:64 Q0:32 Q1:32 Q2:32 QD:32 S1:32 S2:32 LQ:32 CH0:32 CH1:32 CH2:32 ST:64 NS:64 "
+        "DS:64 DT:64 LV:64 B1:128 B2:64 B3:64 B4:32 B5:32 BEST:32 XF:16 STR:32 SR2:64 SR4:128 LANE:32 NL512:32 XC:8 NX:8 IQF:128 IOF:256 C255:8 CNX:8 "
+        "CMID:8 CNM:8", True)
+declare("int32", "LI:128 LY:128 U1I:32 PRI:32 SHI:32 UMI:32 CA:256 B8:32 MI:32 MTT:32 HD:32 DNI:32 KI:32 QCI:64 XI1:32 LI0:32 LI1:32 LI2:32", True)
 for _k in range(8):
     SCRATCH["P%d" % _k] = ("psum", [128, 512], "float32")
 
-SEMAPHORES = ["cV", "cS", "cP", "cG", "arr0", "arr1", "snt0", "snt1"] + ["d%d" % k for k in range(16)]
+SEMAPHORES = ["cV", "cS", "cP", "cG", "arr0", "arr1", "snt0", "snt1"] + ["d%d" % k for k in range(25)]
+
+GATHER, SCATTER, PE, WAKE, WAKE_SAME = 1.56, 3.8, 0.5, 180.0, 140.0
+PASSES, SWEEPS, SHORT, LEAD = 4, 3, 78, 1000.0
+ORDER = []
+
+
+def arrange(calls):
+    n = len(calls)
+    cost = [c["cost"] for c in calls]
+    after, before = [[] for _ in range(n)], [[] for _ in range(n)]
+    for k, c in enumerate(calls):
+        for d, by_sem in c["deps"].items():
+            gap = calls[d]["late"] + ((WAKE_SAME if calls[d]["q"] == c["q"] else WAKE) if by_sem else 0.0)
+            after[d].append((k, gap))
+            before[k].append((d, gap))
+
+    def run(users, makers, way, ready):
+        left = [len(m) for m in makers]
+        pool, free, order, end = {}, {}, [], [0.0] * n
+        for k in range(n):
+            free[calls[k]["q"]] = 0.0
+            if not left[k]:
+                pool.setdefault(calls[k]["q"], []).append(k)
+        while len(order) < n:
+            now, q = min((max(free[q], min(ready[k] for k in p)), q) for q, p in pool.items() if p)
+            k = max((k for k in pool[q] if ready[k] <= now), key=lambda k: (way[k], -k))
+            for y in pool[q]:
+                if now < ready[y] < now + cost[k]:
+                    if max(ready[y] + way[y], ready[y] + cost[y] + way[k]) < max(now + way[k], now + cost[k] + way[y]):
+                        now, k = ready[y], y
+            pool[q].remove(k)
+            order.append(k)
+            end[k] = free[q] = now + cost[k]
+            for u, gap in users[k]:
+                ready[u] = max(ready[u], end[k] + gap)
+                left[u] -= 1
+                if not left[u]:
+                    pool.setdefault(calls[u]["q"], []).append(u)
+        return order, end
+
+    way = [0.0] * n
+    for k in reversed(range(n)):
+        way[k] = cost[k] + max([gap + way[u] for u, gap in after[k]], default=calls[k]["late"])
+    lead = [LEAD if c["cost"] <= SHORT and c["q"] in "PV" and any(calls[u]["q"] != c["q"] for u, gap in after[k]) else 0.0 for k, c in enumerate(calls)]
+    best = None
+    for _ in range(PASSES):
+        order, end = run(after, before, [w + x for w, x in zip(way, lead)], [0.0] * n)
+        total = max(e + c["late"] for e, c in zip(end, calls))
+        if best is None or total < best[0]:
+            best = (total, order)
+        way = run(before, after, end, [c["late"] for c in calls])[1]
+    return polish(calls, best[1], before)
+
+
+def polish(calls, order, before):
+    n = len(calls)
+    qs = {}
+    for k in order:
+        qs.setdefault(calls[k]["q"], []).append(k)
+    cost = [c["cost"] for c in calls]
+    late = [c["late"] for c in calls]
+
+    def times():
+        end, why, at, free, seq = [None] * n, [None] * n, {q: 0 for q in qs}, {q: 0.0 for q in qs}, []
+        moved = True
+        while moved:
+            moved = False
+            for q, L in qs.items():
+                i, t = at[q], free[q]
+                while i < len(L):
+                    k = L[i]
+                    s, w = t, (L[i - 1] if i else None)
+                    for d, gap in before[k]:
+                        e = end[d]
+                        if e is None:
+                            break
+                        if e + gap > s:
+                            s, w = e + gap, d
+                    else:
+                        t = end[k] = s + cost[k]
+                        why[k] = w
+                        seq.append(k)
+                        i += 1
+                        continue
+                    break
+                if i > at[q]:
+                    at[q], free[q], moved = i, t, True
+        if len(seq) < n:
+            return 1e18, 1e18, None, None
+        return max(e + l for e, l in zip(end, late)), sum(end), why, (seq, end)
+
+    best = times()
+    for _ in range(SWEEPS):
+        k = max(range(n), key=lambda k: best[3][1][k] + late[k])
+        path = []
+        while k is not None:
+            path.append(k)
+            k = best[2][k]
+        for y, x in zip(path, path[1:]):
+            L = qs[calls[y]["q"]]
+            if calls[x]["q"] != calls[y]["q"]:
+                continue
+            for k, moves in ((y, (-1, -2, -3, -4)), (x, (1, 2, 3, 4))):
+                i = L.index(k)
+                for m in moves:
+                    if 0 <= i + m < len(L):
+                        L.insert(i + m, L.pop(i))
+                        t = times()
+                        if t[0] < best[0] - 1 or (t[0] <= best[0] and t[1] < best[1] - 1):
+                            best = t
+                            break
+                        L.insert(i, L.pop(i + m))
+    return best[3][0]
 
 
 def rank_program(g, core, T, topo):
@@ -45,23 +161,21 @@ def rank_program(g, core, T, topo):
         return
     n_ranks = len(T.cores)
     ENG = {"V": g.vector, "S": g.scalar, "P": g.tensor, "G": g, "Y": g.sync}
-    cnt = {s: 0 for s in SEMAPHORES}
-    seen = {q: {} for q in ENG}
-    clocks = {}
+    calls = []
     acc = {}
     dmas = [0]
 
     def ap(r):
         if r[0] == "ind":
             return ap(r[1]).indirect(ap(r[2]))
-        b, lo, hi, st, p0, p1 = r
+        b, lo, hi, st = r
         if b in PLACE:
             b, o = PLACE[b]
             lo, hi = lo + o, hi + o
-        return T[b][p0:p1, lo:hi] if st == 1 else T[b][p0:p1, lo:hi:st]
+        return T[b][:, lo:hi] if st == 1 else T[b][:, lo:hi:st]
 
-    def R(b, lo, hi, st=1, p0=0, p1=128):
-        return (b, lo, hi, st, p0, p1)
+    def R(b, lo, hi, st=1):
+        return (b, lo, hi, st)
 
     def sub(r, a, b):
         return R(r[0], r[1] + a, r[1] + b)
@@ -69,65 +183,48 @@ def rank_program(g, core, T, topo):
     def is_psum(b):
         return b[0] == "P" and len(b) == 2
 
-    def wait(q, sem, n):
-        if seen[q].get(sem, 0) >= n:
-            return
-        ENG[q].wait_ge(T.sem[sem], n)
-        s = seen[q]
-        for k, v in list(clocks.get((sem, n), {}).items()) + [(sem, n)]:
-            s[k] = max(s.get(k, 0), v)
-
-    def sync_for(q, reads, writes):
-        need = {}
+    def emit(q, fn, reads, writes, cost, sem=None, late=0.0):
+        me, deps = len(calls), {}
         for rs, w in ((reads, False), (writes, True)):
-            for (b, lo, hi, st, p0, p1) in rs:
+            for (b, lo, hi, st) in rs:
                 ps = is_psum(b)
                 if ps:
-                    lo, hi, p0, p1 = 0, 512, 0, 128
-                for (q2, sem, n, lo2, hi2, a0, a1, w2) in acc.get(b, ()):
-                    if lo2 >= hi or hi2 <= lo or a0 >= p1 or a1 <= p0:
+                    lo, hi = 0, 512
+                for (k, lo2, hi2, w2) in acc.get(b, ()):
+                    same = calls[k]["q"] == q
+                    if lo2 >= hi or hi2 <= lo or not (w or w2 or (ps and not same)):
                         continue
-                    if ps and q2 == q and (q == "P" or not (w or w2)):
-                        continue
-                    if not ps and not (w or w2):
-                        continue
-                    need[sem] = max(need.get(sem, 0), cnt[sem] if sem[0] == "d" else n)
-        for sem in sorted(need, key=lambda s: -sum(clocks.get((s, need[s]), {}).values())):
-            wait(q, sem, need[sem])
-
-    def note(q, sem, n, reads, writes):
+                    deps[k] = calls[k]["sem"] is not None and not (same and q == "P")
         for rs, w in ((writes, True), (reads, False)):
-            for (b, lo, hi, st, p0, p1) in rs:
-                if is_psum(b):
-                    lo, hi, p0, p1 = 0, 512, 0, 128
+            for (b, lo, hi, st) in rs:
+                ps = is_psum(b)
+                if ps:
+                    lo, hi = 0, 512
                 L = acc.setdefault(b, [])
-                if w and st == 1:
-                    L[:] = [e for e in L if not (lo <= e[3] and e[4] <= hi and p0 <= e[5] and e[6] <= p1)]
-                elif not w:
-                    L[:] = [e for e in L if not (e[0] == q and not e[7] and lo <= e[3] and e[4] <= hi and p0 <= e[5] and e[6] <= p1)]
-                L.append((q, sem, n, lo, hi, p0, p1, w))
+                if w and (st == 1 or ps):
+                    L[:] = [e for e in L if not (lo <= e[1] and e[2] <= hi)]
+                elif ps:
+                    L[:] = [e for e in L if e[3] or e[0] == me or calls[e[0]]["q"] == q]
+                L.append((me, lo, hi, w))
+        calls.append(dict(q=q, fns=fn if isinstance(fn, list) else [fn], deps=deps, cost=cost, late=late, sem="c" + q if sem is None else sem or None))
 
-    def emit(q, fn, reads, writes):
-        sync_for(q, reads, writes)
-        sem = "c" + q
-        cnt[sem] += 1
-        fn().then_inc(T.sem[sem], 1)
-        clocks[(sem, cnt[sem])] = dict(seen[q], **{sem: cnt[sem]})
-        note(q, sem, cnt[sem], reads, writes)
-
-    def newd():
+    def dma(q, out, in_, reads, writes):
         dmas[0] += 1
-        return "d%d" % (dmas[0] - 1)
+        emit(q, lambda: ENG[q].dma_start(out, in_), reads, writes, 60.0, "d%d" % (dmas[0] - 1), 1500.0)
 
-    def dma(q, sem, out, in_, reads, writes):
-        sync_for(q, reads, writes)
-        cnt[sem] += 16
-        ENG[q].dma_start(out, in_).then_inc(T.sem[sem], 16)
-        c = dict(seen[q])
-        for k, v in clocks.get((sem, cnt[sem] - 16), {}).items():
-            c[k] = max(c.get(k, 0), v)
-        clocks[(sem, cnt[sem])] = c
-        note(q, sem, cnt[sem], reads, writes)
+    def width(r):
+        return 16 * width(r[2]) if r[0] == "ind" else -(-(r[2] - r[1]) // r[3])
+
+    def narrow(*rs):
+        return all(not is_psum(r[0]) and SCRATCH[PLACE.get(r[0], r)[0]][2][-2:] == "16" for r in rs)
+
+    def vcost(out, *ins):
+        if out[0] == "ind":
+            return 50 + SCATTER * width(out)
+        if any(r[0] == "ind" for r in ins):
+            return 50 + (1.8 if len(ins) == 2 else GATHER) * width(out)
+        both = 2.0 if len(ins) == 2 and not any(is_psum(r[0]) for r in ins) else 1.0
+        return max(72, width(out) * both * (0.5 if narrow(out, *ins) else 1.0))
 
     def IND(win, off):
         return ("ind", win, off)
@@ -143,348 +240,258 @@ def rank_program(g, core, T, topo):
         return ap(x) if isinstance(x, tuple) else x
 
     def tt(out, a, b, op):
-        emit("V", lambda: g.vector.tensor_tensor(ap(out), ap(a), ap(b), op), rd(a, b), [out])
+        emit("V", lambda: g.vector.tensor_tensor(ap(out), ap(a), ap(b), op), rd(a, b), [out], vcost(out, a, b))
 
     def ts(out, a, s1, op0, s2=None, op1=None):
         if op1 is None:
-            emit("V", lambda: g.vector.tensor_scalar(ap(out), ap(a), num(s1), None, op0), rd(a, s1), [out])
+            emit("V", lambda: g.vector.tensor_scalar(ap(out), ap(a), num(s1), None, op0), rd(a, s1), [out], vcost(out, a))
         else:
-            emit("V", lambda: g.vector.tensor_scalar(ap(out), ap(a), num(s1), num(s2), op0, op1), rd(a, s1, s2), [out])
+            emit("V", lambda: g.vector.tensor_scalar(ap(out), ap(a), num(s1), num(s2), op0, op1), rd(a, s1, s2), [out], vcost(out, a))
 
     def cp(out, a):
         if out[0] == "ind":
-            emit("V", lambda: g.vector.tensor_copy(ap(out), ap(a)), rd(a) + [out[2]], [out[1]])
+            emit("V", lambda: g.vector.tensor_copy(ap(out), ap(a)), rd(a) + [out[2]], [out[1]], vcost(out, a))
         else:
-            emit("V", lambda: g.vector.tensor_copy(ap(out), ap(a)), rd(a), [out])
+            emit("V", lambda: g.vector.tensor_copy(ap(out), ap(a)), rd(a), [out], vcost(out, a))
 
     def ms(out, v):
-        emit("V", lambda: g.vector.memset(ap(out), v), [], [out])
+        emit("V", lambda: g.vector.memset(ap(out), v), [], [out], vcost(out))
 
     def vtr(out, a):
-        emit("V", lambda: g.vector.transpose(ap(out), ap(a)), [a], [out])
+        emit("V", lambda: g.vector.transpose(ap(out), ap(a)), [a], [out], vcost(out, a))
 
-    def act(out, a, func=F.Identity, scale=1.0, bias=0.0):
-        emit("S", lambda: g.scalar.activation(ap(out), ap(a), func, bias=num(bias), scale=num(scale)), rd(a, scale, bias), [out])
+    def act(out, a, func=F.Identity, scale=1.0, bias=0.0, also=()):
+        emit("S", lambda: g.scalar.activation(ap(out), ap(a), func, bias=num(bias), scale=num(scale)), rd(a, scale, bias, *also), [out],
+             65 + width(out) * (GATHER if a[0] == "ind" else 1.0))
 
-    def mm(out, lhsT, rhs, start, stop):
-        emit("P", lambda: g.tensor.matmul(ap(out), ap(lhsT), ap(rhs), start, stop), [lhsT, rhs], [out])
+    def mms(items):
+        emit("P", [lambda x=x: g.tensor.matmul(ap(x[0]), ap(x[1]), ap(x[2]), x[3], x[4]) for x in items], [r for x in items for r in x[1:3]],
+             [x[0] for x in items], sum(PE * max(min(64, width(x[1])), width(x[2])) for x in items))
+
+    def mm(*x):
+        mms([x])
 
     def iota(out, pat, base, chm, small=True):
         if small:
-            emit("G", lambda: g.iota(ap(out), pat, base, chm, allow_small_or_imprecise_dtypes=True), [], [out])
+            emit("G", lambda: g.iota(ap(out), pat, base, chm, allow_small_or_imprecise_dtypes=True), [], [out], 130 + 2 * width(out))
         else:
-            emit("G", lambda: g.iota(ap(out), pat, base, chm), [], [out])
+            emit("G", lambda: g.iota(ap(out), pat, base, chm), [], [out], 130 + 2 * width(out))
 
     def asel(out, in_, pat, op, base, chm):
-        emit("G", lambda: g.affine_select(ap(out), ap(in_), pat, op, 0.0, base, chm), [in_], [out])
+        emit("G", lambda: g.affine_select(ap(out), ap(in_), pat, op, 0.0, base, chm), [in_], [out], 170 + 2 * width(out))
 
-    def phases(out_b, lo, n, Z, src, s0, first, last):
-        for q in range(16):
-            mm(R(out_b, lo, lo + n), R(Z, 15 - q, 143 - q), R(src, s0 + q, s0 + 16 * n, 16), first and q == 0, last and q == 15)
+    def phases(out, Z, src, first, last):
+        mms([(out, R(Z, 15 - q, 143 - q), R(src[0], src[1] + q, src[2], 16), first and q == 0, last and q == 15) for q in range(16)])
 
     def to_row(P, r, src, first, last):
-        for q in range(16):
-            mm(R(P, q, 512, 16), R("KQ", 16 + 128 * q - r, 144 + 128 * q - r), src, first and q == 0, last and q == 15)
+        mms([(R(P, q, 512, 16), R("KQ", 16 + 128 * q - r, 144 + 128 * q - r), src, first and q == 0, last and q == 15) for q in range(16)])
 
     a128 = lambda b: R(b, 0, 128)
+    a256 = lambda b: R(b, 0, 256)
+    a512 = lambda b: R(b, 0, 512)
     c32 = lambda b, k=0: R(b, 32 * k, 32 * k + 32)
+    c64 = lambda b: R(b, 0, 64)
     col = lambda b, k=0: R(b, k, k + 1)
     HALF = ((0, 256), (256, 512))
+    I, NI = a128("IB"), a128("NI")
 
-    dK, dM, dL, dT, dW = [newd() for _ in range(5)]
-    dma("S", dK, ap(R("KLD", 0, 256)), T.kid[:, :], [], [R("KLD", 0, 256)])
-    dma("Y", dM, ap(R("MLD", 0, 128)), T.mx[:, :], [], [R("MLD", 0, 128)])
-    dma("Y", dL, ap(R("YT", H, H + 1536)), T.lv[:, :], [], [R("YT", H, H + 1536)])
-    dma("Y", dT, ap(R("TG", 0, 512)), T.tg[:, :], [], [R("TG", 0, 512)])
-    dma("Y", dW, ap(R("WTI", 0, 2)), T.wt[:, :], [], [R("WTI", 0, 2)])
+    dma("S", ap(a256("KLD")), T.kid[:, :], [], [a256("KLD")])
+    dma("Y", ap(a128("MLD")), T.mx[:, :], [], [a128("MLD")])
+    dma("Y", ap(R("YT", H, H + 1536)), T.lv[:, :], [], [R("YT", H, H + 1536)])
+    dma("Y", ap(a512("TG")), T.tg[:, :], [], [a512("TG")])
+    dma("Y", ap(R("WTI", 0, 2)), T.wt[:, :], [], [R("WTI", 0, 2)])
 
-    O256 = R("O256", 0, 512)
+    O256 = a512("O256")
     ms(a128("ONE"), 1.0)
     ms(O256, 256.0)
-    ms(R("YT", 0, H), 0.0)
-    ms(R("KQ", 0, 16), 0.0)
-    ms(R("ZM", 0, 144), 0.0)
-    ms(R("C255", 0, 8), 255.0)
-    ms(R("CNX", 0, 8), -1535.0 - H)
+    for r in (R("YT", 0, H), R("KQ", 0, 16), R("ZM", 0, 144), R("ZAB", 0, 1), R("ZAB", 2049, SIDE + 1), R("SG", 0, 1),
+              R("KT", 0, 513)):
+        ms(r, 0.0)
+    for b, v in (("C255", 255.0), ("CNX", MID - 1535.0), ("CMID", MID), ("CNM", -MID)):
+        ms(R(b, 0, 8), v)
     ms(R("S16", 0, 16), 16.0)
-    ms(c32("DEAD", 1), 0.0)
-    ms(R("KT", 0, 512), 0.0)
-    asel(a128("IB"), a128("ONE"), [[-1, 128]], A.is_equal, 0, 1)
+    asel(I, a128("ONE"), [[-1, 128]], A.is_equal, 0, 1)
     iota(c32("LI1"), [[0, 32]], 0, 1, False)
     asel(a128("UP"), a128("ONE"), [[1, 128]], A.is_equal, -16, -1)
     asel(a128("DN"), a128("ONE"), [[1, 128]], A.is_equal, 16, -1)
     for j in range(4):
         asel(R("BQ", 512 * j, 512 * j + 512), O256, [[-1, 4], [-16, 8], [0, 16]], A.is_equal, -4 * j, 1)
+        asel(R("KQ", 16 + 512 * j, 528 + 512 * j), O256, [[-1, 4], [-16, 8], [1000, 16]], A.is_equal, -4 * j, 1)
     asel(a128("BD1"), a128("ONE"), [[-16, 8], [0, 16]], A.is_ge, 0, 1)
     asel(a128("BD"), a128("BD1"), [[16, 8], [0, 16]], A.is_ge, 15, -1)
     iota(c32("LI0"), [[16, 32]], 0, 0, False)
-    for j in range(4):
-        asel(R("KQ", 16 + 512 * j, 528 + 512 * j), O256, [[-1, 4], [-16, 8], [1000, 16]], A.is_equal, -4 * j, 1)
     asel(a128("LT"), a128("BD"), [[1, 128]], A.is_gt, 0, -1)
-    iota(R("MCI", 0, 256), [[1, 8], [0, 32]], 0, 0)
+    iota(a256("MCI"), [[1, 8], [0, 32]], 0, 0)
     iota(a128("IQF"), [[-1, 16], [0, 8]], -1025, 0)
-    iota(R("IOF", 0, 256), [[1, 256]], H, 0)
+    iota(a256("IOF"), [[SIDE // 16, 2], [1, 128]], -int(MID), 0)
     asel(a128("TRI"), a128("O256"), [[-1, 128]], A.is_ge, 0, 1)
-    asel(R("SEL2", 0, 16), R("ONE", 0, 16), [[-1, 2], [-16, 8]], A.is_equal, -1, 1)
+    asel(R("SEL1", 0, 8), R("ONE", 0, 8), [[-16, 8]], A.is_equal, -1, 1)
     asel(a128("RQ"), a128("ONE"), [[0, 16], [-16, 8]], A.is_equal, 0, 1)
     iota(R("BC0", 0, 1024), [[-240, 8], [0, 128]], 1, 15)
     asel(R("BC", 0, 1024), R("BC0", 0, 1024), [[-16, 8], [0, 128]], A.is_ge, 0, 1)
     asel(R("BC", 0, 1024), R("BC", 0, 1024), [[16, 8], [0, 128]], A.is_ge, 1, -1)
+    act(R("NBC", 0, 1024), R("BC", 0, 1024), scale=-1.0)
     for lo, hi in ((0, 448), (448, 896), (1024, 1472), (1472, 1920)):
-        asel(R("WZ", lo, hi), R("O256", 0, hi - lo), [[0, hi - lo]], A.is_ge, -1, 0)
+        for b in ("WZ0", "WZ1"):
+            act(R(b, lo, hi), R("O256", 0, hi - lo), scale=0.0)
     ts(c32("XI1"), c32("LI1"), 4, A.arith_shift_right, 1, A.bitwise_and)
-    ts(a128("NI"), a128("IB"), -1.0, A.mult)
     cp(R("XC", 0, 8), R("XI1", 0, 8))
-    ts(c32("LI2"), c32("LI1"), 15, A.bitwise_and)
     ts(R("NX", 0, 8), R("XC", 0, 8), -1.0, A.mult, 1.0, A.add)
     for u, v, b in ((0, 0, "IB"), (1, 1, "IB"), (0, 1, "UP"), (1, 0, "DN")):
         ts(a128("L%d%d" % (u, v)), a128(b), col("XC" if u else "NX"), A.mult)
-
-    def strip(Z, w):
+    for b, w in (("NI", -1.0), ("N256", -256.0), ("I2", 2.0), ("IH", 0.5), ("NH", -0.5)):
+        ts(a128(b), I, w, A.mult)
+    ts(c32("LI2"), c32("LI1"), 15, A.bitwise_and)
+    for k in range(3):
+        ts(c32("Q%d" % k), c32("LI2"), float(k), A.is_equal)
+    tt(c32("QD"), c32("Q1"), c32("Q0"), A.subtract)
+    cp(R("WTF", 0, 2), R("WTI", 0, 2))
+    cp(R("ZM", 15, 128, 16), R("BD", 0, 128, 16))
+    for Z, w in (("ZA0", col("Q0")), ("ZAD", col("QD")), ("ZR2", col("Q2")), ("ZMN", -1.0), ("ZM2", 2.0), ("ZW1", col("WTF", 0)), ("ZW2", col("WTF", 1))):
         ts(R(Z, 0, 144), R("ZM", 0, 144), w, A.mult)
-
-    def constants_0():
-        ts(a128("N256"), a128("IB"), -256.0, A.mult)
-        ts(a128("I2"), a128("IB"), 2.0, A.mult)
-        ts(c32("Q0"), c32("LI2"), 0.0, A.is_equal)
-        ts(c32("Q1"), c32("LI2"), 1.0, A.is_equal)
-
-    def constants_1():
-        cp(R("ZM", 15, 128, 16), R("BD", 0, 128, 16))
-        tt(c32("LANE"), c32("LI2"), c32("LI0"), A.add)
-        tt(c32("QD"), c32("Q1"), c32("Q0"), A.subtract)
-        strip("ZA0", col("Q0"))
-        ts(c32("NB0"), c32("LANE"), 1536.0, A.add, 1.0 / 2048, A.mult)
-        ts(c32("LQ"), c32("LANE"), 1.0 / 512, A.mult)
-        strip("ZAD", col("QD"))
-
-    def constants_2():
-        cp(R("WTF", 0, 2), R("WTI", 0, 2))
-        strip("ZMN", -1.0)
-        strip("ZM2", 2.0)
-        ts(R("MC", 0, 256), R("MCI", 0, 256), 0.125, A.mult)
-        strip("ZW1", col("WTF", 0))
-        strip("ZW2", col("WTF", 1))
-
-    def constants_3():
-        ts(c32("L512"), c32("LANE"), 512.0, A.add)
-        ts(c32("NL512"), c32("LANE"), -1.0, A.mult, -512.0, A.add)
-        tt(a128("LB"), a128("LT"), a128("BD"), A.subtract)
-        cp(a128("IQN"), a128("IQF"))
-        cp(R("IOC", 0, 256), R("IOF", 0, 256))
-        act(R("NBC", 0, 1024), R("BC", 0, 1024), scale=-1.0)
-
-    def unscramble(P, src, nb):
-        for k in range(nb):
-            for c2 in range(2):
-                for x in range(2):
-                    mm(R(P, 2 * k + c2, 32 * nb, 2 * nb), a128("L%d%d" % (c2, x)), R(src, 32 * k + 16 * x, 32 * k + 16 * x + 16), x == 0, x == 1)
-
-    def signs(l):
-        P = "P%d" % (2 + l)
-        for r in range(4):
-            mm(R(P, 128 * r, 128 * r + 128), R("BQ", 512 * l + 128 * r, 512 * l + 128 * r + 128), a128("SGB"), True, True)
-        act(R("SG", 512 * l, 512 * l + 512), R(P, 0, 512), scale=1.0 / 256)
+    tt(c32("LANE"), c32("LI2"), c32("LI0"), A.add)
+    ts(c32("CH2"), c32("LANE"), 1537.0, A.add)
+    ts(c32("L512"), c32("LANE"), 512.0, A.add)
+    ts(c32("NL512"), c32("LANE"), -1.0, A.mult, -512.0, A.add)
+    ts(c32("LQ"), c32("LANE"), 1.0 / 512, A.mult)
+    ts(a256("MC"), a256("MCI"), 0.125, A.mult)
+    tt(a128("LB"), a128("LT"), a128("BD"), A.subtract)
+    cp(a128("IQN"), a128("IQF"))
+    cp(a256("IOC"), a256("IOF"))
 
     def load_lists():
+        ts(a256("KLF"), a256("KLD"), -MID, A.add)
+        vtr(a256("KLH"), a256("KLF"))
+        mms([(R("P7", 2 * k + c2, 256, 16), a128("L%d%d" % (c2, x)), R("KLH", 32 * k + 16 * x, 32 * k + 16 * x + 16), x == 0, x == 1)
+             for k in range(8) for c2 in range(2) for x in range(2)])
+        ts(a256("UL"), a256("P7"), MID + H, A.add)
+        act(a256("WF"), a256("P7"))
         ts(a128("SGB"), a128("MLD"), 2.0, A.mult, -1.0, A.add)
-        ts(R("KLF", 0, 256), R("KLD", 0, 256), -1792.0, A.add)
-        signs(0)
-        ts(a128("MLB"), a128("MLD"), -1.0, A.mult, 1.0, A.add)
-        vtr(R("KLH", 0, 256), R("KLF", 0, 256))
-        unscramble("P7", "KLH", 8)
-        vtr(a128("MLT"), a128("MLB"))
-        unscramble("P6", "MLT", 4)
-        constants_0()
-        ts(R("UL", 0, 256), R("P7", 0, 256), 1792.0 + H, A.add)
+        for l in range(4):
+            P = "P%d" % (2 + l)
+            for r in range(4):
+                mm(R(P, 128 * r, 128 * r + 128), R("BQ", 512 * l + 128 * r, 512 * l + 128 * r + 128), a128("SGB"), True, True)
+            act(R("SG", 1 + 512 * l, 513 + 512 * l), a512(P), scale=1.0 / 256)
 
-    def load_lists_2():
-        ts(R("WK", 0, 256), R("P7", 0, 256), 1792.0 + H, A.add)
-        cp(R("NW", 0, 128), R("P6", 0, 128))
+    def lists():
+        act(a256("NXF"), a256("WF"), F.Relu, bias=col("CNX"))
+        for l in (1, 2):
+            P = "P%d" % (5 + l)
+            for k in range(2):
+                to_row(P, k, R("NXF", 128 * k + 32 * l, 128 * k + 32 * l + 32), k == 0, k == 1)
+            act(R("KT", 1 + 512 * l, 513 + 512 * l), a512(P), scale=1.0 / 256)
 
-    def lists_2():
-        tt(R("NKB", 0, 128), R("WK", 128, 256), R("NW", 0, 128), A.mult)
-        act(R("NXF", 0, 256), R("WK", 0, 256), F.Relu, bias=col("CNX"))
-        cp(R("UL", 256, 384), R("NKB", 0, 128))
-
-    def wf():
-        ts(R("WF", 0, 256), R("WK", 0, 256), -1792.0 - H, A.add)
-
-    ul = lambda k, l, a=0, b=512: R("UL", 128 * k + 32 * l + a // 16, 128 * k + 32 * l + b // 16)
+    ul = lambda k, l, a, b: R("UL", 128 * k + 32 * l + a // 16, 128 * k + 32 * l + b // 16)
     below = lambda l: R("YT", 0, H + 1536 + 512 * l)
+    tab = lambda b, o, l: R(b, o + 1 + 512 * l, o + 513 + 512 * l)
+    yt = lambda l: R("YT", H + 1536 + 512 * l, H + 2048 + 512 * l)
 
-    def table_p(l, a=0, b=512, q="S"):
-        (act if q == "S" else cp)(R("BP", 512 * l + a, 512 * l + b), IND(below(l), ul(2, l, a, b)))
-
-    def level(l, out, first=None, behind=None):
-        za, yb = R("ZAB", 512 * l, 512 * l + 512), R("ZAB", 2048 + 512 * l, 2560 + 512 * l)
-        for h, (a, b) in enumerate(HALF):
-            tt(sub(za, a, b), IND(below(l), ul(0, l, a, b)), R("SG", 512 * l + a, 512 * l + b), A.mult)
-            act(sub(yb, a, b), IND(below(l), ul(1, l, a, b)))
-            if h == 0 and first:
-                first()
-            ts(R("MN", a, b), sub(za, a, b), 0.0, A.min)
+    def level(l, out, cut):
+        za, yb, mn = tab("ZAB", 0, l), tab("ZAB", SIDE, l), R("MN", 512 * (l % 2), 0)
+        for h, c in enumerate(((0, 288), (288, 512)) if out else HALF):
+            tt(sub(za, *c), IND(below(l), ul(0, l, *c)), sub(tab("SG", 0, l), *c), A.mult)
+            act(sub(yb, *c), IND(below(l), ul(1, l, *c)))
+            ts(sub(mn, *c), sub(za, *c), 0.0, A.min)
             if out:
-                mm(R("P%d" % h, 0, 256), a128("IB"), sub(yb, a, b), True, False)
-                mm(R("P%d" % h, 0, 256), a128("NI"), R("MN", a, b), False, True)
-        if behind:
-            behind()
-        if out:
-            for h, (a, b) in enumerate(HALF):
-                tt(sub(out, a, b), R("P%d" % h, 0, 256), sub(za, a, b), A.max)
+                P = R("P%d" % (2 * (l % 2) + h), 0, c[1] - c[0])
+                mm(P, I, sub(yb, *c), True, False)
+                mm(P, NI, sub(mn, *c), False, True)
+                tt(R("UU", *c) if cut else sub(out, *c), P, sub(za, *c), A.max)
+                if cut:
+                    ts(sub(out, *c), R("UU", *c), 255.0, A.min)
 
-    def clamp(l):
-        o = H + 1536 + 512 * l
-        for a, b in HALF:
-            ts(R("YT", o + a, o + b), R("UU", a, b), 255.0, A.min)
+    def levels():
+        lists()
+        for l in range(4):
+            level(l, yt(l) if l < 3 else None, True)
 
-    def kt(l):
-        P = "P%d" % (5 + l)
-        for k in range(2):
-            to_row(P, k, R("NXF", 128 * k + 32 * l, 128 * k + 32 * l + 32), k == 0, k == 1)
-
-    def kt_copy(l):
-        act(R("KT", 512 * l, 512 * l + 512), R("P%d" % (5 + l), 0, 512), scale=1.0 / 256)
-
-    def levels(first):
-        UU = R("UU", 0, 512)
-        sg = signs if first else lambda l: None
-        level(0, UU, load_lists_2 if first else None, lambda: (lists_2(), sg(1), table_p(0)))
-        clamp(0)
-        level(1, UU, None, lambda: (sg(2), table_p(1)))
-        clamp(1)
-        level(2, UU, None, lambda: (sg(3), table_p(2), kt(1)))
-        clamp(2)
-        level(3, None)
-        kt(2)
-        table_p(3, 0, 256)
-        table_p(3, 256, 512, "V")
-        kt_copy(1)
-        kt_copy(2)
-
-    def step(st, fill, fill2):
-        Wc, Wn = "WAB%d" % (st % 2), "WAB%d" % ((st + 1) % 2)
-        I, NI = a128("IB"), a128("NI")
-        mn = R("MN", 0, 512)
+    def step(st):
+        TOB, ES, zb = "TOB%d" % st, "ES%d" % st, a512("ZB")
         if st == 0:
-            D = R("TG", 0, 512)
-            za, yb, bp = R("ZAB", 1536, 2048), R("ZAB", 3584, 4096), R("BP", 1536, 2048)
+            D, mn, za, yb = a512("TG"), R("MN", 512, 1024), tab("ZAB", 0, 3), tab("ZAB", SIDE, 3)
+            for c in HALF:
+                tt(sub(zb, *c), sub(yb, *c), sub(tab("SG", 0, 3), *c), A.mult)
         else:
-            D = R(Wc, 1024, 1536)
-            za, yb, bp = R("Y2", 0, 512), R("Y2", 512, 1024), R("Y2P", 0, 512)
-            nl = lambda a, b: R("NL", a // 16, b // 16)
-            cut = 256 if st == 1 else 512
-            act(yb, IND(R("ZAB", 2048, 3584), c32("NL")))
-            act(sub(bp, 0, cut), IND(R("BP", 0, 1536), nl(0, cut)))
-            for a, b in HALF:
-                cp(sub(za, a, b), IND(R("ZAB", 0, 1536), nl(a, b)))
-                ts(sub(mn, a, b), sub(za, a, b), 0.0, A.min)
+            D, mn, za, yb = a512("DA" if st == 1 else "DB"), a512("MN"), a512("Y2"), R("Y2", 512, 1024)
+            for c in HALF:
+                nl = R("NL", c[0] // 16, c[1] // 16)
+                cp(sub(za, *c), IND(R("ZAB", 0, 1537), nl))
+                act(sub(yb, *c), IND(R("ZAB", SIDE, SIDE + 1537), nl))
+                tt(sub(zb, *c), IND(R("SG", 0, 1537), nl), sub(yb, *c), A.mult)
+                ts(sub(mn, *c), sub(za, *c), 0.0, A.min)
             if st == 1:
-                act(R("KTG", 0, 512), IND(R("KT", 0, 1536), c32("NL")))
-        PB = lambda h: R("P%d" % (2 + h), 0, 256)
-        EB = lambda h: R("P%d" % (2 + h), 256, 512)
-        EA = lambda h: R("P%d" % (4 + h), 0, 256)
-        mm(R("P0", 0, 512), I, D, True, True)
+                act(a512("KTG"), IND(R("KT", 0, 1537), c32("NL")))
         for h, c in enumerate(HALF):
-            mm(PB(h), I, sub(D, *c), True, False)
-        mm(R("P1", 0, 512), I, D, True, False)
-
-        def less_a(h):
-            mm(EA(h), NI, sub(za, *HALF[h]), True, False)
-            mm(EA(h), a128("I2"), sub(mn, *HALF[h]), False, False)
-
-        for h, (a, b) in enumerate(HALF):
-            mm(PB(h), I, sub(mn, a, b), False, False)
-            if h == 0:
-                less_a(0)
-            tt(R("CB", a, b), sub(za, a, b), R("P0", a, b), A.is_gt)
-            mm(PB(h), a128("N256"), R("CB", a, b), False, True)
-            act(R(Wc, 512 + a, 512 + b), PB(h), F.Relu)
-        if st == 1:
-            cp(sub(bp, 256, 512), IND(R("BP", 0, 1536), nl(256, 512)))
-        mm(R("P1", 0, 256), NI, sub(bp, 0, 256), False, False)
-        for h, (a, b) in enumerate(HALF):
-            mm(EB(h), NI, sub(yb, a, b), True, False)
-            mm(EB(h), I, R(Wc, 512 + a, 512 + b), False, True)
-            act(R("AB", 512 + a, 512 + b), EB(h), F.Abs)
-            tt(R("SA", a, b), sub(yb, a, b), R("P0", a, b), A.is_le)
-            if h == 0:
-                mm(R("P1", 256, 512), NI, sub(bp, 256, 512), False, True)
-        less_a(1)
-        for h, (a, b) in enumerate(HALF):
-            tt(R(Wc, a, b), R("SA", a, b), R("P1", a, b), A.mult)
-            mm(EA(h), I, R(Wc, a, b), False, True)
-            act(R("AB", a, b), EA(h), F.Abs)
-        fill()
+            PD, EA, PA = a256("P%d" % h), R("P%d" % h, 256, 512), a256("P%d" % (4 + h))
+            PB, EB = a256("P%d" % (2 + h)), R("P%d" % (2 + h), 256, 512)
+            d, wa, wb = sub(D, *c), R("WAB", *c), sub(R("WAB", 512, 0), *c)
+            mm(PD, I, d, True, True)
+            mm(PB, I, d, True, False)
+            mm(PB, I, sub(mn, *c), False, False)
+            tt(R("CB", *c), sub(za, *c), PD, A.is_gt)
+            mm(PB, a128("N256"), R("CB", *c), False, True)
+            act(wb, PB, F.Relu)
+            mm(EB, NI, sub(yb, *c), True, False)
+            mm(EB, I, wb, False, True)
+            act(sub(R("AB", 512, 0), *c), EB, F.Abs)
+            tt(R("SA", *c), sub(yb, *c), PD, A.is_le)
+            mm(PA, I, d, True, False)
+            mm(PA, a128("NH"), sub(yb, *c), False, False)
+            mm(PA, a128("IH"), sub(zb, *c), False, True)
+            tt(wa, R("SA", *c), PA, A.mult)
+            mm(EA, NI, sub(za, *c), True, False)
+            mm(EA, a128("I2"), sub(mn, *c), False, False)
+            mm(EA, I, wa, False, True)
+            act(R("AB", *c), EA, F.Abs)
         if st == 0:
-            tt(c32("DK"), R("NXF", 224, 256), R("NXF", 96, 128), A.subtract)
             na, dk = R("NXF", 96, 128), c32("DK")
+            tt(dk, R("NXF", 224, 256), na, A.subtract)
         elif st == 1:
-            phases("P7", 0, 32, "ZA0", "KTG", 0, True, True)
-            phases("P7", 32, 32, "ZAD", "KTG", 0, True, True)
             na, dk = c32("P7"), c32("P7", 1)
-        if st:
-            mm(R("P6", 0, 64), a128("N256"), R("DEAD", 0, 64), True, False)
-        phases("P6", 0, 64, "ZM", "AB", 0, st == 0, True)
-        fill2()
-        cp(R("ES", 0, 64), R("P6", 0, 64))
-        tt(c32("TOB"), c32("ES", 1), c32("ES"), A.is_lt)
+            phases(na, "ZA0", a512("KTG"), True, True)
+            phases(dk, "ZAD", a512("KTG"), True, True)
+        phases(c64("P6"), "ZM", R("AB", 0, 1024), True, True)
+        cp(c64(ES), c64("P6"))
+        tt(c32(TOB), c32(ES, 1), c32(ES), A.is_lt)
         if st < 2:
-            tt(c32("S2"), c32("TOB"), dk, A.mult)
-        tt(c32("S1"), c32("TOB"), c32("SB" if st else "LQ"), A.add)
-        if st < 2:
-            tt(c32("CHI"), c32("S2"), na, A.add)
+            tt(c32("S2"), c32(TOB), dk, A.mult)
+            tt(c32("CH%d" % st), c32("S2"), na, A.add)
+            cp(c32("NL"), c32("CH%d" % st))
+        tt(c32("S1"), c32(TOB), c32("LQ"), A.add)
         ts(c32("SEL"), c32("S1"), 512.0, A.mult)
-        win = R(Wc, 0, 1024 if st == 0 else 1536)
-        act(R(Wn, 1024, 1280), IND(win, R("SEL", 0, 16)))
-        if st < 2:
-            ts(c32("NL"), c32("CHI"), -1.0, A.add, 0.0, A.max)
-        X = "ST" if st == 0 else "NS"
-        cp(R(Wn, 1280, 1536), IND(win, R("SEL", 16, 32)))
-
-        def rest():
-            tt(c32(X), c32("TOB"), c32("NB" if st else "NB0"), A.add)
-            tt(c32(X, 1), c32("ES"), c32("ES", 1), A.min)
-            if st < 2:
-                ts(c32("NB"), c32("CHI"), -1.0, A.add, 1.0 / 2048, A.mult)
-            if st:
-                tt(R("DS", 0, 64), R("NS", 0, 64), R("ST", 0, 64), A.subtract)
-            if st:
-                tt(R("DS", 0, 64), R("DS", 0, 64), R("LV", 0, 64), A.mult)
-            if st == 1:
-                ts(c32("S3"), c32("CHI"), 1.0, A.is_ge)
-            if st:
-                tt(R("ST", 0, 64), R("DS", 0, 64), R("ST", 0, 64), A.add)
-            for k in range(2 if st < 2 else 0):
-                if st == 0:
-                    ts(c32("LV", k), c32("CHI"), 1.0, A.is_ge)
-                else:
-                    tt(c32("LV", k), c32("LV", k), c32("S3"), A.mult)
-            if st < 2:
-                ts(c32("DEAD"), c32("LV"), -16.0, A.mult, 16.0, A.add)
-                ts(c32("S3"), c32("LV"), -2.0, A.mult, 2.0, A.add)
-                tt(c32("SB"), c32("S3"), c32("LQ"), A.add)
-        return rest
+        for h, c in enumerate(HALF):
+            (cp if h and st == 2 else act)(R("DB" if st == 1 else "DA", *c), IND(R("WAB", 0, 1024), R("SEL", c[0] // 16, c[1] // 16)))
+        X, was = "ST" if st == 0 else "NS", c32("CH%d" % ((st + 2) % 3))
+        ts(c32("T2"), c32(TOB), float(SIDE), A.mult)
+        tt(c32(X), c32("T2"), was, A.add)
+        tt(c32(X, 1), c32(ES), c32(ES, 1), A.min)
+        if st:
+            for k in range(2):
+                ts(c32("LV", k), was, 1.0, A.is_ge)
+            tt(c64("DS"), c64("NS"), c64("ST"), A.subtract)
+            tt(c64("DT"), c64("DS"), c64("LV"), A.mult)
+            tt(c64("ST"), c64("DT"), c64("ST"), A.add)
 
     BY_S, RELU = (1, 2, 3), (4, 5, 6, 7)
 
-    def donors(t, rest):
-        D = R("WAB1", 1024, 1536)
+    def donors(t):
+        n = LIB if t == 0 else 128
+        for k in range(7):
+            dma("Y", ap(R("LT7", LIB * k, LIB * k + n)), ap(R("YT", H, H + n)), [R("YT", H, H + n)], [R("LT7", LIB * k, LIB * k + n)])
+        D = a512("DA")
         SL = "SL%d" % t
-        I, NI = a128("IB"), a128("NI")
-        phases("P6", 0, 32, "ZW1", "WAB1", 1024, True, True)
-        phases("P6", 32, 32, "ZW2", "WAB1", 1024, True, True)
-        rest()
-        ts(c32("KEYU"), c32("ST"), 2048.0, A.mult)
-        ts(c32("KI"), c32("ST"), 2048.0, A.mult)
-        act(R("YC", 0, 512), IND(R("ZAB", 0, 4096), c32("KEYU")), F.Abs)
+        phases(c32("P6"), "ZW1", D, True, True)
+        phases(c32("P6", 1), "ZW2", D, True, True)
+        cp(c32("KEYU"), c32("ST"))
+        act(a512("YC"), IND(R("ZAB", 0, SIDE + 2049), c32("KEYU")), F.Abs)
+        ts(c32("KI"), c32("ST"), -1.0, A.add)
         ts(c32("QCI"), c32("KI"), 15, A.bitwise_and)
         ts(c32("QCI", 1), c32("KI"), 4, A.arith_shift_right)
+        cp(c64("QCH"), c64("QCI"))
         cp(c32("U1I"), c32("P6"))
-        cp(R("QCH", 0, 64), R("QCI", 0, 64))
         tt(c32("PRI"), c32("U1I"), c32("P6", 1), A.mult)
         ts(c32("UMI"), c32("U1I"), 127, A.bitwise_and)
-        ts(c32("SHI"), c32("PRI"), 5, A.arith_shift_right)
+        ts(c32("SHI"), c32("PRI"), 5, A.arith_shift_right, 1023, A.bitwise_and)
         ts(c32("STR"), c32("UMI"), 2.0, A.mult, 1.0, A.add)
         tt(c32("CA"), c32("SHI"), c32("P6", 1), A.add)
         for k in range(2):
@@ -492,196 +499,177 @@ def rank_program(g, core, T, topo):
         for k in range(4):
             act(c32("SR4", k), c32("STR"), scale=4.0)
         tt(c32("CA", 1), c32("CA"), c32("STR"), A.add)
-        ms(R(SL, 0, 128), SENT)
-        ts(R("CI", 0, 64), R("CA", 0, 64), 1023, A.bitwise_and)
-        tt(R("CA", 64, 128), R("CA", 0, 64), R("SR2", 0, 64), A.add)
-        cp(R("CU", 0, 64), R("CI", 0, 64))
-        ts(R("CI", 64, 128), R("CA", 64, 128), 1023, A.bitwise_and)
-        LW = R("YT", H, H + LIB)
-        df = lambda m, b="DF": R(b, 512 * m, 512 * m + 512)
+        tt(R("CA", 64, 128), c64("CA"), c64("SR2"), A.add)
+        tt(R("CA", 128, 256), a128("CA"), a128("SR4"), A.add)
+        for c in ((0, 64), (64, 128), (128, 256)):
+            cp(R("CU", *c), R("CA", *c))
+        ms(a128(SL), SENT)
+        LW = R("LT7", 0, 7 * LIB)
+        df = lambda m, b="DF", n=1: R(b, 512 * m, 512 * (m + n))
         banks = {1: "P0", 2: "P1", 3: "P4"}
-
-        def fetch(m):
+        mm(a512("P5"), I, a512("YC"), True, False)
+        to_row("P5", 0, c32("QCH"), False, False)
+        to_row("P5", 1, c32("QCH", 1), False, False)
+        to_row("P5", 2, c32("L512"), False, True)
+        act(a512("PAY"), a512("P5"))
+        for m in range(8):
             if m in BY_S:
                 k = BY_S.index(m)
                 act(df(k, "GV"), IND(LW, c32("CU", m)))
-                mm(R(banks[m], 0, 512), NI, D, True, False)
-                mm(R(banks[m], 0, 512), I, df(k, "GV"), False, True)
-            else:
-                tt(df(RELU.index(m), "DD") if m in RELU else df(m), IND(LW, c32("CU", m)), D, A.subtract)
-
-        def size(m):
-            if m in RELU:
+                mm(a512(banks[m]), NI, D, True, False)
+                mm(a512(banks[m]), I, df(k, "GV"), False, True)
+                act(df(m), a512(banks[m]), F.Abs, scale=0.5)
+            elif m in RELU:
+                tt(df(RELU.index(m), "DD"), IND(LW, c32("CU", m)), D, A.subtract)
                 ts(df(m), df(RELU.index(m), "DD"), 0.0, A.max)
             else:
-                act(df(m), R(banks[m], 0, 512) if m in BY_S else df(m), F.Abs, scale=0.5)
-
-        def sums(P, lo, m, last):
-            phases(P, lo, 64, "ZM2", "DF", 512 * m, False, last)
-
-        mm(R("P5", 0, 512), I, R("YC", 0, 512), True, False)
-        to_row("P5", 0, c32("QCH"), False, False)
-        to_row("P5", 1, c32("QCH", 1), False, False)
-        for P, lo, n in (("P2", 0, 128), ("P3", 128, 64), ("P7", 192, 64)):
-            mm(R(P, 0, n), I, R("MC", lo, lo + n), True, False)
-        fetch(1)
-        tt(R("CA", 128, 256), R("CA", 0, 128), R("SR4", 0, 128), A.add)
-        cp(R("CU", 64, 128), R("CI", 64, 128))
-        fetch(0)
-        ts(R("CI", 128, 256), R("CA", 128, 256), 1023, A.bitwise_and)
-        fetch(2)
-        cp(R("CU", 128, 256), R("CI", 128, 256))
-        size(1)
-        fetch(4)
-        size(0)
-        fetch(3)
-        fetch(5)
-        sums("P2", 0, 0, False)
-        size(4)
-        size(5)
-        phases("P3", 0, 64, "ZMN", "DD", 0, False, False)
-        size(2)
-        fetch(6)
-        sums("P3", 0, 4, True)
-        size(3)
-        fetch(7)
-        sums("P2", 64, 2, True)
-        mm(c32("P6"), I, c32("L512"), True, False)
-        phases("P7", 0, 64, "ZMN", "DD", 1024, False, False)
-        size(6)
-        size(7)
-        sums("P7", 0, 6, True)
-        cp(R("B1", 0, 128), R("P2", 0, 128))
-        tt(R("B3", 0, 64), R("B1", 0, 64), R("B1", 64, 128), A.min)
-        tt(R("B2", 0, 64), R("B3", 0, 64), R("P3", 0, 64), A.min)
+                tt(df(m), IND(LW, c32("CU", m)), D, A.subtract)
+                act(df(m), df(m), F.Abs, scale=0.5)
+        for P, m, n in (("P2", 0, 4), ("P3", 4, 2), ("P7", 6, 2)):
+            mm(R(P, 0, 32 * n), I, R("MC", 32 * m, 32 * (m + n)), True, False)
+            for k in range(0, n, 2):
+                if m + k in RELU:
+                    phases(R(P, 32 * k, 32 * k + 64), "ZMN", df(RELU.index(m + k), "DD", 2), False, False)
+                phases(R(P, 32 * k, 32 * k + 64), "ZM2", df(m + k, "DF", 2), False, k == n - 2)
+        cp(a128("B1"), a128("P2"))
+        tt(c64("B3"), c64("B1"), R("B1", 64, 128), A.min)
+        tt(c64("B2"), c64("B3"), c64("P3"), A.min)
         tt(c32("B4"), c32("B2"), c32("B2", 1), A.min)
         tt(c32("B5"), c32("B4"), c32("P7"), A.min)
         tt(c32("BEST"), c32("B5"), c32("P7", 1), A.min)
-        ts(c32("B8"), c32("BEST"), 8.0, A.mult)
         tt(c32("HIT"), c32("BEST"), c32("ST", 1), A.is_lt)
-        ts(c32("MI"), c32("B8"), 7, A.bitwise_and)
-        emit("V", lambda: g.vector.tensor_tensor_scan(ap(c32("INC")), ap(R("ONE", 0, 32)), ap(c32("HIT")), 0.0, A.mult, A.add),
-             [R("ONE", 0, 32), c32("HIT")], [c32("INC")])
-        tt(c32("MTT"), c32("MI"), c32("STR"), A.mult)
+        emit("V", lambda: g.vector.tensor_tensor_scan(ap(c32("INC")), ap(c32("ONE")), ap(c32("HIT")), 0.0, A.mult, A.add),
+             [c32("ONE"), c32("HIT")], [c32("INC")], 64)
         tt(c32("HL"), c32("HIT"), c32("NL512"), A.mult)
-        tt(c32("HD"), c32("MTT"), c32("CA"), A.add)
+        mm(c32("P6"), I, c32("L512"), True, False)
         mm(c32("P6"), a128("LB"), c32("HIT"), False, False)
         mm(c32("P6"), a128("BD"), c32("INC"), False, False)
         mm(c32("P6"), I, c32("HL"), False, True)
+        cp(c32("SLOT"), c32("P6"))
+        ts(c32("B8"), c32("BEST"), 8.0, A.mult)
+        ts(c32("MI"), c32("B8"), 7, A.bitwise_and)
+        tt(c32("MTT"), c32("MI"), c32("STR"), A.mult)
+        tt(c32("HD"), c32("MTT"), c32("CA"), A.add)
         ts(c32("DNI"), c32("HD"), 1023, A.bitwise_and)
         cp(c32("DNH"), c32("DNI"))
-        to_row("P5", 2, c32("DNH"), False, True)
-        cp(c32("SLOT"), c32("P6"))
-        act(R("PAY", 0, 512), R("P5", 0, 512))
-        for h in range(8):
-            mm(R("P%d" % (h // 4), 128 * (h % 4), 128 * (h % 4) + 128), a128("N256"), a128("TRI"), h % 4 == 0, False)
-        mm(a128("P4"), I, a128("IQN"), True, False)
-        cp(IND(R(SL, 0, 1536), c32("SLOT")), R("PAY", 0, 512))
+        to_row("P5", 0, c32("DNH"), True, True)
+        act(a512("DR"), a512("P5"), scale=1.0 / 256)
+        cp(IND(R(SL, 0, 1536), c32("SLOT")), a512("PAY"))
 
     def send(t):
         dst = T.cores[(rank + 1) % n_ranks]
         rid, pid, _ = topo.addr(dst)
-        sl = R("SL%d" % t, 0, 128)
-        sync_for("G", [sl], [])
-        g.remote_dma(T["LAND%d" % t][:, :], ap(sl), T.sem["arr%d" % t], T.sem["snt%d" % t], pid, rid, topo.mask(core, dst))
+        sl = a128("SL%d" % t)
+        emit("G", lambda: g.remote_dma(T["LAND%d" % t][:, :], ap(sl), T.sem["arr%d" % t], T.sem["snt%d" % t], pid, rid, topo.mask(core, dst)),
+             [sl], [R("sent", t, t + 1)], 500.0, False, 3000.0)
 
     def grafts(t):
         at = lambda gr, w=128: (w * gr, w * gr + w)
         XH = a128("XH")
-        ts(XH, R("SL%d" % t, 0, 128), 1.0 / 256, A.mult, 1024.5 + 1.0 / 512, A.add)
-        mm(R("P6", 0, 16), XH, R("SEL2", 0, 16), True, True)
         for h in range(2):
-            mm(R("P%d" % h, 0, 512), XH, R("NBC", *at(h, 512)), False, False)
-            for gr in range(4 * h, 4 * h + 4):
-                mm(R("P%d" % h, *at(gr % 4)), R("BC", *at(gr)), XH, False, gr % 4 == 3)
-        mm(a128("P4"), XH, a128("RQ"), False, False)
-        ts(R("XF", 0, 16), R("P6", 0, 16), H - 1025.0, A.add)
-
-        def one_hot(gr):
-            ts(R("CHM", *at(gr, 256)), R("IOC", 0, 256), col("XF", gr), A.is_equal, col("XF", 8 + gr), A.mult)
-        one_hot(0)
+            mms([(R("P%d" % h, *at(k)), a128("N256"), a128("TRI"), k == 0, False) for k in range(4)])
+            mm(a128("P%d" % (2 + h)), I, a128("IQN"), True, False)
+        ts(XH, a128("SL%d" % t), 1.0 / 256, A.mult, 1024.5 + 1.0 / 512, A.add)
+        mm(R("P6", 0, 8), XH, R("SEL1", 0, 8), True, True)
+        ts(R("XF", 0, 8), R("P6", 0, 8), -1025.0 - MID, A.add)
+        phases(R("P7", 0, 8), "ZR2", XH, True, True)
+        ts(R("LL", 0, 8), R("P7", 0, 8), -1025.0 - 512.0, A.add)
+        act(a128("DG"), IND(a512("DR"), R("LL", 0, 8)), bias=col("CNM"))
+        mm(a128("P4"), a128("DG"), a128("RQ"), True, True)
         for h in range(2):
-            ts(R("EQ", *at(h, 512)), R("P%d" % h, 0, 512), 0.0, A.is_equal)
+            P, Q, WZ = "P%d" % h, "P%d" % (2 + h), "WZ%d" % h
+            mms([(a512(P), XH, R("NBC", *at(h, 512)), False, False)] + [(R(P, *at(k)), R("BC", *at(4 * h + k)), XH, False, k == 3) for k in range(4)])
+            mm(a128(Q), XH, a128("RQ"), False, False)
+            ts(R("EQ", *at(h, 512)), a512(P), 0.0, A.is_equal)
+            mms([(R(Q, gr, 128, 8), R("EQ", *at(gr)), R("S16", 0, 16), False, gr % 4 == 3) for gr in range(4 * h, 4 * h + 4)])
+            ts(R("WW", *at(h)), a128(Q), 0.0, A.is_equal)
+            tt(R(WZ, 896, 1024), R("WW", *at(h)), a128("P4"), A.mult)
             for gr in range(4 * h, 4 * h + 4):
-                mm(R("P4", gr, 128, 8), R("EQ", *at(gr)), R("S16", 0, 16), False, gr == 7)
-        for gr in (1, 2, 3):
-            one_hot(gr)
-        ts(R("WZ", 896, 1024), a128("P4"), 0.0, A.is_equal)
-        for gr in range(8):
-            if gr > 3:
-                one_hot(gr)
-            o = 896 - 127 * gr
-            mm(R("P5", 0, 256), R("WZ", o, o + 1017, 8), R("CHM", *at(gr, 256)), gr == 0, gr == 7)
-
-    def merge(a, b):
-        ts(R("ZU", a, b), R("P5", a, b), 0.0, A.is_equal)
-        tt(R("ZT", a, b), R("WK", a, b), R("ZU", a, b), A.mult)
-        tt(R("WK", a, b), R("ZT", a, b), R("P5", a, b), A.add)
-        cp(R("UL", a, b), R("WK", a, b))
+                ts(R("CHM", *at(gr, 256)), a256("IOC"), col("XF", gr), A.is_equal)
+                o = 896 - 127 * gr
+                mm(a256("P5"), R(WZ, o, o + 1017, 8), R("CHM", *at(gr, 256)), gr == 0, gr == 7)
+        ts(a256("ZU"), a256("P5"), 0.0, A.is_equal)
+        tt(a256("ZT"), a256("WF"), a256("ZU"), A.mult)
+        tt(a256("WF"), a256("ZT"), a256("P5"), A.add)
+        ts(a256("UL"), a256("WF"), MID + H, A.add)
 
     def receive(t):
         lib = R("YT", H + 128 * t, H + 128 * t + 128)
         src = T.cores[(rank - 1) % n_ranks]
-        L = "LAND%d" % t
-        g.vector.wait_ge(T.sem["arr%d" % t], len(topo.engines(src, core)))
-        ts(a128("LF"), a128(L), -700000.0, A.is_lt)
-        cp(a128("LI"), a128(L))
+        L, sent, seen = a128("LAND%d" % t), R("sent", t, t + 1), R("seen", t, t + 1)
+        n = len(topo.engines(src, core))
+        emit("V", lambda: g.vector.wait_ge(T.sem["arr%d" % t], n), [sent, R("CHM", 1792, 2048)], [L], 1.0, False)
+        emit("S", lambda: g.scalar.wait_ge(T.sem["arr%d" % t], n), [sent, R("WZ1", 896, 1024)], [seen], 1.0, False)
+        emit("S", lambda: g.scalar.activation(ap(a128("LF")), ap(L), F.Relu, scale=1.0 / SENT), [seen], [a128("LF")], 193.0)
+        cp(a128("LI"), L)
         tt(a128("LT2"), lib, a128("LF"), A.mult)
         ts(a128("LY"), a128("LI"), 255, A.bitwise_and)
         tt(lib, a128("LT2"), a128("LY"), A.add)
 
-    do, dko = newd(), newd()
-
     def out(lo, hi, src):
-        dma("Y", do, T.yo[:, lo:hi], ap(src), [src], [])
-
-    def kids_out_1():
-        for k in range(8):
-            for x in range(2):
-                for c2 in range(2):
-                    mm(R("P2", 32 * k + 16 * x, 32 * k + 16 * x + 16), a128("L%d%d" % (x, c2)), R("WF", 2 * k + c2, 256, 16), c2 == 0, c2 == 1)
-
-    def kids_out_2():
-        act(R("KOF", 0, 256), R("P2", 0, 256), bias=col("CNX", 1))
-        vtr(R("KOT", 0, 256), R("KOF", 0, 256))
-        dma("Y", dko, T.ko[:, :], ap(R("KOT", 0, 256)), [R("KOT", 0, 256)], [])
+        dma("Y", T.yo[:, lo:hi], ap(src), [src], [])
 
     def last_levels():
-        yt = lambda l: R("YT", H + 1536 + 512 * l, H + 2048 + 512 * l)
         yo = lambda l: R("YO", 512 * l, 512 * l + 512)
-
-        def cut(l):
-            act(R("YR", 0, 512), yt(l), F.Relu, scale=-1.0, bias=col("C255"))
-            act(yo(l), R("YR", 0, 512), scale=-1.0, bias=col("C255"))
-            out(1536 + 512 * l, 2048 + 512 * l, yo(l))
         out(0, 1536, R("YT", H, H + 1536))
-        level(0, yt(0), None, lambda: (wf(), ms(col("CNX", 1), 1792.0), kids_out_1()))
-        level(1, yt(1), None, lambda: (cut(0), kids_out_2()))
-        level(2, yt(2), None, lambda: cut(1))
-        level(3, R("UU", 0, 512), None, lambda: cut(2))
-        ts(yo(3), R("UU", 0, 512), 255.0, A.min)
+        for k in range(8):
+            mms([(R("P4", 32 * k + 16 * x, 32 * k + 16 * x + 16), a128("L%d%d" % (x, c2)), R("WF", 2 * k + c2, 256, 16), c2 == 0, c2 == 1)
+                 for x in range(2) for c2 in range(2)])
+        act(a256("KOF"), a256("P4"), bias=col("CMID"))
+        vtr(a256("KOT"), a256("KOF"))
+        dma("Y", T.ko[:, :], ap(a256("KOT")), [a256("KOT")], [])
+        for l in range(3):
+            level(l, yt(l), False)
+            act(a512("YR"), yt(l), F.Relu, scale=-1.0, bias=col("C255"))
+            act(yo(l), a512("YR"), scale=-1.0, bias=col("C255"))
+            out(1536 + 512 * l, 2048 + 512 * l, yo(l))
+        level(3, yo(3), True)
         out(3072, 3584, yo(3))
 
     load_lists()
-    levels(True)
-
-    none = lambda: None
     for t in range(2):
-        first = t == 0
-        r0 = step(0, constants_1 if first else none, none)
-        r1 = step(1, r0, constants_2 if first else none)
-        r2 = step(2, r1, constants_3 if first else none)
-        donors(t, r2)
+        levels()
+        for st in range(3):
+            step(st)
+        donors(t)
         send(t)
         grafts(t)
-        merge(0, 256)
         receive(t)
-        if first:
-            levels(False)
-        else:
-            last_levels()
+    last_levels()
 
-    for s in ["cV", "cS", "cP", "cG"] + ["d%d" % k for k in range(dmas[0])]:
+    if not ORDER:
+        ORDER.extend(arrange(calls))
+    cnt = {}
+    seen = {q: {} for q in ENG}
+    clocks = {}
+
+    def wait(q, sem, n):
+        if seen[q].get(sem, 0) < n:
+            ENG[q].wait_ge(T.sem[sem], n)
+            for k, v in clocks[(sem, n)].items():
+                seen[q][k] = max(seen[q].get(k, 0), v)
+
+    for k in ORDER:
+        c = calls[k]
+        need = {}
+        for d, by_sem in c["deps"].items():
+            if by_sem:
+                sem, n = calls[d]["done"]
+                need[sem] = max(need.get(sem, 0), n)
+        for sem in sorted(need, key=lambda s: -sum(clocks[(s, need[s])].values())):
+            wait(c["q"], sem, need[sem])
+        sem = c["sem"]
+        for fn in c["fns"]:
+            ins = fn()
+            if sem:
+                inc = 16 if sem[0] == "d" else 1
+                ins.then_inc(T.sem[sem], inc)
+                cnt[sem] = cnt.get(sem, 0) + inc
+        if sem:
+            c["done"] = (sem, cnt[sem])
+            clocks[c["done"]] = dict(seen[c["q"]], **{sem: cnt[sem]})
+
+    for s in sorted(cnt):
         wait("G", s, cnt[s])
     dst = T.cores[(rank + 1) % n_ranks]
     for t in range(2):

@@ -23,7 +23,7 @@ def declare(dtype, text, packed=False):
 
 
 declare("bfloat16", "YT:3616 ZAB:4128 SG:2064 TG:512 WAB:1024 DA:512 DB:512 Y2:1024 ZB:512 MN:1024 UU:512 CB:512 SA:512 AB:1024 DF:4096 DD:2048 "
-        "GV:2048 LT7:7168 YO:2048 YR:512 YC:512 EQ:1024 O256:512 BQ:2048 KQ:2064 BC0:1024 BC:1024 NBC:1024")
+        "GV:2048 RAW:2048 LT7:7168 YO:2048 YR:512 YC:512 EQ:1024 O256:512 BQ:2048 KQ:2064 BC0:1024 BC:1024 NBC:1024")
 declare("bfloat16", "LF:128 LT2:128 HIT:32 INC:32 ONE:128 IB:128 NI:128 N256:128 I2:128 IH:128 NH:128 BD:128 BD1:128 L00:128 L01:128 L10:128 L11:128 "
         "UP:128 DN:128 SGB:128 LB:128 LT:128 TRI:128 MCI:256 MC:256 ZM:144 ZM2:144 ZMN:144 ZW1:144 ZW2:144 ZA0:144 ZAD:144 ZR2:144 SEL1:16 RQ:128 "
         "S16:16 WW:256", True)
@@ -32,17 +32,17 @@ declare("float16", "QCH:64 DNH:32 XH:128 IQN:128 IOC:256 L512:32 HL:32 DG:128", 
 declare("uint16", "UL:256 SEL:32 NL:32 KEYU:32 CU:256 SLOT:32 LL:8")
 declare("int32", "KLD:256 MLD:128 WTI:2")
 declare("float32", "KT:1552 PAY:512 DR:512 SL0:1536 SL1:1536 LAND0:128 LAND1:128 KOF:256 KOT:256 WTF:2")
-declare("float32", "TOB0:32 TOB1:32 TOB2:32 T2:32 DK:32 ES0:64 ES1:64 ES2:64 Q0:32 Q1:32 Q2:32 QD:32 S1:32 S2:32 LQ:32 CH0:32 CH1:32 CH2:32 ST:64 NS:64 "
-        "DS:64 DT:64 LV:64 B1:128 B2:64 B3:64 B4:32 B5:32 BEST:32 XF:16 STR:32 SR2:64 SR4:128 LANE:32 NL512:32 XC:8 NX:8 IQF:128 IOF:256 C255:8 CNX:8 "
+declare("float32", "TOB0:32 TOB1:32 TOB2:32 T2:32 UA:64 UD:64 UM:64 DK:32 ES0:32 ES1:32 ES2:32 Q0:32 Q1:32 Q2:32 QD:32 S1:32 S2:32 LQ:32 CH0:32 CH1:32 CH2:32 ST:64 NS:64 "
+        "DS:64 DT:64 LV:64 B1:64 B2:64 B3:64 B4:64 BEST:32 XF:16 STR:32 SR2:64 SR4:128 LANE:32 NL512:32 XC:8 NX:8 IQF:128 IOF:256 C255:8 CNX:8 "
         "CMID:8 CNM:8", True)
-declare("int32", "LI:128 LY:128 U1I:32 PRI:32 SHI:32 UMI:32 CA:256 B8:32 MI:32 MTT:32 HD:32 DNI:32 KI:32 QCI:64 XI1:32 LI0:32 LI1:32 LI2:32", True)
+declare("int32", "LI:128 LY:128 UI:64 PRI:32 SHI:32 UMI:32 CA:256 B8:32 MI:32 MTT:32 HD:32 DNI:32 KI:32 QCI:64 XI1:32 LI0:32 LI1:32 LI2:32", True)
 for _k in range(8):
     SCRATCH["P%d" % _k] = ("psum", [128, 512], "float32")
 
 SEMAPHORES = ["cV", "cS", "cP", "cG", "arr0", "arr1", "snt0", "snt1"] + ["d%d" % k for k in range(25)]
 
-GATHER, SCATTER, PE, WAKE, WAKE_SAME = 1.56, 3.8, 0.5, 180.0, 140.0
-PASSES, SWEEPS, SHORT, LEAD = 4, 3, 78, 1000.0
+GATHER, SCATTER, PE, WAKE, WAKE_SAME = 1.35, 3.0, 0.42, 230.0, 250.0
+PASSES, SWEEPS, SHORT, LEAD = 4, 3, 72, 1000.0
 ORDER = []
 
 
@@ -65,11 +65,13 @@ def arrange(calls):
                 pool.setdefault(calls[k]["q"], []).append(k)
         while len(order) < n:
             now, q = min((max(free[q], min(ready[k] for k in p)), q) for q, p in pool.items() if p)
-            k = max((k for k in pool[q] if ready[k] <= now), key=lambda k: (way[k], -k))
-            for y in pool[q]:
-                if now < ready[y] < now + cost[k]:
-                    if max(ready[y] + way[y], ready[y] + cost[y] + way[k]) < max(now + way[k], now + cost[k] + way[y]):
-                        now, k = ready[y], y
+            for k in sorted((k for k in pool[q] if ready[k] <= now), key=lambda k: (-way[k], k)):
+                if not any(now < ready[y] < now + cost[k] and max(ready[y] + way[y], ready[y] + cost[y] + way[k]) < max(now + way[k], now + cost[k] + way[y])
+                           for y in pool[q]):
+                    break
+            else:
+                k = min((y for y in pool[q] if ready[y] > now), key=lambda y: (ready[y], -way[y]))
+                now = ready[k]
             pool[q].remove(k)
             order.append(k)
             end[k] = free[q] = now + cost[k]
@@ -207,6 +209,11 @@ def rank_program(g, core, T, topo):
                     L[:] = [e for e in L if e[3] or e[0] == me or calls[e[0]]["q"] == q]
                 L.append((me, lo, hi, w))
         calls.append(dict(q=q, fns=fn if isinstance(fn, list) else [fn], deps=deps, cost=cost, late=late, sem="c" + q if sem is None else sem or None))
+        return me
+
+    def chain(*ks):
+        for a, b in zip(ks, ks[1:]):
+            calls[b]["deps"].setdefault(a, False)
 
     def dma(q, out, in_, reads, writes):
         dmas[0] += 1
@@ -222,9 +229,10 @@ def rank_program(g, core, T, topo):
         if out[0] == "ind":
             return 50 + SCATTER * width(out)
         if any(r[0] == "ind" for r in ins):
-            return 50 + (1.8 if len(ins) == 2 else GATHER) * width(out)
-        both = 2.0 if len(ins) == 2 and not any(is_psum(r[0]) for r in ins) else 1.0
-        return max(72, width(out) * both * (0.5 if narrow(out, *ins) else 1.0))
+            return 50 + (1.4 if len(ins) == 2 else GATHER) * width(out)
+        if len(ins) == 2 and not any(is_psum(r[0]) for r in ins):
+            return max(66, 2.0 * width(out))
+        return max(66, width(out) * (0.5 if narrow(out, *ins) else 1.0))
 
     def IND(win, off):
         return ("ind", win, off)
@@ -240,13 +248,12 @@ def rank_program(g, core, T, topo):
         return ap(x) if isinstance(x, tuple) else x
 
     def tt(out, a, b, op):
-        emit("V", lambda: g.vector.tensor_tensor(ap(out), ap(a), ap(b), op), rd(a, b), [out], vcost(out, a, b))
+        return emit("V", lambda: g.vector.tensor_tensor(ap(out), ap(a), ap(b), op), rd(a, b), [out], vcost(out, a, b))
 
     def ts(out, a, s1, op0, s2=None, op1=None):
         if op1 is None:
-            emit("V", lambda: g.vector.tensor_scalar(ap(out), ap(a), num(s1), None, op0), rd(a, s1), [out], vcost(out, a))
-        else:
-            emit("V", lambda: g.vector.tensor_scalar(ap(out), ap(a), num(s1), num(s2), op0, op1), rd(a, s1, s2), [out], vcost(out, a))
+            return emit("V", lambda: g.vector.tensor_scalar(ap(out), ap(a), num(s1), None, op0), rd(a, s1), [out], vcost(out, a))
+        return emit("V", lambda: g.vector.tensor_scalar(ap(out), ap(a), num(s1), num(s2), op0, op1), rd(a, s1, s2), [out], vcost(out, a))
 
     def cp(out, a):
         if out[0] == "ind":
@@ -265,11 +272,11 @@ def rank_program(g, core, T, topo):
              65 + width(out) * (GATHER if a[0] == "ind" else 1.0))
 
     def mms(items):
-        emit("P", [lambda x=x: g.tensor.matmul(ap(x[0]), ap(x[1]), ap(x[2]), x[3], x[4]) for x in items], [r for x in items for r in x[1:3]],
-             [x[0] for x in items], sum(PE * max(min(64, width(x[1])), width(x[2])) for x in items))
+        return emit("P", [lambda x=x: g.tensor.matmul(ap(x[0]), ap(x[1]), ap(x[2]), x[3], x[4]) for x in items], [r for x in items for r in x[1:3]],
+                    [x[0] for x in items], sum(PE * max(min(64, width(x[1])), width(x[2])) for x in items))
 
     def mm(*x):
-        mms([x])
+        return mms([x])
 
     def iota(out, pat, base, chm, small=True):
         if small:
@@ -281,7 +288,7 @@ def rank_program(g, core, T, topo):
         emit("G", lambda: g.affine_select(ap(out), ap(in_), pat, op, 0.0, base, chm), [in_], [out], 170 + 2 * width(out))
 
     def phases(out, Z, src, first, last):
-        mms([(out, R(Z, 15 - q, 143 - q), R(src[0], src[1] + q, src[2], 16), first and q == 0, last and q == 15) for q in range(16)])
+        return mms([(out, R(Z, 15 - q, 143 - q), R(src[0], src[1] + q, src[2], 16), first and q == 0, last and q == 15) for q in range(16)])
 
     def to_row(P, r, src, first, last):
         mms([(R(P, q, 512, 16), R("KQ", 16 + 128 * q - r, 144 + 128 * q - r), src, first and q == 0, last and q == 15) for q in range(16)])
@@ -386,12 +393,14 @@ def rank_program(g, core, T, topo):
     tab = lambda b, o, l: R(b, o + 1 + 512 * l, o + 513 + 512 * l)
     yt = lambda l: R("YT", H + 1536 + 512 * l, H + 2048 + 512 * l)
 
-    def level(l, out, cut):
+    def level(l, out, cut, tables=False):
         za, yb, mn = tab("ZAB", 0, l), tab("ZAB", SIDE, l), R("MN", 512 * (l % 2), 0)
+        if tables and l:
+            za, yb = R("RAW", 1024 * (l % 2), 1024 * (l % 2) + 512), R("RAW", 1024 * (l % 2) + 512, 1024 * (l % 2) + 1024)
         for h, c in enumerate(((0, 288), (288, 512)) if out else HALF):
             tt(sub(za, *c), IND(below(l), ul(0, l, *c)), sub(tab("SG", 0, l), *c), A.mult)
             act(sub(yb, *c), IND(below(l), ul(1, l, *c)))
-            ts(sub(mn, *c), sub(za, *c), 0.0, A.min)
+            ts(sub(mn, *c), sub(za, *c), 0.0, A.min, -255.0, A.max)
             if out:
                 P = R("P%d" % (2 * (l % 2) + h), 0, c[1] - c[0])
                 mm(P, I, sub(yb, *c), True, False)
@@ -399,11 +408,15 @@ def rank_program(g, core, T, topo):
                 tt(R("UU", *c) if cut else sub(out, *c), P, sub(za, *c), A.max)
                 if cut:
                     ts(sub(out, *c), R("UU", *c), 255.0, A.min)
+        if tables and l:
+            for c in HALF if l == 3 else ((0, 512),):
+                ts(sub(tab("ZAB", 0, l), *c), sub(za, *c), 255.0, A.min, -255.0, A.max)
+                ts(sub(tab("ZAB", SIDE, l), *c), sub(yb, *c), 255.0, A.min)
 
     def levels():
         lists()
         for l in range(4):
-            level(l, yt(l) if l < 3 else None, True)
+            level(l, yt(l) if l < 3 else None, False, True)
 
     def step(st):
         TOB, ES, zb = "TOB%d" % st, "ES%d" % st, a512("ZB")
@@ -450,9 +463,19 @@ def rank_program(g, core, T, topo):
             na, dk = c32("P7"), c32("P7", 1)
             phases(na, "ZA0", a512("KTG"), True, True)
             phases(dk, "ZAD", a512("KTG"), True, True)
-        phases(c64("P6"), "ZM", R("AB", 0, 1024), True, True)
-        cp(c64(ES), c64("P6"))
-        tt(c32(TOB), c32(ES, 1), c32(ES), A.is_lt)
+        phases(c32("P6"), "ZMN", R("AB", 512, 1024), True, False)
+        phases(c32("P6"), "ZM", a512("AB"), False, True)
+        phases(c32("P4"), "ZM", R("AB", 512, 1024), True, True)
+        ts(c32(TOB), c32("P6"), 0.0, A.is_gt)
+        ts(c32(ES), c32("P6"), 0.0, A.min)
+        if st == 2:
+            for k in range(2):
+                P = ("P5", "P7")[k]
+                phases(c64(P), "ZW%d" % (k + 1), R("WAB", 0, 1024), True, True)
+                act(c32("UA", k), c32(P))
+                tt(c32("UD", k), c32(P, 1), c32("UA", k), A.subtract)
+                tt(c32("UM", k), c32("UD", k), c32(TOB), A.mult)
+                tt(c32("UI", k), c32("UM", k), c32("UA", k), A.add)
         if st < 2:
             tt(c32("S2"), c32(TOB), dk, A.mult)
             tt(c32("CH%d" % st), c32("S2"), na, A.add)
@@ -464,7 +487,7 @@ def rank_program(g, core, T, topo):
         X, was = "ST" if st == 0 else "NS", c32("CH%d" % ((st + 2) % 3))
         ts(c32("T2"), c32(TOB), float(SIDE), A.mult)
         tt(c32(X), c32("T2"), was, A.add)
-        tt(c32(X, 1), c32(ES), c32(ES, 1), A.min)
+        tt(c32(X, 1), c32(ES), c32("P4"), A.add)
         if st:
             for k in range(2):
                 ts(c32("LV", k), was, 1.0, A.is_ge)
@@ -480,20 +503,18 @@ def rank_program(g, core, T, topo):
             dma("Y", ap(R("LT7", LIB * k, LIB * k + n)), ap(R("YT", H, H + n)), [R("YT", H, H + n)], [R("LT7", LIB * k, LIB * k + n)])
         D = a512("DA")
         SL = "SL%d" % t
-        phases(c32("P6"), "ZW1", D, True, True)
-        phases(c32("P6", 1), "ZW2", D, True, True)
         cp(c32("KEYU"), c32("ST"))
         act(a512("YC"), IND(R("ZAB", 0, SIDE + 2049), c32("KEYU")), F.Abs)
         ts(c32("KI"), c32("ST"), -1.0, A.add)
         ts(c32("QCI"), c32("KI"), 15, A.bitwise_and)
         ts(c32("QCI", 1), c32("KI"), 4, A.arith_shift_right)
         cp(c64("QCH"), c64("QCI"))
-        cp(c32("U1I"), c32("P6"))
-        tt(c32("PRI"), c32("U1I"), c32("P6", 1), A.mult)
-        ts(c32("UMI"), c32("U1I"), 127, A.bitwise_and)
+        u1, u2 = c32("UI"), c32("UI", 1)
+        tt(c32("PRI"), u1, u2, A.mult)
+        ts(c32("UMI"), u1, 127, A.bitwise_and)
         ts(c32("SHI"), c32("PRI"), 5, A.arith_shift_right, 1023, A.bitwise_and)
         ts(c32("STR"), c32("UMI"), 2.0, A.mult, 1.0, A.add)
-        tt(c32("CA"), c32("SHI"), c32("P6", 1), A.add)
+        tt(c32("CA"), c32("SHI"), u2, A.add)
         for k in range(2):
             act(c32("SR2", k), c32("STR"), scale=2.0)
         for k in range(4):
@@ -507,11 +528,12 @@ def rank_program(g, core, T, topo):
         LW = R("LT7", 0, 7 * LIB)
         df = lambda m, b="DF", n=1: R(b, 512 * m, 512 * (m + n))
         banks = {1: "P0", 2: "P1", 3: "P4"}
-        mm(a512("P5"), I, a512("YC"), True, False)
+        to_row("P5", 2, c32("L512"), True, False)
         to_row("P5", 0, c32("QCH"), False, False)
         to_row("P5", 1, c32("QCH", 1), False, False)
-        to_row("P5", 2, c32("L512"), False, True)
+        mm(a512("P5"), I, a512("YC"), False, True)
         act(a512("PAY"), a512("P5"))
+        cut = {}
         for m in range(8):
             if m in BY_S:
                 k = BY_S.index(m)
@@ -520,23 +542,24 @@ def rank_program(g, core, T, topo):
                 mm(a512(banks[m]), I, df(k, "GV"), False, True)
                 act(df(m), a512(banks[m]), F.Abs, scale=0.5)
             elif m in RELU:
-                tt(df(RELU.index(m), "DD"), IND(LW, c32("CU", m)), D, A.subtract)
-                ts(df(m), df(RELU.index(m), "DD"), 0.0, A.max)
+                got = tt(df(RELU.index(m), "DD"), IND(LW, c32("CU", m)), D, A.subtract)
+                if m - 2 in RELU:
+                    chain(cut[m - 2], got)
+                cut[m] = ts(df(m), df(RELU.index(m), "DD"), 0.0, A.max)
             else:
                 tt(df(m), IND(LW, c32("CU", m)), D, A.subtract)
                 act(df(m), df(m), F.Abs, scale=0.5)
-        for P, m, n in (("P2", 0, 4), ("P3", 4, 2), ("P7", 6, 2)):
+        for P, m, n in (("P2", 0, 2), ("P3", 4, 2), ("P6", 2, 2), ("P7", 6, 2)):
             mm(R(P, 0, 32 * n), I, R("MC", 32 * m, 32 * (m + n)), True, False)
             for k in range(0, n, 2):
                 if m + k in RELU:
                     phases(R(P, 32 * k, 32 * k + 64), "ZMN", df(RELU.index(m + k), "DD", 2), False, False)
                 phases(R(P, 32 * k, 32 * k + 64), "ZM2", df(m + k, "DF", 2), False, k == n - 2)
-        cp(a128("B1"), a128("P2"))
-        tt(c64("B3"), c64("B1"), R("B1", 64, 128), A.min)
-        tt(c64("B2"), c64("B3"), c64("P3"), A.min)
-        tt(c32("B4"), c32("B2"), c32("B2", 1), A.min)
-        tt(c32("B5"), c32("B4"), c32("P7"), A.min)
-        tt(c32("BEST"), c32("B5"), c32("P7", 1), A.min)
+        act(c64("B1"), c64("P3"))
+        tt(c64("B2"), c64("B1"), c64("P2"), A.min)
+        tt(c64("B3"), c64("B2"), c64("P6"), A.min)
+        tt(c64("B4"), c64("B3"), c64("P7"), A.min)
+        tt(c32("BEST"), c32("B4"), c32("B4", 1), A.min)
         tt(c32("HIT"), c32("BEST"), c32("ST", 1), A.is_lt)
         emit("V", lambda: g.vector.tensor_tensor_scan(ap(c32("INC")), ap(c32("ONE")), ap(c32("HIT")), 0.0, A.mult, A.add),
              [c32("ONE"), c32("HIT")], [c32("INC")], 64)
@@ -552,8 +575,8 @@ def rank_program(g, core, T, topo):
         tt(c32("HD"), c32("MTT"), c32("CA"), A.add)
         ts(c32("DNI"), c32("HD"), 1023, A.bitwise_and)
         cp(c32("DNH"), c32("DNI"))
-        to_row("P5", 0, c32("DNH"), True, True)
-        act(a512("DR"), a512("P5"), scale=1.0 / 256)
+        to_row("P4", 0, c32("DNH"), True, True)
+        act(a512("DR"), a512("P4"), scale=1.0 / 256)
         cp(IND(R(SL, 0, 1536), c32("SLOT")), a512("PAY"))
 
     def send(t):
@@ -561,7 +584,7 @@ def rank_program(g, core, T, topo):
         rid, pid, _ = topo.addr(dst)
         sl = a128("SL%d" % t)
         emit("G", lambda: g.remote_dma(T["LAND%d" % t][:, :], ap(sl), T.sem["arr%d" % t], T.sem["snt%d" % t], pid, rid, topo.mask(core, dst)),
-             [sl], [R("sent", t, t + 1)], 500.0, False, 3000.0)
+             [sl], [R("sent", t, t + 1)], 500.0, False, 2200.0)
 
     def grafts(t):
         at = lambda gr, w=128: (w * gr, w * gr + w)
@@ -570,15 +593,18 @@ def rank_program(g, core, T, topo):
             mms([(R("P%d" % h, *at(k)), a128("N256"), a128("TRI"), k == 0, False) for k in range(4)])
             mm(a128("P%d" % (2 + h)), I, a128("IQN"), True, False)
         ts(XH, a128("SL%d" % t), 1.0 / 256, A.mult, 1024.5 + 1.0 / 512, A.add)
-        mm(R("P6", 0, 8), XH, R("SEL1", 0, 8), True, True)
+        diff = lambda h: mms([(a512("P%d" % h), XH, R("NBC", *at(h, 512)), False, False)]
+                             + [(R("P%d" % h, *at(k)), R("BC", *at(4 * h + k)), XH, False, k == 3) for k in range(4)])
+        chain(mm(R("P6", 0, 8), XH, R("SEL1", 0, 8), True, True),
+              diff(0),
+              phases(R("P7", 0, 8), "ZR2", XH, True, True),
+              diff(1))
         ts(R("XF", 0, 8), R("P6", 0, 8), -1025.0 - MID, A.add)
-        phases(R("P7", 0, 8), "ZR2", XH, True, True)
         ts(R("LL", 0, 8), R("P7", 0, 8), -1025.0 - 512.0, A.add)
         act(a128("DG"), IND(a512("DR"), R("LL", 0, 8)), bias=col("CNM"))
         mm(a128("P4"), a128("DG"), a128("RQ"), True, True)
         for h in range(2):
             P, Q, WZ = "P%d" % h, "P%d" % (2 + h), "WZ%d" % h
-            mms([(a512(P), XH, R("NBC", *at(h, 512)), False, False)] + [(R(P, *at(k)), R("BC", *at(4 * h + k)), XH, False, k == 3) for k in range(4)])
             mm(a128(Q), XH, a128("RQ"), False, False)
             ts(R("EQ", *at(h, 512)), a512(P), 0.0, A.is_equal)
             mms([(R(Q, gr, 128, 8), R("EQ", *at(gr)), R("S16", 0, 16), False, gr % 4 == 3) for gr in range(4 * h, 4 * h + 4)])
@@ -588,8 +614,8 @@ def rank_program(g, core, T, topo):
                 ts(R("CHM", *at(gr, 256)), a256("IOC"), col("XF", gr), A.is_equal)
                 o = 896 - 127 * gr
                 mm(a256("P5"), R(WZ, o, o + 1017, 8), R("CHM", *at(gr, 256)), gr == 0, gr == 7)
-        ts(a256("ZU"), a256("P5"), 0.0, A.is_equal)
-        tt(a256("ZT"), a256("WF"), a256("ZU"), A.mult)
+        ts(a256("P6"), a256("P5"), 0.0, A.is_equal)
+        tt(a256("ZT"), a256("WF"), a256("P6"), A.mult)
         tt(a256("WF"), a256("ZT"), a256("P5"), A.add)
         ts(a256("UL"), a256("WF"), MID + H, A.add)
 

@@ -4,7 +4,6 @@ H = 16
 LIB = 1024
 MID = 1792.0
 SIDE = 2064
-SENT = -1048576.0
 
 SCRATCH, PLACE = {}, {}
 
@@ -23,25 +22,26 @@ def declare(dtype, text, packed=False):
 
 
 declare("bfloat16", "YT:3616 ZAB:4128 SG:2064 TG:512 WAB:1024 DA:512 DB:512 Y2:1024 ZB:512 MN:1024 UU:512 CB:512 SA:512 AB:1024 DF:4096 DD:2048 "
-        "GV:2048 RAW:2048 LT7:7168 YO:2048 YR:512 YC:512 EQ:1024 O256:512 BQ:2048 KQ:2064 BC0:1024 BC:1024 NBC:1024")
-declare("bfloat16", "LF:128 LT2:128 HIT:32 INC:32 ONE:128 IB:128 NI:128 N256:128 I2:128 IH:128 NH:128 BD:128 BD1:128 L00:128 L01:128 L10:128 L11:128 "
-        "UP:128 DN:128 SGB:128 LB:128 LT:128 TRI:128 MCI:256 MC:256 ZM:144 ZM2:144 ZMN:144 ZW1:144 ZW2:144 ZA0:144 ZAD:144 ZR2:144 SEL1:16 RQ:128 "
-        "S16:16 WW:256", True)
-declare("float16", "KLF:256 KLH:256 WF:256 NXF:256 KTG:512 CHM:2048 WZ0:1920 WZ1:1920 ZU:256 ZT:256")
-declare("float16", "QCH:64 DNH:32 XH:128 IQN:128 IOC:256 L512:32 HL:32 DG:128", True)
-declare("uint16", "UL:256 SEL:32 NL:32 KEYU:32 CU:256 SLOT:32 LL:8")
+        "GV:2048 RAW:2048 LT4:4096 YO:2048 YR:512 YC0:512 YC1:512 YIN0:640 YIN1:640 PAY:512 SL0:1536 SL1:1536 LLO:512 LHI:512 "
+        "EQ:1024 O256:512 BQ:2048 KQ:2064 BC:1024 NBC:1024")
+declare("bfloat16", "HIT:32 INC:32 ONE:128 IB:128 NI:128 N256:128 I2:128 I4:128 IH:128 NH:128 BD:128 BD1:128 L00:128 L01:128 L10:128 L11:128 "
+        "SGB:128 LB:128 LT:128 TRI:128 MC:256 ZM:144 ZM8:144 ZN8:144 ZM16:144 ZMN:144 ZW1:144 ZW2:144 ZA0:144 ZAD:144 ZR2:144 SEL1:16 RQ:128 "
+        "S16:16 IQN:128 E2:128 E3:128", True)
+declare("float16", "KLF:256 KLH:256 WF:256 NXF:256 KTG:512 CHM:2048 WZ:2944 WN:2944 ZT:256")
+declare("float16", "QCH:64 DNH:32 IOC:256 L512:32 HL:32 DG:128 H16:64", True)
+declare("uint16", "UL:256 SEL:32 NL:32 KEYU:32 CU:256 SLOT:32 LL0:8 LL1:8 LIN0:8 LIN1:8")
 declare("int32", "KLD:256 MLD:128 WTI:2")
-declare("float32", "KT:1552 PAY:512 DR:512 SL0:1536 SL1:1536 LAND0:128 LAND1:128 KOF:256 KOT:256 WTF:2")
-declare("float32", "TOB0:32 TOB1:32 TOB2:32 T2:32 UA:64 UD:64 UM:64 DK:32 ES0:32 ES1:32 ES2:32 Q0:32 Q1:32 Q2:32 QD:32 S1:32 S2:32 LQ:32 CH0:32 CH1:32 CH2:32 ST:64 NS:64 "
-        "DS:64 DT:64 LV:64 B1:64 B2:64 B3:64 B4:64 BEST:32 XF:16 STR:32 SR2:64 SR4:128 LANE:32 NL512:32 XC:8 NX:8 IQF:128 IOF:256 C255:8 CNX:8 "
-        "CMID:8 CNM:8", True)
-declare("int32", "LI:128 LY:128 UI:64 PRI:32 SHI:32 UMI:32 CA:256 B8:32 MI:32 MTT:32 HD:32 DNI:32 KI:32 QCI:64 XI1:32 LI0:32 LI1:32 LI2:32", True)
+declare("float32", "KT:1552 DR:640 KOF:256 KOT:256 WTF:2")
+declare("float32", "TOB0:32 TOB1:32 TOB2:32 T2:32 UA:128 UD:64 UM:64 DK:32 ES0:32 ES1:32 ES2:32 Q0:32 Q1:32 Q2:32 Q3:32 QD:32 QL:8 QE:8 QI:8 S1:32 S2:32 LQ:32 CH0:32 CH1:32 CH2:32 ST:64 NS:64 "
+        "DS:64 DT:64 LV:64 B1:64 B2:64 B3:64 B4:64 XF:16 LANE:32 NL512:32 IOF:256 C255:8 CNX:8 "
+        "CMID:8", True)
+declare("int32", "UI:128 U2M:64 PRI:64 SHI:64 UMI:64 BEST:32 MI:32 MTT:32 HD:32 DNI:32 KI:32 QCI:64 LI0:32 LI1:32 LI2:32", True)
 for _k in range(8):
     SCRATCH["P%d" % _k] = ("psum", [128, 512], "float32")
 
-SEMAPHORES = ["cV", "cS", "cP", "cG", "arr0", "arr1", "snt0", "snt1"] + ["d%d" % k for k in range(25)]
+SEMAPHORES = ["cV", "cS", "cP", "cG", "arr0", "arr1", "arr2", "arr3", "snt0", "snt1", "snt2", "snt3"] + ["d%d" % k for k in range(27)]
 
-GATHER, SCATTER, PE, WAKE, WAKE_SAME = 1.35, 3.0, 0.42, 230.0, 250.0
+GATHER, SCATTER, PE, WAKE, WAKE_SAME = 1.4, 3.0, 0.4, 250.0, 270.0
 PASSES, SWEEPS, SHORT, LEAD = 4, 3, 72, 1000.0
 ORDER = []
 
@@ -166,6 +166,7 @@ def rank_program(g, core, T, topo):
     calls = []
     acc = {}
     dmas = [0]
+    mark = {}
 
     def ap(r):
         if r[0] == "ind":
@@ -257,9 +258,8 @@ def rank_program(g, core, T, topo):
 
     def cp(out, a):
         if out[0] == "ind":
-            emit("V", lambda: g.vector.tensor_copy(ap(out), ap(a)), rd(a) + [out[2]], [out[1]], vcost(out, a))
-        else:
-            emit("V", lambda: g.vector.tensor_copy(ap(out), ap(a)), rd(a), [out], vcost(out, a))
+            return emit("V", lambda: g.vector.tensor_copy(ap(out), ap(a)), rd(a) + [out[2]], [out[1]], vcost(out, a))
+        return emit("V", lambda: g.vector.tensor_copy(ap(out), ap(a)), rd(a), [out], vcost(out, a))
 
     def ms(out, v):
         emit("V", lambda: g.vector.memset(ap(out), v), [], [out], vcost(out))
@@ -268,8 +268,8 @@ def rank_program(g, core, T, topo):
         emit("V", lambda: g.vector.transpose(ap(out), ap(a)), [a], [out], vcost(out, a))
 
     def act(out, a, func=F.Identity, scale=1.0, bias=0.0, also=()):
-        emit("S", lambda: g.scalar.activation(ap(out), ap(a), func, bias=num(bias), scale=num(scale)), rd(a, scale, bias, *also), [out],
-             65 + width(out) * (GATHER if a[0] == "ind" else 1.0))
+        return emit("S", lambda: g.scalar.activation(ap(out), ap(a), func, bias=num(bias), scale=num(scale)), rd(a, scale, bias, *also), [out],
+                    65 + width(out) * (GATHER if a[0] == "ind" else 1.0))
 
     def mms(items):
         return emit("P", [lambda x=x: g.tensor.matmul(ap(x[0]), ap(x[1]), ap(x[2]), x[3], x[4]) for x in items], [r for x in items for r in x[1:3]],
@@ -287,11 +287,14 @@ def rank_program(g, core, T, topo):
     def asel(out, in_, pat, op, base, chm):
         emit("G", lambda: g.affine_select(ap(out), ap(in_), pat, op, 0.0, base, chm), [in_], [out], 170 + 2 * width(out))
 
-    def phases(out, Z, src, first, last):
-        return mms([(out, R(Z, 15 - q, 143 - q), R(src[0], src[1] + q, src[2], 16), first and q == 0, last and q == 15) for q in range(16)])
+    def phases(out, Z, src, first, last, by=16):
+        for j in range(0, 16, by):
+            k = mms([(out, R(Z, 15 - q, 143 - q), R(src[0], src[1] + q, src[2], 16), first and q == 0, last and q == 15) for q in range(j, j + by)])
+        return k
 
     def to_row(P, r, src, first, last):
-        mms([(R(P, q, 512, 16), R("KQ", 16 + 128 * q - r, 144 + 128 * q - r), src, first and q == 0, last and q == 15) for q in range(16)])
+        for j in range(0, 16, 4):
+            mms([(R(P, q, 512, 16), R("KQ", 16 + 128 * q - r, 144 + 128 * q - r), src, first and q == 0, last and q == 15) for q in range(j, j + 4)])
 
     a128 = lambda b: R(b, 0, 128)
     a256 = lambda b: R(b, 0, 256)
@@ -306,21 +309,24 @@ def rank_program(g, core, T, topo):
     dma("Y", ap(a128("MLD")), T.mx[:, :], [], [a128("MLD")])
     dma("Y", ap(R("YT", H, H + 1536)), T.lv[:, :], [], [R("YT", H, H + 1536)])
     dma("Y", ap(a512("TG")), T.tg[:, :], [], [a512("TG")])
+    for t in range(2):
+        dma("Y", ap(R("YIN%d" % t, 512, 640)), T.lv[:, 128 * t:128 * t + 128], [], [R("YIN%d" % t, 512, 640)])
     dma("Y", ap(R("WTI", 0, 2)), T.wt[:, :], [], [R("WTI", 0, 2)])
 
     O256 = a512("O256")
     ms(a128("ONE"), 1.0)
     ms(O256, 256.0)
     for r in (R("YT", 0, H), R("KQ", 0, 16), R("ZM", 0, 144), R("ZAB", 0, 1), R("ZAB", 2049, SIDE + 1), R("SG", 0, 1),
-              R("KT", 0, 513)):
+              R("DR", 512, 640), R("KT", 0, 513)):
         ms(r, 0.0)
-    for b, v in (("C255", 255.0), ("CNX", MID - 1535.0), ("CMID", MID), ("CNM", -MID)):
+    for b, v in (("C255", 255.0), ("CNX", MID - 1535.0), ("CMID", MID)):
         ms(R(b, 0, 8), v)
     ms(R("S16", 0, 16), 16.0)
     asel(I, a128("ONE"), [[-1, 128]], A.is_equal, 0, 1)
     iota(c32("LI1"), [[0, 32]], 0, 1, False)
-    asel(a128("UP"), a128("ONE"), [[1, 128]], A.is_equal, -16, -1)
-    asel(a128("DN"), a128("ONE"), [[1, 128]], A.is_equal, 16, -1)
+    for u in range(2):
+        for v in range(2):
+            asel(a128("L%d%d" % (u, v)), a128("ONE"), [[-32, 4], [1000, 2], [-1, 16]], A.is_equal, -16 * u - 1000 * v, 1)
     for j in range(4):
         asel(R("BQ", 512 * j, 512 * j + 512), O256, [[-1, 4], [-16, 8], [0, 16]], A.is_equal, -4 * j, 1)
         asel(R("KQ", 16 + 512 * j, 528 + 512 * j), O256, [[-1, 4], [-16, 8], [1000, 16]], A.is_equal, -4 * j, 1)
@@ -328,50 +334,55 @@ def rank_program(g, core, T, topo):
     asel(a128("BD"), a128("BD1"), [[16, 8], [0, 16]], A.is_ge, 15, -1)
     iota(c32("LI0"), [[16, 32]], 0, 0, False)
     asel(a128("LT"), a128("BD"), [[1, 128]], A.is_gt, 0, -1)
-    iota(a256("MCI"), [[1, 8], [0, 32]], 0, 0)
-    iota(a128("IQF"), [[-1, 16], [0, 8]], -1025, 0)
+    iota(a256("MC"), [[1, 8], [0, 32]], 0, 0)
+    iota(a128("IQN"), [[-1, 16], [0, 8]], 0, 0)
+    iota(a512("LLO"), [[0, 4], [1, 128]], 0, 0)
+    iota(a512("LHI"), [[1, 4], [0, 128]], 0, 0)
     iota(a256("IOF"), [[SIDE // 16, 2], [1, 128]], -int(MID), 0)
     asel(a128("TRI"), a128("O256"), [[-1, 128]], A.is_ge, 0, 1)
     asel(R("SEL1", 0, 8), R("ONE", 0, 8), [[-16, 8]], A.is_equal, -1, 1)
     asel(a128("RQ"), a128("ONE"), [[0, 16], [-16, 8]], A.is_equal, 0, 1)
-    iota(R("BC0", 0, 1024), [[-240, 8], [0, 128]], 1, 15)
-    asel(R("BC", 0, 1024), R("BC0", 0, 1024), [[-16, 8], [0, 128]], A.is_ge, 0, 1)
-    asel(R("BC", 0, 1024), R("BC", 0, 1024), [[16, 8], [0, 128]], A.is_ge, 1, -1)
-    act(R("NBC", 0, 1024), R("BC", 0, 1024), scale=-1.0)
-    for lo, hi in ((0, 448), (448, 896), (1024, 1472), (1472, 1920)):
-        for b in ("WZ0", "WZ1"):
-            act(R(b, lo, hi), R("O256", 0, hi - lo), scale=0.0)
-    ts(c32("XI1"), c32("LI1"), 4, A.arith_shift_right, 1, A.bitwise_and)
-    cp(R("XC", 0, 8), R("XI1", 0, 8))
-    ts(R("NX", 0, 8), R("XC", 0, 8), -1.0, A.mult, 1.0, A.add)
-    for u, v, b in ((0, 0, "IB"), (1, 1, "IB"), (0, 1, "UP"), (1, 0, "DN")):
-        ts(a128("L%d%d" % (u, v)), a128(b), col("XC" if u else "NX"), A.mult)
-    for b, w in (("NI", -1.0), ("N256", -256.0), ("I2", 2.0), ("IH", 0.5), ("NH", -0.5)):
+    for b, x in (("BC", 1), ("NBC", -1)):
+        iota(R(b, 0, 1024), [[-240 * x, 8], [0, 128]], x, 15 * x)
+        asel(R(b, 0, 1024), R(b, 0, 1024), [[-16, 8], [0, 128]], A.is_ge, 0, 1)
+        asel(R(b, 0, 1024), R(b, 0, 1024), [[16, 8], [0, 128]], A.is_ge, 1, -1)
+    for lo in (0, 448):
+        act(R("WZ", lo, lo + 448), R("O256", 0, 448), scale=0.0)
+    for b, lo in (("WZ", 1024), ("WZ", 2048), ("WN", 0), ("WN", 1024), ("WN", 2048)):
+        dma("Y", ap(R(b, lo, lo + 896)), ap(R("WZ", 0, 896)), [R("WZ", 0, 896)], [R(b, lo, lo + 896)])
+    for b, w in (("NI", -1.0), ("N256", -256.0), ("I2", 2.0), ("I4", 4.0), ("IH", 0.5), ("NH", -0.5)):
         ts(a128(b), I, w, A.mult)
     ts(c32("LI2"), c32("LI1"), 15, A.bitwise_and)
-    for k in range(3):
+    for k in range(4):
         ts(c32("Q%d" % k), c32("LI2"), float(k), A.is_equal)
     tt(c32("QD"), c32("Q1"), c32("Q0"), A.subtract)
+    for k in (2, 3):
+        ts(a128("E%d" % k), I, col("Q%d" % k), A.mult, 256.0, A.mult)
+    ts(col("QL"), col("Q3"), 128.0, A.mult, col("Q2"), A.add)
+    ts(col("QE"), col("LI2"), 2.0, A.is_lt, -4096.0, A.mult)
+    ts(col("QI"), col("Q3"), 4.0, A.mult, col("QE"), A.add)
     cp(R("WTF", 0, 2), R("WTI", 0, 2))
     cp(R("ZM", 15, 128, 16), R("BD", 0, 128, 16))
-    for Z, w in (("ZA0", col("Q0")), ("ZAD", col("QD")), ("ZR2", col("Q2")), ("ZMN", -1.0), ("ZM2", 2.0), ("ZW1", col("WTF", 0)), ("ZW2", col("WTF", 1))):
+    for Z, w in (("ZA0", col("Q0")), ("ZAD", col("QD")), ("ZR2", col("QL")), ("ZMN", -1.0), ("ZM8", 8.0), ("ZN8", -8.0), ("ZM16", 16.0),
+                 ("ZW1", col("WTF", 0)), ("ZW2", col("WTF", 1))):
         ts(R(Z, 0, 144), R("ZM", 0, 144), w, A.mult)
     tt(c32("LANE"), c32("LI2"), c32("LI0"), A.add)
     ts(c32("CH2"), c32("LANE"), 1537.0, A.add)
     ts(c32("L512"), c32("LANE"), 512.0, A.add)
     ts(c32("NL512"), c32("LANE"), -1.0, A.mult, -512.0, A.add)
     ts(c32("LQ"), c32("LANE"), 1.0 / 512, A.mult)
-    ts(a256("MC"), a256("MCI"), 0.125, A.mult)
     tt(a128("LB"), a128("LT"), a128("BD"), A.subtract)
-    cp(a128("IQN"), a128("IQF"))
     cp(a256("IOC"), a256("IOF"))
 
     def load_lists():
-        ts(a256("KLF"), a256("KLD"), -MID, A.add)
-        vtr(a256("KLH"), a256("KLF"))
-        mms([(R("P7", 2 * k + c2, 256, 16), a128("L%d%d" % (c2, x)), R("KLH", 32 * k + 16 * x, 32 * k + 16 * x + 16), x == 0, x == 1)
-             for k in range(8) for c2 in range(2) for x in range(2)])
-        ts(a256("UL"), a256("P7"), MID + H, A.add)
+        for j in range(2):
+            c = (128 * j, 128 * j + 128)
+            ts(R("KLF", *c), R("KLD", *c), -MID, A.add)
+            vtr(R("KLH", *c), R("KLF", *c))
+            mms([(R("P7", 2 * k + c2, 256, 16), a128("L%d%d" % (c2, x)), R("KLH", 32 * k + 16 * x, 32 * k + 16 * x + 16), x == 0, x == 1)
+                 for k in range(4 * j, 4 * j + 4) for c2 in range(2) for x in range(2)])
+        for c in ((0, 160), (160, 256)):
+            ts(R("UL", *c), R("P7", *c), MID + H, A.add)
         act(a256("WF"), a256("P7"))
         ts(a128("SGB"), a128("MLD"), 2.0, A.mult, -1.0, A.add)
         for l in range(4):
@@ -397,9 +408,13 @@ def rank_program(g, core, T, topo):
         za, yb, mn = tab("ZAB", 0, l), tab("ZAB", SIDE, l), R("MN", 512 * (l % 2), 0)
         if tables and l:
             za, yb = R("RAW", 1024 * (l % 2), 1024 * (l % 2) + 512), R("RAW", 1024 * (l % 2) + 512, 1024 * (l % 2) + 1024)
-        for h, c in enumerate(((0, 288), (288, 512)) if out else HALF):
+        for h, c in enumerate(HALF if out else HALF):
             tt(sub(za, *c), IND(below(l), ul(0, l, *c)), sub(tab("SG", 0, l), *c), A.mult)
-            act(sub(yb, *c), IND(below(l), ul(1, l, *c)))
+            if tables and l == 3:
+                act(sub(yb, *c), IND(below(l), ul(1, l, *c)), F.Relu, scale=-1.0, bias=col("C255"))
+                act(sub(tab("ZAB", SIDE, l), *c), sub(yb, *c), scale=-1.0, bias=col("C255"))
+            else:
+                act(sub(yb, *c), IND(below(l), ul(1, l, *c)))
             ts(sub(mn, *c), sub(za, *c), 0.0, A.min, -255.0, A.max)
             if out:
                 P = R("P%d" % (2 * (l % 2) + h), 0, c[1] - c[0])
@@ -411,7 +426,8 @@ def rank_program(g, core, T, topo):
         if tables and l:
             for c in HALF if l == 3 else ((0, 512),):
                 ts(sub(tab("ZAB", 0, l), *c), sub(za, *c), 255.0, A.min, -255.0, A.max)
-                ts(sub(tab("ZAB", SIDE, l), *c), sub(yb, *c), 255.0, A.min)
+                if l < 3:
+                    ts(sub(tab("ZAB", SIDE, l), *c), sub(yb, *c), 255.0, A.min)
 
     def levels():
         lists()
@@ -422,8 +438,9 @@ def rank_program(g, core, T, topo):
         TOB, ES, zb = "TOB%d" % st, "ES%d" % st, a512("ZB")
         if st == 0:
             D, mn, za, yb = a512("TG"), R("MN", 512, 1024), tab("ZAB", 0, 3), tab("ZAB", SIDE, 3)
+            mm(a512("P6"), I, tab("SG", 0, 3), True, True)
             for c in HALF:
-                tt(sub(zb, *c), sub(yb, *c), sub(tab("SG", 0, 3), *c), A.mult)
+                tt(sub(zb, *c), sub(yb, *c), R("P6", *c), A.mult)
         else:
             D, mn, za, yb = a512("DA" if st == 1 else "DB"), a512("MN"), a512("Y2"), R("Y2", 512, 1024)
             for c in HALF:
@@ -461,83 +478,93 @@ def rank_program(g, core, T, topo):
             tt(dk, R("NXF", 224, 256), na, A.subtract)
         elif st == 1:
             na, dk = c32("P7"), c32("P7", 1)
-            phases(na, "ZA0", a512("KTG"), True, True)
-            phases(dk, "ZAD", a512("KTG"), True, True)
+            phases(na, "ZA0", a512("KTG"), True, True, 4)
+            phases(dk, "ZAD", a512("KTG"), True, True, 4)
         phases(c32("P6"), "ZMN", R("AB", 512, 1024), True, False)
         phases(c32("P6"), "ZM", a512("AB"), False, True)
-        phases(c32("P4"), "ZM", R("AB", 512, 1024), True, True)
+        phases(c32("P4"), "ZM8", R("AB", 512, 1024), True, True)
         ts(c32(TOB), c32("P6"), 0.0, A.is_gt)
-        ts(c32(ES), c32("P6"), 0.0, A.min)
+        ts(c32(ES), c32("P6"), 0.0, A.min, 8.0, A.mult)
         if st == 2:
             for k in range(2):
-                P = ("P5", "P7")[k]
-                phases(c64(P), "ZW%d" % (k + 1), R("WAB", 0, 1024), True, True)
-                act(c32("UA", k), c32(P))
-                tt(c32("UD", k), c32(P, 1), c32("UA", k), A.subtract)
+                phases(c64(("P5", "P7")[k]), "ZW%d" % (k + 1), R("WAB", 0, 1024), True, True)
+                cp(R("UI", 64 * k, 64 * k + 64), c64(("P5", "P7")[k]))
+            tt(c64("PRI"), c64("UI"), c64("P7"), A.mult)
+            ts(c64("UMI"), c64("UI"), 127, A.bitwise_and)
+            ts(c64("SHI"), c64("PRI"), 5, A.arith_shift_right, 1023, A.bitwise_and)
+            ts(c64("U2M"), R("UI", 64, 128), 1023, A.bitwise_and)
+            tt(c64("UA"), c64("SHI"), c64("U2M"), A.add)
+            ts(R("UA", 64, 128), c64("UMI"), 2.0, A.mult, 1.0, A.add)
+            for k in range(2):
+                tt(c32("UD", k), c32("UA", 2 * k + 1), c32("UA", 2 * k), A.subtract)
                 tt(c32("UM", k), c32("UD", k), c32(TOB), A.mult)
-                tt(c32("UI", k), c32("UM", k), c32("UA", k), A.add)
+                tt(c32("H16", k), c32("UM", k), c32("UA", 2 * k), A.add)
         if st < 2:
             tt(c32("S2"), c32(TOB), dk, A.mult)
             tt(c32("CH%d" % st), c32("S2"), na, A.add)
             cp(c32("NL"), c32("CH%d" % st))
         tt(c32("S1"), c32(TOB), c32("LQ"), A.add)
         ts(c32("SEL"), c32("S1"), 512.0, A.mult)
-        for h, c in enumerate(HALF):
-            (cp if h and st == 2 else act)(R("DB" if st == 1 else "DA", *c), IND(R("WAB", 0, 1024), R("SEL", c[0] // 16, c[1] // 16)))
-        X, was = "ST" if st == 0 else "NS", c32("CH%d" % ((st + 2) % 3))
-        ts(c32("T2"), c32(TOB), float(SIDE), A.mult)
-        tt(c32(X), c32("T2"), was, A.add)
-        tt(c32(X, 1), c32(ES), c32("P4"), A.add)
-        if st:
+        for c in HALF:
+            act(R("DB" if st == 1 else "DA", *c), IND(R("WAB", 0, 1024), R("SEL", c[0] // 16, c[1] // 16)))
+        was = c32("CH%d" % ((st + 2) % 3))
+        ts(c32("T2"), c32("P6"), 0.0, A.is_gt, float(SIDE), A.mult)
+        if st == 0:
+            tt(c32("ST"), c32("T2"), was, A.add)
+            tt(c32("ST", 1), c32(ES), c32("P4"), A.add)
+        else:
+            ts(c32("LV"), was, 1.0, A.is_ge)
+            ts(c32("LV", 1), was, 1.0, A.is_lt)
             for k in range(2):
-                ts(c32("LV", k), was, 1.0, A.is_ge)
-            tt(c64("DS"), c64("NS"), c64("ST"), A.subtract)
-            tt(c64("DT"), c64("DS"), c64("LV"), A.mult)
-            tt(c64("ST"), c64("DT"), c64("ST"), A.add)
+                tt(c32("DS", k), c32("ST", k), c32("LV", 1), A.mult)
+            tt(c32("DT"), c32("DS"), was, A.add)
+            tt(c32("ST"), c32("T2"), c32("DT"), A.add)
+            tt(c32("NS"), c32(ES), c32("P4"), A.add)
+            tt(c32("NS", 1), c32("NS"), c32("LV"), A.mult)
+            tt(c32("ST", 1), c32("NS", 1), c32("DS", 1), A.add)
 
     BY_S, RELU = (1, 2, 3), (4, 5, 6, 7)
 
+    def send(k, to, what, late):
+        dst = T.cores[(rank + 1) % n_ranks]
+        rid, pid, _ = topo.addr(dst)
+        emit("G", lambda: g.remote_dma(ap(to), ap(what), T.sem["arr%d" % k], T.sem["snt%d" % k], pid, rid, topo.mask(core, dst)),
+             [what], [R("sent", k, k + 1)], 500.0, False, late)
+
     def donors(t):
         n = LIB if t == 0 else 128
-        for k in range(7):
-            dma("Y", ap(R("LT7", LIB * k, LIB * k + n)), ap(R("YT", H, H + n)), [R("YT", H, H + n)], [R("LT7", LIB * k, LIB * k + n)])
+        for k in range(4):
+            dma("Y", ap(R("LT4", LIB * k, LIB * k + n)), ap(R("YT", H, H + n)), [R("YT", H, H + n)], [R("LT4", LIB * k, LIB * k + n)])
         D = a512("DA")
         SL = "SL%d" % t
         cp(c32("KEYU"), c32("ST"))
-        act(a512("YC"), IND(R("ZAB", 0, SIDE + 2049), c32("KEYU")), F.Abs)
+        yc = act(a512("YC%d" % t), IND(R("ZAB", 0, SIDE + 2049), c32("KEYU")), F.Abs)
+        send(2 * t, a512("YIN%d" % t), a512("YC%d" % t), 8000.0)
         ts(c32("KI"), c32("ST"), -1.0, A.add)
         ts(c32("QCI"), c32("KI"), 15, A.bitwise_and)
         ts(c32("QCI", 1), c32("KI"), 4, A.arith_shift_right)
         cp(c64("QCH"), c64("QCI"))
-        u1, u2 = c32("UI"), c32("UI", 1)
-        tt(c32("PRI"), u1, u2, A.mult)
-        ts(c32("UMI"), u1, 127, A.bitwise_and)
-        ts(c32("SHI"), c32("PRI"), 5, A.arith_shift_right, 1023, A.bitwise_and)
-        ts(c32("STR"), c32("UMI"), 2.0, A.mult, 1.0, A.add)
-        tt(c32("CA"), c32("SHI"), u2, A.add)
-        for k in range(2):
-            act(c32("SR2", k), c32("STR"), scale=2.0)
-        for k in range(4):
-            act(c32("SR4", k), c32("STR"), scale=4.0)
-        tt(c32("CA", 1), c32("CA"), c32("STR"), A.add)
-        tt(R("CA", 64, 128), c64("CA"), c64("SR2"), A.add)
-        tt(R("CA", 128, 256), a128("CA"), a128("SR4"), A.add)
-        for c in ((0, 64), (64, 128), (128, 256)):
-            cp(R("CU", *c), R("CA", *c))
-        ms(a128(SL), SENT)
-        LW = R("LT7", 0, 7 * LIB)
+        hh, stride = c32("H16"), c32("H16", 1)
+        for P, some in (("P4", (0, 1)), ("P1", (2, 3, 4, 5, 6, 7))):
+            steps = [(m, W) for j, W in enumerate(("IB", "I2", "I4")) for m in some if m >> j & 1]
+            mms([(c32(P, m - some[0]), a128(W), stride, k == 0, False) for k, (m, W) in enumerate(steps)])
+            mms([(c32(P, m - some[0]), I, hh, False, m == some[-1]) for m in some])
+            cp(R("CU", 32 * some[0], 32 * some[-1] + 32), R(P, 0, 32 * len(some)))
+        ts(a128(SL), a128("LLO"), col("Q2"), A.mult, col("QI"), A.add)
+        LW = R("LT4", 0, 4 * LIB)
         df = lambda m, b="DF", n=1: R(b, 512 * m, 512 * (m + n))
         banks = {1: "P0", 2: "P1", 3: "P4"}
-        to_row("P5", 2, c32("L512"), True, False)
+        mms([(a512("P5"), a128("E2"), a512("LLO"), True, False), (a512("P5"), a128("E3"), a512("LHI"), False, False)])
         to_row("P5", 0, c32("QCH"), False, False)
-        to_row("P5", 1, c32("QCH", 1), False, False)
-        mm(a512("P5"), I, a512("YC"), False, True)
-        act(a512("PAY"), a512("P5"))
+        to_row("P5", 1, c32("QCH", 1), False, True)
+        act(a512("PAY"), a512("P5"), scale=1.0 / 256)
         cut = {}
         for m in range(8):
             if m in BY_S:
                 k = BY_S.index(m)
-                act(df(k, "GV"), IND(LW, c32("CU", m)))
+                got = act(df(k, "GV"), IND(LW, c32("CU", m)))
+                if k == 1:
+                    chain(yc, got)
                 mm(a512(banks[m]), NI, D, True, False)
                 mm(a512(banks[m]), I, df(k, "GV"), False, True)
                 act(df(m), a512(banks[m]), F.Abs, scale=0.5)
@@ -549,16 +576,16 @@ def rank_program(g, core, T, topo):
             else:
                 tt(df(m), IND(LW, c32("CU", m)), D, A.subtract)
                 act(df(m), df(m), F.Abs, scale=0.5)
-        for P, m, n in (("P2", 0, 2), ("P3", 4, 2), ("P6", 2, 2), ("P7", 6, 2)):
+        for P, m, n in (("P2", 0, 2), ("P3", 4, 2), ("P7", 6, 2), ("P6", 2, 2)):
             mm(R(P, 0, 32 * n), I, R("MC", 32 * m, 32 * (m + n)), True, False)
             for k in range(0, n, 2):
                 if m + k in RELU:
-                    phases(R(P, 32 * k, 32 * k + 64), "ZMN", df(RELU.index(m + k), "DD", 2), False, False)
-                phases(R(P, 32 * k, 32 * k + 64), "ZM2", df(m + k, "DF", 2), False, k == n - 2)
+                    phases(R(P, 32 * k, 32 * k + 64), "ZN8", df(RELU.index(m + k), "DD", 2), False, False)
+                mark["sums"] = phases(R(P, 32 * k, 32 * k + 64), "ZM16", df(m + k, "DF", 2), False, k == n - 2)
         act(c64("B1"), c64("P3"))
         tt(c64("B2"), c64("B1"), c64("P2"), A.min)
-        tt(c64("B3"), c64("B2"), c64("P6"), A.min)
-        tt(c64("B4"), c64("B3"), c64("P7"), A.min)
+        tt(c64("B3"), c64("B2"), c64("P7"), A.min)
+        tt(c64("B4"), c64("B3"), c64("P6"), A.min)
         tt(c32("BEST"), c32("B4"), c32("B4", 1), A.min)
         tt(c32("HIT"), c32("BEST"), c32("ST", 1), A.is_lt)
         emit("V", lambda: g.vector.tensor_tensor_scan(ap(c32("INC")), ap(c32("ONE")), ap(c32("HIT")), 0.0, A.mult, A.add),
@@ -569,68 +596,56 @@ def rank_program(g, core, T, topo):
         mm(c32("P6"), a128("BD"), c32("INC"), False, False)
         mm(c32("P6"), I, c32("HL"), False, True)
         cp(c32("SLOT"), c32("P6"))
-        ts(c32("B8"), c32("BEST"), 8.0, A.mult)
-        ts(c32("MI"), c32("B8"), 7, A.bitwise_and)
-        tt(c32("MTT"), c32("MI"), c32("STR"), A.mult)
-        tt(c32("HD"), c32("MTT"), c32("CA"), A.add)
+        ts(c32("MI"), c32("BEST"), 7, A.bitwise_and)
+        tt(c32("MTT"), c32("MI"), stride, A.mult)
+        tt(c32("HD"), c32("MTT"), hh, A.add)
         ts(c32("DNI"), c32("HD"), 1023, A.bitwise_and)
-        cp(c32("DNH"), c32("DNI"))
+        dn = cp(c32("DNH"), c32("DNI"))
         to_row("P4", 0, c32("DNH"), True, True)
         act(a512("DR"), a512("P4"), scale=1.0 / 256)
-        cp(IND(R(SL, 0, 1536), c32("SLOT")), a512("PAY"))
-
-    def send(t):
-        dst = T.cores[(rank + 1) % n_ranks]
-        rid, pid, _ = topo.addr(dst)
-        sl = a128("SL%d" % t)
-        emit("G", lambda: g.remote_dma(T["LAND%d" % t][:, :], ap(sl), T.sem["arr%d" % t], T.sem["snt%d" % t], pid, rid, topo.mask(core, dst)),
-             [sl], [R("sent", t, t + 1)], 500.0, False, 2200.0)
+        chain(dn, cp(IND(R(SL, 0, 1536), c32("SLOT")), a512("PAY")))
 
     def grafts(t):
         at = lambda gr, w=128: (w * gr, w * gr + w)
-        XH = a128("XH")
+        XH, LL = a128("SL%d" % t), R("LL%d" % t, 0, 8)
         for h in range(2):
-            mms([(R("P%d" % h, *at(k)), a128("N256"), a128("TRI"), k == 0, False) for k in range(4)])
+            chain(mark["sums"], mms([(R("P%d" % h, *at(k)), a128("N256"), a128("TRI"), k == 0, False) for k in range(4)]))
             mm(a128("P%d" % (2 + h)), I, a128("IQN"), True, False)
-        ts(XH, a128("SL%d" % t), 1.0 / 256, A.mult, 1024.5 + 1.0 / 512, A.add)
         diff = lambda h: mms([(a512("P%d" % h), XH, R("NBC", *at(h, 512)), False, False)]
                              + [(R("P%d" % h, *at(k)), R("BC", *at(4 * h + k)), XH, False, k == 3) for k in range(4)])
         chain(mm(R("P6", 0, 8), XH, R("SEL1", 0, 8), True, True),
-              diff(0),
               phases(R("P7", 0, 8), "ZR2", XH, True, True),
+              diff(0),
               diff(1))
-        ts(R("XF", 0, 8), R("P6", 0, 8), -1025.0 - MID, A.add)
-        ts(R("LL", 0, 8), R("P7", 0, 8), -1025.0 - 512.0, A.add)
-        act(a128("DG"), IND(a512("DR"), R("LL", 0, 8)), bias=col("CNM"))
+        ts(R("XF", 0, 8), R("P6", 0, 8), -MID, A.add)
+        ll = cp(LL, R("P7", 0, 8))
+        send(2 * t + 1, R("LIN%d" % t, 0, 8), LL, 2500.0)
+        act(a128("DG"), IND(R("DR", 0, 640), LL), scale=-1.0, bias=col("CMID"))
         mm(a128("P4"), a128("DG"), a128("RQ"), True, True)
+        mms([(R("P6", *at(k)), I, a128("ONE"), k == 0, False) for k in range(2)])
         for h in range(2):
-            P, Q, WZ = "P%d" % h, "P%d" % (2 + h), "WZ%d" % h
+            P, Q, z = "P%d" % h, "P%d" % (2 + h), 896 + 1024 * h
             mm(a128(Q), XH, a128("RQ"), False, False)
-            ts(R("EQ", *at(h, 512)), a512(P), 0.0, A.is_equal)
+            chain(ll, ts(R("EQ", *at(h, 512)), a512(P), 0.0, A.is_equal))
             mms([(R(Q, gr, 128, 8), R("EQ", *at(gr)), R("S16", 0, 16), False, gr % 4 == 3) for gr in range(4 * h, 4 * h + 4)])
-            ts(R("WW", *at(h)), a128(Q), 0.0, A.is_equal)
-            tt(R(WZ, 896, 1024), R("WW", *at(h)), a128("P4"), A.mult)
+            ts(R("WN", z, z + 128), a128(Q), 0.0, A.is_equal, -1.0, A.mult)
+            tt(R("WZ", z, z + 128), R("WN", z, z + 128), a128("P4"), A.mult)
             for gr in range(4 * h, 4 * h + 4):
                 ts(R("CHM", *at(gr, 256)), a256("IOC"), col("XF", gr), A.is_equal)
-                o = 896 - 127 * gr
-                mm(a256("P5"), R(WZ, o, o + 1017, 8), R("CHM", *at(gr, 256)), gr == 0, gr == 7)
-        ts(a256("P6"), a256("P5"), 0.0, A.is_equal)
-        tt(a256("ZT"), a256("WF"), a256("P6"), A.mult)
-        tt(a256("WF"), a256("ZT"), a256("P5"), A.add)
-        ts(a256("UL"), a256("WF"), MID + H, A.add)
+                o = z - 127 * gr
+                mm(a256("P6"), R("WN", o, o + 1017, 8), R("CHM", *at(gr, 256)), False, gr == 7)
+                mm(a256("P5"), R("WZ", o, o + 1017, 8), R("CHM", *at(gr, 256)), gr == 0, gr == 7)
+        for c in ((0, 160), (160, 256)):
+            tt(R("ZT", *c), R("WF", *c), R("P6", *c), A.mult)
+            tt(R("WF", *c), R("ZT", *c), R("P5", *c), A.add)
+            ts(R("UL", *c), R("WF", *c), MID + H, A.add)
 
     def receive(t):
-        lib = R("YT", H + 128 * t, H + 128 * t + 128)
-        src = T.cores[(rank - 1) % n_ranks]
-        L, sent, seen = a128("LAND%d" % t), R("sent", t, t + 1), R("seen", t, t + 1)
-        n = len(topo.engines(src, core))
-        emit("V", lambda: g.vector.wait_ge(T.sem["arr%d" % t], n), [sent, R("CHM", 1792, 2048)], [L], 1.0, False)
-        emit("S", lambda: g.scalar.wait_ge(T.sem["arr%d" % t], n), [sent, R("WZ1", 896, 1024)], [seen], 1.0, False)
-        emit("S", lambda: g.scalar.activation(ap(a128("LF")), ap(L), F.Relu, scale=1.0 / SENT), [seen], [a128("LF")], 193.0)
-        cp(a128("LI"), L)
-        tt(a128("LT2"), lib, a128("LF"), A.mult)
-        ts(a128("LY"), a128("LI"), 255, A.bitwise_and)
-        tt(lib, a128("LT2"), a128("LY"), A.add)
+        n = len(topo.engines(T.cores[(rank - 1) % n_ranks], core))
+        Y, L = R("YIN%d" % t, 0, 640), R("LIN%d" % t, 0, 8)
+        for k, r in ((2 * t, a512(Y[0])), (2 * t + 1, L)):
+            emit("S", lambda k=k: g.scalar.wait_ge(T.sem["arr%d" % k], n), [R("sent", k, k + 1), a128("DG")], [r], 1.0, False)
+        act(R("YT", H + 128 * t, H + 128 * t + 128), IND(Y, L))
 
     def out(lo, hi, src):
         dma("Y", T.yo[:, lo:hi], ap(src), [src], [])
@@ -650,7 +665,8 @@ def rank_program(g, core, T, topo):
             act(yo(l), a512("YR"), scale=-1.0, bias=col("C255"))
             out(1536 + 512 * l, 2048 + 512 * l, yo(l))
         level(3, yo(3), True)
-        out(3072, 3584, yo(3))
+        for a, b in HALF:
+            out(3072 + a, 3072 + b, sub(yo(3), a, b))
 
     load_lists()
     for t in range(2):
@@ -658,7 +674,6 @@ def rank_program(g, core, T, topo):
         for st in range(3):
             step(st)
         donors(t)
-        send(t)
         grafts(t)
         receive(t)
     last_levels()
@@ -695,8 +710,8 @@ def rank_program(g, core, T, topo):
             c["done"] = (sem, cnt[sem])
             clocks[c["done"]] = dict(seen[c["q"]], **{sem: cnt[sem]})
 
-    for s in sorted(cnt):
+    for s in sorted(cnt, key=lambda s: (s[0] == "d", len(s), s)):
         wait("G", s, cnt[s])
     dst = T.cores[(rank + 1) % n_ranks]
-    for t in range(2):
+    for t in range(4):
         g.wait_ge(T.sem["snt%d" % t], len(topo.engines(core, dst)))

@@ -1,8 +1,12 @@
-from concourse.mybir import AluOpType as A, ActivationFunctionType as F
+from concourse.mybir import AluOpType as A, ActivationFunctionType as F, AxisListType as AX
 
 H = 16
 LIB = 1024
+BY_SLOT = (1,)
+UP = 32.0
+ROUND = 1.5 * 2 ** 23
 MID = 1792.0
+BIG = 2.0 ** 23
 SIDE = 2064
 
 SCRATCH, PLACE = {}, {}
@@ -21,28 +25,31 @@ def declare(dtype, text, packed=False):
         SCRATCH["SM" + dtype] = ("sbuf", [128, o], dtype)
 
 
-declare("bfloat16", "YT:3616 ZAB:4128 SG:2064 TG:512 WAB:1024 DA:512 DB:512 Y2:1024 ZB:512 MN:1024 UU:512 CB:512 SA:512 AB:1024 DF:4096 DD:2048 "
-        "GV:2048 RAW:2048 LT4:4096 YO:2048 YR:512 YC0:512 YC1:512 YIN0:640 YIN1:640 PAY:512 SL0:1536 SL1:1536 LLO:512 LHI:512 "
-        "EQ:1024 O256:512 BQ:2048 KQ:2064 BC:1024 NBC:1024")
-declare("bfloat16", "HIT:32 INC:32 ONE:128 IB:128 NI:128 N256:128 I2:128 I4:128 IH:128 NH:128 BD:128 BD1:128 L00:128 L01:128 L10:128 L11:128 "
-        "SGB:128 LB:128 LT:128 TRI:128 MC:256 ZM:144 ZM8:144 ZN8:144 ZM16:144 ZMN:144 ZW1:144 ZW2:144 ZA0:144 ZAD:144 ZR2:144 SEL1:16 RQ:128 "
-        "S16:16 IQN:128 E2:128 E3:128", True)
-declare("float16", "KLF:256 KLH:256 WF:256 NXF:256 KTG:512 CHM:2048 WZ:2944 WN:2944 ZT:256")
+declare("bfloat16", "YT:3616 ZAB:4128 SG:2064 NT:2064 TG:512 WAB:1024 DA:512 DB:512 Y2:1024 ZB:512 MN:1024 UU:512 CB:512 SA:512 AB:2048 DF:4096 DD:2048 "
+        "GV:2048 RAW:2048 LT4:4096 YO:2048 YR:512 YC0:512 YC1:512 YIN0:640 YIN1:512 PAY:512 SL0:1536 SL1:1536 LLO:512 LHI:512 "
+        "O256:512 BQ:2048 KQ:2064 BC:1024 NBC:1024")
+declare("bfloat16", "HIT:32 INC:32 ONE:160 JB:160 NI:128 N256:128 I2:128 I3:128 I4:128 I255:128 I5:128 I6:128 I7:128 BD:128 BD1:128 L00:128 L01:128 L10:128 L11:128 "
+        "SGB:128 LB:128 LT:128 TRI:128 MC:256 ZM:144 ZM8:144 ZN8:144 ZM16:144 ZMN:144 ZW1:144 ZW2:144 ZAD:144 ZR2:144 SEL1:16 RQ:128 "
+        "IQN:128 E2:128 E3:128 ZMK:144 C4:128 KQ1:128", True)
+declare("float16", "KLF:256 KLH:256 WF:256 NXF:256 KTG:1024 CHM:2048 WZ:1920 WN:1920 ZT:256")
 declare("float16", "QCH:64 DNH:32 IOC:256 L512:32 HL:32 DG:128 H16:64", True)
-declare("uint16", "UL:256 SEL:32 NL:32 KEYU:32 CU:256 SLOT:32 LL0:8 LL1:8 LIN0:8 LIN1:8")
+declare("uint16", "UL:256 SEL:32 NK:64 NL:32 KEYU:32 CU:256 SLOT0:32 SLOT1:32 LL0:8 LL1:8 LIN0:32 LIN1:32")
 declare("int32", "KLD:256 MLD:128 WTI:2")
-declare("float32", "KT:1552 DR:640 KOF:256 KOT:256 WTF:2")
-declare("float32", "TOB0:32 TOB1:32 TOB2:32 T2:32 UA:128 UD:64 UM:64 DK:32 ES0:32 ES1:32 ES2:32 Q0:32 Q1:32 Q2:32 Q3:32 QD:32 QL:8 QE:8 QI:8 S1:32 S2:32 LQ:32 CH0:32 CH1:32 CH2:32 ST:64 NS:64 "
+declare("float32", "YF:512 YL:128 YW:1536 KT:1552 DR:640 KOF:256 KOT:256 WTF:2")
+declare("float32", "XN:128 XH:256 XS:128 ON:128 OH:256 OS:128 T2:32 UA:64 UN:64 ES:96 Q0:32 Q1:32 Q2:32 Q3:32 QD:8 QL:8 QE:8 QI:8 UH:8 S1:32 CH0:32 CH1:32 CH2:32 ST:64 NS:96 NW:96 LW:96 "
         "DS:64 DT:64 LV:64 B1:64 B2:64 B3:64 B4:64 XF:16 LANE:32 NL512:32 IOF:256 C255:8 CNX:8 "
-        "CMID:8", True)
-declare("int32", "UI:128 U2M:64 PRI:64 SHI:64 UMI:64 BEST:32 MI:32 MTT:32 HD:32 DNI:32 KI:32 QCI:64 LI0:32 LI1:32 LI2:32", True)
+        "CMID:8 CUP:8", True)
+declare("int32", "U16:8 KA:96 UI:128 PRI:64 SHI:64 UMI:64 BEST:32 MI:32 MTT:32 HD:32 DNI:32 KI:32 QCI:64 LI0:32 LI1:32 LI2:32", True)
 for _k in range(8):
     SCRATCH["P%d" % _k] = ("psum", [128, 512], "float32")
 
 SEMAPHORES = ["cV", "cS", "cP", "cG", "arr0", "arr1", "arr2", "arr3", "snt0", "snt1", "snt2", "snt3"] + ["d%d" % k for k in range(27)]
 
-GATHER, SCATTER, PE, WAKE, WAKE_SAME = 1.4, 3.0, 0.4, 250.0, 270.0
-PASSES, SWEEPS, SHORT, LEAD = 4, 3, 72, 1000.0
+GATHER, SCATTER, PE, CYCLE, WAKE, WAKE_SAME = 1.1, 2.5, 0.42, 0.83, 215.0, 240.0
+TABLE = 1400.0
+PASSES, SHORT, LEAD = 4, 72, 1000.0
+SWEEPS, TRIES = ((100, 400.0), (70, 300.0), (50, 250.0), (80, 300.0), (60, 200.0), (90, 200.0), (56, 150.0)), 2500
+PACES = ((1.0, 1.0, 1.0, 0.8), (1.45, 2.1, 0.9, 1.0), (1.2, 1.3, 1.5, 1.2))
 ORDER = []
 
 
@@ -52,7 +59,7 @@ def arrange(calls):
     after, before = [[] for _ in range(n)], [[] for _ in range(n)]
     for k, c in enumerate(calls):
         for d, by_sem in c["deps"].items():
-            gap = calls[d]["late"] + ((WAKE_SAME if calls[d]["q"] == c["q"] else WAKE) if by_sem else 0.0)
+            gap = calls[d]["late"] * (by_sem is not None) + ((WAKE_SAME if calls[d]["q"] == c["q"] else WAKE) if by_sem else 0.0)
             after[d].append((k, gap))
             before[k].append((d, gap))
 
@@ -93,68 +100,103 @@ def arrange(calls):
         if best is None or total < best[0]:
             best = (total, order)
         way = run(before, after, end, [c["late"] for c in calls])[1]
-    return polish(calls, best[1], before)
+    return polish(calls, best[1])
 
 
-def polish(calls, order, before):
+def polish(calls, order):
     n = len(calls)
-    qs = {}
-    for k in order:
-        qs.setdefault(calls[k]["q"], []).append(k)
-    cost = [c["cost"] for c in calls]
-    late = [c["late"] for c in calls]
+    qof = ["VSPGY".index(c["q"]) for c in calls]
+    paces = []
+    for plain, indexed, wake, far in PACES:
+        late = [c["late"] * far for c in calls]
+        before, after = [[] for _ in range(n)], [[] for _ in range(n)]
+        for k, c in enumerate(calls):
+            for d, by_sem in c["deps"].items():
+                gap = late[d] * (by_sem is not None) + ((WAKE_SAME if qof[d] == qof[k] else WAKE) * wake if by_sem else 0.0)
+                before[k].append((d, gap))
+                after[d].append((k, gap))
+        paces.append(([c["cost"] * (indexed if c["indexed"] else plain) for c in calls], late, before, after, [0.0] * n))
+    links = [[[u for u, gap in x] for x in paces[0][j]] for j in (2, 3)]
+    seq, x = list(order), [1]
 
-    def times():
-        end, why, at, free, seq = [None] * n, [None] * n, {q: 0 for q in qs}, {q: 0.0 for q in qs}, []
-        moved = True
-        while moved:
-            moved = False
-            for q, L in qs.items():
-                i, t = at[q], free[q]
-                while i < len(L):
-                    k = L[i]
-                    s, w = t, (L[i - 1] if i else None)
-                    for d, gap in before[k]:
-                        e = end[d]
-                        if e is None:
-                            break
-                        if e + gap > s:
-                            s, w = e + gap, d
-                    else:
-                        t = end[k] = s + cost[k]
-                        why[k] = w
-                        seq.append(k)
-                        i += 1
-                        continue
-                    break
-                if i > at[q]:
-                    at[q], free[q], moved = i, t, True
-        if len(seq) < n:
-            return 1e18, 1e18, None, None
-        return max(e + l for e, l in zip(end, late)), sum(end), why, (seq, end)
+    def draw(m):
+        x[0] = (x[0] * 1103515245 + 12345) % 2147483648
+        return (x[0] >> 8) % m
 
-    best = times()
-    for _ in range(SWEEPS):
-        k = max(range(n), key=lambda k: best[3][1][k] + late[k])
-        path = []
-        while k is not None:
-            path.append(k)
-            k = best[2][k]
-        for y, x in zip(path, path[1:]):
-            L = qs[calls[y]["q"]]
-            if calls[x]["q"] != calls[y]["q"]:
-                continue
-            for k, moves in ((y, (-1, -2, -3, -4)), (x, (1, 2, 3, 4))):
-                i = L.index(k)
-                for m in moves:
-                    if 0 <= i + m < len(L):
-                        L.insert(i + m, L.pop(i))
-                        t = times()
-                        if t[0] < best[0] - 1 or (t[0] <= best[0] and t[1] < best[1] - 1):
-                            best = t
-                            break
-                        L.insert(i, L.pop(i + m))
-    return best[3][0]
+    def times(ks, free, cost, before, end):
+        for k in ks:
+            s = free[qof[k]]
+            for d, gap in before[k]:
+                if end[d] + gap > s:
+                    s = end[d] + gap
+            end[k] = free[qof[k]] = s + cost[k]
+
+    for lo, size, heat in [(lo, size, heat) for size, heat in SWEEPS for lo in range(0, n - 1, size // 2)]:
+        given = []
+        for j, (cost, late, before, after, end) in enumerate(paces):
+            times(seq, [0.0] * 5, cost, before, end)
+            if j == 0:
+                seq.sort(key=lambda k: end[k] - cost[k])
+                win = seq[lo:lo + size]
+            tail, head, free = {}, [0.0] * 5, [0.0] * 5
+            for k in reversed(seq[lo + size:]):
+                tail[k] = head[qof[k]] = cost[k] + max([late[k], head[qof[k]]] + [gap + tail[u] for u, gap in after[k]])
+            for k in seq[:lo]:
+                free[qof[k]] = end[k]
+            out = {k: max([late[k]] + [gap + tail[u] for u, gap in after[k] if u in tail]) for k in win}
+            given.append((cost, before, end, head, out, free, 1e5 / max(end)))
+
+        def score(ks, a):
+            total = 0.0
+            for cost, before, end, head, out, free, w in given:
+                free = free[:]
+                for k in ks[:a]:
+                    free[qof[k]] = end[k]
+                times(ks[a:], free, cost, before, end)
+                far = [end[k] + out[k] for k in ks]
+                total += w * (max(max(far), max(f + h for f, h in zip(free, head))) + 5e-4 * sum(far))
+            return total
+
+        def longest(ks):
+            path = []
+            for cost, before, end, head, out, free, w in given:
+                prev, last = {}, {}
+                for k in ks:
+                    prev[k], last[qof[k]] = last.get(qof[k]), k
+                k = max([(end[k] + out[k], k) for k in ks] + [(end[k] + head[q], k) for q, k in last.items()])[1]
+                while k in prev:
+                    path.append(k)
+                    k = max([(end[d] + gap, d) for d, gap in before[k]] + [(end[prev[k]] if prev[k] is not None else free[qof[k]], prev[k])],
+                            key=lambda e: e[0])[1]
+            return path
+
+        now, clean = score(win, 0), len(win)
+        best, path = (now, win), longest(win)
+        for it in range(TRIES):
+            y = path[draw(len(path))]
+            i = win.index(y)
+            way = -1 if draw(2) else 1
+            if way > 0:
+                while i > 0 and (win[i] == y or qof[win[i]] != qof[y]):
+                    i -= 1
+                y = win[i]
+            j, m = i, 1 + draw(2 << draw(4))
+            while 0 <= j + way < len(win) and m:
+                j += way
+                m -= qof[win[j]] == qof[y]
+            a, b = min(i, j), max(i, j) + 1
+            need = {y}
+            for k in win[a:b][::way]:
+                if k in need:
+                    need.update(links[way > 0][k])
+            new = win[:a] + sorted(win[a:b], key=lambda k: (k in need) != (way < 0)) + win[b:]
+            if new != win:
+                s, clean = score(new, min(a, clean)), a
+                if s < now + heat * (1 - it / TRIES) * (draw(1024) / 1024) ** 2:
+                    win, now, path, clean = new, s, longest(new), len(win)
+                    best = min(best, (s, new))
+        seq[lo:lo + size] = best[1]
+    return seq
 
 
 def rank_program(g, core, T, topo):
@@ -193,9 +235,11 @@ def rank_program(g, core, T, topo):
                 ps = is_psum(b)
                 if ps:
                     lo, hi = 0, 512
-                for (k, lo2, hi2, w2) in acc.get(b, ()):
+                for (k, lo2, hi2, w2, st2) in acc.get(b, ()):
                     same = calls[k]["q"] == q
                     if lo2 >= hi or hi2 <= lo or not (w or w2 or (ps and not same)):
+                        continue
+                    if same and not ps and st == st2 and (lo - lo2) % st:
                         continue
                     deps[k] = calls[k]["sem"] is not None and not (same and q == "P")
         for rs, w in ((writes, True), (reads, False)):
@@ -208,17 +252,20 @@ def rank_program(g, core, T, topo):
                     L[:] = [e for e in L if not (lo <= e[1] and e[2] <= hi)]
                 elif ps:
                     L[:] = [e for e in L if e[3] or e[0] == me or calls[e[0]]["q"] == q]
-                L.append((me, lo, hi, w))
-        calls.append(dict(q=q, fns=fn if isinstance(fn, list) else [fn], deps=deps, cost=cost, late=late, sem="c" + q if sem is None else sem or None))
+                L.append((me, lo, hi, w, st))
+        calls.append(dict(q=q, fns=fn if isinstance(fn, list) else [fn], deps=deps, cost=cost, late=late,
+                          indexed=q in "VS" and any(SCRATCH.get(r[0], "...")[2] == "uint16" for r in reads), sem="c" + q if sem is None else sem or None))
         return me
 
     def chain(*ks):
         for a, b in zip(ks, ks[1:]):
-            calls[b]["deps"].setdefault(a, False)
+            calls[b]["deps"].setdefault(a, None)
 
     def dma(q, out, in_, reads, writes):
         dmas[0] += 1
-        emit(q, lambda: ENG[q].dma_start(out, in_), reads, writes, 60.0, "d%d" % (dmas[0] - 1), 1500.0)
+        r = (writes or reads)[0]
+        size = width(r) * (2 if narrow(r) else 4)
+        emit(q, lambda: ENG[q].dma_start(out, in_), reads, writes, 60.0, "d%d" % (dmas[0] - 1), 1600.0 + 0.6 * size)
 
     def width(r):
         return 16 * width(r[2]) if r[0] == "ind" else -(-(r[2] - r[1]) // r[3])
@@ -230,10 +277,10 @@ def rank_program(g, core, T, topo):
         if out[0] == "ind":
             return 50 + SCATTER * width(out)
         if any(r[0] == "ind" for r in ins):
-            return 50 + (1.4 if len(ins) == 2 else GATHER) * width(out)
+            return 50 + GATHER * width(out)
         if len(ins) == 2 and not any(is_psum(r[0]) for r in ins):
-            return max(66, 2.0 * width(out))
-        return max(66, width(out) * (0.5 if narrow(out, *ins) else 1.0))
+            return 10 + CYCLE * max(64, 2 * width(out))
+        return 10 + CYCLE * max(64, width(out) * (0.5 if narrow(out, *ins) else 1.0))
 
     def IND(win, off):
         return ("ind", win, off)
@@ -269,7 +316,7 @@ def rank_program(g, core, T, topo):
 
     def act(out, a, func=F.Identity, scale=1.0, bias=0.0, also=()):
         return emit("S", lambda: g.scalar.activation(ap(out), ap(a), func, bias=num(bias), scale=num(scale)), rd(a, scale, bias, *also), [out],
-                    65 + width(out) * (GATHER if a[0] == "ind" else 1.0))
+                    65 + width(out) * GATHER if a[0] == "ind" else 90 + width(out) * CYCLE)
 
     def mms(items):
         return emit("P", [lambda x=x: g.tensor.matmul(ap(x[0]), ap(x[1]), ap(x[2]), x[3], x[4]) for x in items], [r for x in items for r in x[1:3]],
@@ -280,12 +327,12 @@ def rank_program(g, core, T, topo):
 
     def iota(out, pat, base, chm, small=True):
         if small:
-            emit("G", lambda: g.iota(ap(out), pat, base, chm, allow_small_or_imprecise_dtypes=True), [], [out], 130 + 2 * width(out))
+            emit("G", lambda: g.iota(ap(out), pat, base, chm, allow_small_or_imprecise_dtypes=True), [], [out], 170 + 2.2 * width(out))
         else:
-            emit("G", lambda: g.iota(ap(out), pat, base, chm), [], [out], 130 + 2 * width(out))
+            emit("G", lambda: g.iota(ap(out), pat, base, chm), [], [out], 170 + 2.2 * width(out))
 
     def asel(out, in_, pat, op, base, chm):
-        emit("G", lambda: g.affine_select(ap(out), ap(in_), pat, op, 0.0, base, chm), [in_], [out], 170 + 2 * width(out))
+        emit("G", lambda: g.affine_select(ap(out), ap(in_), pat, op, 0.0, base, chm), [in_], [out], 220 + 2.2 * width(out))
 
     def phases(out, Z, src, first, last, by=16):
         for j in range(0, 16, by):
@@ -303,33 +350,35 @@ def rank_program(g, core, T, topo):
     c64 = lambda b: R(b, 0, 64)
     col = lambda b, k=0: R(b, k, k + 1)
     HALF = ((0, 256), (256, 512))
-    I, NI = a128("IB"), a128("NI")
+    I, NI = R("JB", 16, 144), a128("NI")
 
     dma("S", ap(a256("KLD")), T.kid[:, :], [], [a256("KLD")])
     dma("Y", ap(a128("MLD")), T.mx[:, :], [], [a128("MLD")])
     dma("Y", ap(R("YT", H, H + 1536)), T.lv[:, :], [], [R("YT", H, H + 1536)])
     dma("Y", ap(a512("TG")), T.tg[:, :], [], [a512("TG")])
-    for t in range(2):
-        dma("Y", ap(R("YIN%d" % t, 512, 640)), T.lv[:, 128 * t:128 * t + 128], [], [R("YIN%d" % t, 512, 640)])
     dma("Y", ap(R("WTI", 0, 2)), T.wt[:, :], [], [R("WTI", 0, 2)])
+    chain(1, 2, 3, 4)
 
     O256 = a512("O256")
-    ms(a128("ONE"), 1.0)
+    ms(R("ONE", 0, 160), 1.0)
     ms(O256, 256.0)
-    for r in (R("YT", 0, H), R("KQ", 0, 16), R("ZM", 0, 144), R("ZAB", 0, 1), R("ZAB", 2049, SIDE + 1), R("SG", 0, 1),
-              R("DR", 512, 640), R("KT", 0, 513)):
+    for r in (R("YT", 0, H), R("KQ", 0, 1024), R("KQ", 1024, 2064), R("ZM", 0, 144), R("ZAB", 0, 1), R("ZAB", 2049, SIDE + 1), R("NT", 0, 1),
+              R("DR", 512, 640)):
         ms(r, 0.0)
-    for b, v in (("C255", 255.0), ("CNX", MID - 1535.0), ("CMID", MID)):
-        ms(R(b, 0, 8), v)
-    ms(R("S16", 0, 16), 16.0)
-    asel(I, a128("ONE"), [[-1, 128]], A.is_equal, 0, 1)
+    ms(R("KT", 0, 513), 1.0)
+    for b, v in (("C255", 255.0), ("CMID", MID), ("CUP", UP)):
+        iota(R(b, 0, 8), [[0, 8]], int(v), 0)
+    asel(R("JB", 0, 160), R("ONE", 0, 160), [[-1, 160]], A.is_equal, 16, 1)
     iota(c32("LI1"), [[0, 32]], 0, 1, False)
+    ts(col("U16"), col("LI1"), 16, A.bitwise_and)
     for u in range(2):
+        ts(col("UH", u), col("U16"), 16.0 * u, A.is_equal)
         for v in range(2):
-            asel(a128("L%d%d" % (u, v)), a128("ONE"), [[-32, 4], [1000, 2], [-1, 16]], A.is_equal, -16 * u - 1000 * v, 1)
+            ts(a128("L%d%d" % (u, v)), R("JB", 16 * (1 + u - v), 16 * (9 + u - v)), col("UH", u), A.mult)
     for j in range(4):
         asel(R("BQ", 512 * j, 512 * j + 512), O256, [[-1, 4], [-16, 8], [0, 16]], A.is_equal, -4 * j, 1)
-        asel(R("KQ", 16 + 512 * j, 528 + 512 * j), O256, [[-1, 4], [-16, 8], [1000, 16]], A.is_equal, -4 * j, 1)
+    asel(a128("KQ1"), a128("O256"), [[-1, 16], [-16, 8]], A.is_equal, 0, 1)
+    cp(R("KQ", 16, 2064, 16), a128("KQ1"))
     asel(a128("BD1"), a128("ONE"), [[-16, 8], [0, 16]], A.is_ge, 0, 1)
     asel(a128("BD"), a128("BD1"), [[16, 8], [0, 16]], A.is_ge, 15, -1)
     iota(c32("LI0"), [[16, 32]], 0, 0, False)
@@ -339,23 +388,24 @@ def rank_program(g, core, T, topo):
     iota(a512("LLO"), [[0, 4], [1, 128]], 0, 0)
     iota(a512("LHI"), [[1, 4], [0, 128]], 0, 0)
     iota(a256("IOF"), [[SIDE // 16, 2], [1, 128]], -int(MID), 0)
-    asel(a128("TRI"), a128("O256"), [[-1, 128]], A.is_ge, 0, 1)
+    asel(a128("TRI"), a128("O256"), [[1, 128]], A.is_ge, 0, -1)
     asel(R("SEL1", 0, 8), R("ONE", 0, 8), [[-16, 8]], A.is_equal, -1, 1)
     asel(a128("RQ"), a128("ONE"), [[0, 16], [-16, 8]], A.is_equal, 0, 1)
-    for b, x in (("BC", 1), ("NBC", -1)):
-        iota(R(b, 0, 1024), [[-240 * x, 8], [0, 128]], x, 15 * x)
-        asel(R(b, 0, 1024), R(b, 0, 1024), [[-16, 8], [0, 128]], A.is_ge, 0, 1)
-        asel(R(b, 0, 1024), R(b, 0, 1024), [[16, 8], [0, 128]], A.is_ge, 1, -1)
+    iota(R("NBC", 0, 1024), [[-240, 8], [0, 128]], 1, 15)
+    asel(R("BC", 0, 1024), R("NBC", 0, 1024), [[16, 8], [0, 128]], A.is_ge, 1, -1)
+    for j in range(2):
+        act(R("BC", 512 * j, 512 * j + 512), R("BC", 512 * j, 512 * j + 512), F.Relu)
+        act(R("NBC", 512 * j, 512 * j + 512), R("BC", 512 * j, 512 * j + 512), scale=-1.0)
     for lo in (0, 448):
         act(R("WZ", lo, lo + 448), R("O256", 0, 448), scale=0.0)
-    for b, lo in (("WZ", 1024), ("WZ", 2048), ("WN", 0), ("WN", 1024), ("WN", 2048)):
-        dma("Y", ap(R(b, lo, lo + 896)), ap(R("WZ", 0, 896)), [R("WZ", 0, 896)], [R(b, lo, lo + 896)])
-    for b, w in (("NI", -1.0), ("N256", -256.0), ("I2", 2.0), ("I4", 4.0), ("IH", 0.5), ("NH", -0.5)):
+    for b, lo in (("WZ", 1024), ("WN", 0), ("WN", 1024)):
+        dma("Y", ap(R(b, lo, lo + 896)), ap(R("WZ", 0, 896)), [R("WZ", 0, 896), R("YT", H, H + 1)], [R(b, lo, lo + 896)])
+    for b, w in (("NI", -1.0), ("N256", -256.0), ("I255", 255.0 / 256), *[("I%d" % m, float(m)) for m in range(2, 8)]):
         ts(a128(b), I, w, A.mult)
     ts(c32("LI2"), c32("LI1"), 15, A.bitwise_and)
     for k in range(4):
         ts(c32("Q%d" % k), c32("LI2"), float(k), A.is_equal)
-    tt(c32("QD"), c32("Q1"), c32("Q0"), A.subtract)
+    ts(col("QD"), col("Q1"), 2048.0, A.mult, col("Q0"), A.add)
     for k in (2, 3):
         ts(a128("E%d" % k), I, col("Q%d" % k), A.mult, 256.0, A.mult)
     ts(col("QL"), col("Q3"), 128.0, A.mult, col("Q2"), A.add)
@@ -363,25 +413,35 @@ def rank_program(g, core, T, topo):
     ts(col("QI"), col("Q3"), 4.0, A.mult, col("QE"), A.add)
     cp(R("WTF", 0, 2), R("WTI", 0, 2))
     cp(R("ZM", 15, 128, 16), R("BD", 0, 128, 16))
-    for Z, w in (("ZA0", col("Q0")), ("ZAD", col("QD")), ("ZR2", col("QL")), ("ZMN", -1.0), ("ZM8", 8.0), ("ZN8", -8.0), ("ZM16", 16.0),
+    for Z, w in (("ZAD", col("QD")), ("ZR2", col("QL")), ("ZMN", -BIG), ("ZMK", BIG), ("ZM8", 8.0), ("ZN8", -8.0), ("ZM16", 16.0),
                  ("ZW1", col("WTF", 0)), ("ZW2", col("WTF", 1))):
         ts(R(Z, 0, 144), R("ZM", 0, 144), w, A.mult)
     tt(c32("LANE"), c32("LI2"), c32("LI0"), A.add)
     ts(c32("CH2"), c32("LANE"), 1537.0, A.add)
     ts(c32("L512"), c32("LANE"), 512.0, A.add)
     ts(c32("NL512"), c32("LANE"), -1.0, A.mult, -512.0, A.add)
-    ts(c32("LQ"), c32("LANE"), 1.0 / 512, A.mult)
+    for b in ("XH", "XS"):
+        iota(R(b, 0, 96), [[0, 96]], 1, 0)
+    ts(R("XS", 1, 96, 3), c32("LANE"), 513.0, A.add)
+    ts(R("XS", 2, 96, 3), c32("LANE"), -1.0, A.mult, -1.0, A.add)
+    iota(R("C4", 0, 96), [[0, 96]], -1, 0)
+    ms(R("C4", 1, 96, 3), -BIG / 2)
     tt(a128("LB"), a128("LT"), a128("BD"), A.subtract)
-    cp(a256("IOC"), a256("IOF"))
+    act(a256("IOC"), a256("IOF"))
 
     def load_lists():
         for j in range(2):
             c = (128 * j, 128 * j + 128)
             ts(R("KLF", *c), R("KLD", *c), -MID, A.add)
             vtr(R("KLH", *c), R("KLF", *c))
+        for j in range(2):
+            mms([(R("P%d" % j, 16 * i + c2, 16 * i + 16, 2), a128("L%d%d" % (c2, x)), R("KLH", 16 * x + 8 * j + i, 256, 32), x == 0, x == 1)
+                 for i in range(2) for c2 in range(2) for x in range(2)])
+            ts(R("UL", 128 * j, 128 * j + 32), c32("P%d" % j), MID + H, A.add)
+        for j in range(2):
             mms([(R("P7", 2 * k + c2, 256, 16), a128("L%d%d" % (c2, x)), R("KLH", 32 * k + 16 * x, 32 * k + 16 * x + 16), x == 0, x == 1)
                  for k in range(4 * j, 4 * j + 4) for c2 in range(2) for x in range(2)])
-        for c in ((0, 160), (160, 256)):
+        for c in ((32, 128), (160, 256)):
             ts(R("UL", *c), R("P7", *c), MID + H, A.add)
         act(a256("WF"), a256("P7"))
         ts(a128("SGB"), a128("MLD"), 2.0, A.mult, -1.0, A.add)
@@ -390,9 +450,10 @@ def rank_program(g, core, T, topo):
             for r in range(4):
                 mm(R(P, 128 * r, 128 * r + 128), R("BQ", 512 * l + 128 * r, 512 * l + 128 * r + 128), a128("SGB"), True, True)
             act(R("SG", 1 + 512 * l, 513 + 512 * l), a512(P), scale=1.0 / 256)
+            ts(R("NT", 1 + 512 * l, 513 + 512 * l), R("SG", 1 + 512 * l, 513 + 512 * l), 0.0, A.is_lt)
 
     def lists():
-        act(a256("NXF"), a256("WF"), F.Relu, bias=col("CNX"))
+        ts(a256("NXF"), a256("WF"), MID - 1534.0, A.add, 1.0, A.max)
         for l in (1, 2):
             P = "P%d" % (5 + l)
             for k in range(2):
@@ -410,15 +471,18 @@ def rank_program(g, core, T, topo):
             za, yb = R("RAW", 1024 * (l % 2), 1024 * (l % 2) + 512), R("RAW", 1024 * (l % 2) + 512, 1024 * (l % 2) + 1024)
         for h, c in enumerate(HALF if out else HALF):
             tt(sub(za, *c), IND(below(l), ul(0, l, *c)), sub(tab("SG", 0, l), *c), A.mult)
-            if tables and l == 3:
+            if tables and l:
                 act(sub(yb, *c), IND(below(l), ul(1, l, *c)), F.Relu, scale=-1.0, bias=col("C255"))
-                act(sub(tab("ZAB", SIDE, l), *c), sub(yb, *c), scale=-1.0, bias=col("C255"))
+                if l == 3:
+                    act(sub(tab("ZAB", SIDE, l), *c), sub(yb, *c), scale=-1.0, bias=col("C255"))
             else:
                 act(sub(yb, *c), IND(below(l), ul(1, l, *c)))
             ts(sub(mn, *c), sub(za, *c), 0.0, A.min, -255.0, A.max)
             if out:
                 P = R("P%d" % (2 * (l % 2) + h), 0, c[1] - c[0])
-                mm(P, I, sub(yb, *c), True, False)
+                if tables and l:
+                    mm(P, a128("I255"), R("O256", *c), True, False)
+                mm(P, NI if tables and l else I, sub(yb, *c), not (tables and l), False)
                 mm(P, NI, sub(mn, *c), False, True)
                 tt(R("UU", *c) if cut else sub(out, *c), P, sub(za, *c), A.max)
                 if cut:
@@ -427,18 +491,33 @@ def rank_program(g, core, T, topo):
             for c in HALF if l == 3 else ((0, 512),):
                 ts(sub(tab("ZAB", 0, l), *c), sub(za, *c), 255.0, A.min, -255.0, A.max)
                 if l < 3:
-                    ts(sub(tab("ZAB", SIDE, l), *c), sub(yb, *c), 255.0, A.min)
+                    act(sub(tab("ZAB", SIDE, l), *c), sub(yb, *c), scale=-1.0, bias=col("C255"))
 
     def levels():
         lists()
         for l in range(4):
             level(l, yt(l) if l < 3 else None, False, True)
 
+    part = lambda b, j, k=0: R(b, 96 * k + j - 1, 96 * k + 96, 3)
+    a96 = lambda b: R(b, 0, 96)
+
+    def offer(X, a, b, k=0, neg=None):
+        tt(part(X, 1, k), b, a, A.subtract)
+        tt(part(X, 2, k), b, a, A.max)
+        if neg:
+            return tt(part(X, 3, k), neg[0], neg[1], A.max)
+        tt(c32("S1"), b, a, A.min)
+        ts(part(X, 3, k), c32("S1"), -1.0, A.mult)
+
+    def choose(out, X, k=0):
+        o, x = R(out, 96 * k, 96 * k + 96), R(X, 96 * k, 96 * k + 96)
+        emit("V", lambda: g.vector.tensor_tensor_scan(ap(o), ap(a96("P6")), ap(x), -1.0, A.mult, A.min), [a96("P6"), x], [o], vcost(o, a96("P6")))
+
     def step(st):
-        TOB, ES, zb = "TOB%d" % st, "ES%d" % st, a512("ZB")
+        ab, zb = R("AB", 512 * (st + 1), 0), a512("ZB")
         if st == 0:
             D, mn, za, yb = a512("TG"), R("MN", 512, 1024), tab("ZAB", 0, 3), tab("ZAB", SIDE, 3)
-            mm(a512("P6"), I, tab("SG", 0, 3), True, True)
+            mm(a512("P6"), I, tab("NT", 0, 3), True, True)
             for c in HALF:
                 tt(sub(zb, *c), sub(yb, *c), R("P6", *c), A.mult)
         else:
@@ -447,83 +526,99 @@ def rank_program(g, core, T, topo):
                 nl = R("NL", c[0] // 16, c[1] // 16)
                 cp(sub(za, *c), IND(R("ZAB", 0, 1537), nl))
                 act(sub(yb, *c), IND(R("ZAB", SIDE, SIDE + 1537), nl))
-                tt(sub(zb, *c), IND(R("SG", 0, 1537), nl), sub(yb, *c), A.mult)
+                tt(sub(zb, *c), IND(R("NT", 0, 1537), nl), sub(yb, *c), A.mult)
                 ts(sub(mn, *c), sub(za, *c), 0.0, A.min)
-            if st == 1:
-                act(a512("KTG"), IND(R("KT", 0, 1537), c32("NL")))
+        if st == 0:
+            offer("XN", R("NXF", 96, 128), R("NXF", 224, 256))
+        if st == 1:
+            act(a512("KTG"), IND(R("KT", 0, 1537), c32("NL")))
+            phases(c32("P7"), "ZAD", a512("KTG"), True, True, 4)
+            cp(c32("KA"), c32("P7"))
+        if st == 2:
+            mm(c64("P7"), a128("I4"), c64("ONE"), True, False)
+            phases(c64("P7"), "ZM8", R("AB", 512, 1536), False, True, 4)
+            tt(c64("NS"), c64("ES"), c64("P7"), A.add)
+            mms([(a512("P7"), a128("E2"), a512("LLO"), True, False), (a512("P7"), a128("E3"), a512("LHI"), False, False)])
         for h, c in enumerate(HALF):
             PD, EA, PA = a256("P%d" % h), R("P%d" % h, 256, 512), a256("P%d" % (4 + h))
             PB, EB = a256("P%d" % (2 + h)), R("P%d" % (2 + h), 256, 512)
             d, wa, wb = sub(D, *c), R("WAB", *c), sub(R("WAB", 512, 0), *c)
             mm(PD, I, d, True, True)
+            tt(R("CB", *c), sub(za, *c), PD, A.is_gt)
             mm(PB, I, d, True, False)
             mm(PB, I, sub(mn, *c), False, False)
-            tt(R("CB", *c), sub(za, *c), PD, A.is_gt)
             mm(PB, a128("N256"), R("CB", *c), False, True)
             act(wb, PB, F.Relu)
             mm(EB, NI, sub(yb, *c), True, False)
             mm(EB, I, wb, False, True)
-            act(sub(R("AB", 512, 0), *c), EB, F.Abs)
+            act(sub(ab, *c), EB, F.Abs)
             tt(R("SA", *c), sub(yb, *c), PD, A.is_le)
             mm(PA, I, d, True, False)
-            mm(PA, a128("NH"), sub(yb, *c), False, False)
-            mm(PA, a128("IH"), sub(zb, *c), False, True)
+            mm(PA, NI, sub(zb, *c), False, True)
             tt(wa, R("SA", *c), PA, A.mult)
             mm(EA, NI, sub(za, *c), True, False)
             mm(EA, a128("I2"), sub(mn, *c), False, False)
             mm(EA, I, wa, False, True)
             act(R("AB", *c), EA, F.Abs)
-        if st == 0:
-            na, dk = R("NXF", 96, 128), c32("DK")
-            tt(dk, R("NXF", 224, 256), na, A.subtract)
-        elif st == 1:
-            na, dk = c32("P7"), c32("P7", 1)
-            phases(na, "ZA0", a512("KTG"), True, True, 4)
-            phases(dk, "ZAD", a512("KTG"), True, True, 4)
-        phases(c32("P6"), "ZMN", R("AB", 512, 1024), True, False)
-        phases(c32("P6"), "ZM", a512("AB"), False, True)
-        phases(c32("P4"), "ZM8", R("AB", 512, 1024), True, True)
-        ts(c32(TOB), c32("P6"), 0.0, A.is_gt)
-        ts(c32(ES), c32("P6"), 0.0, A.min, 8.0, A.mult)
+        if st == 1:
+            ts(c32("KA", 1), c32("KA"), 2047, A.bitwise_and)
+            ts(c32("KA", 2), c32("KA"), 11, A.arith_shift_right)
+            offer("XN", c32("KA", 1), c32("KA", 2))
+        dif = part("P6", 2)
+        mm(a96("P6"), I, a96("C4"), True, False)
+        phases(dif, "ZMN", sub(ab, 0, 512), False, False)
+        phases(dif, "ZMK", a512("AB"), False, True)
+        ts(c32("ES", st), dif, 8.0 / BIG, A.mult, -4.0, A.min)
         if st == 2:
-            for k in range(2):
-                phases(c64(("P5", "P7")[k]), "ZW%d" % (k + 1), R("WAB", 0, 1024), True, True)
-                cp(R("UI", 64 * k, 64 * k + 64), c64(("P5", "P7")[k]))
-            tt(c64("PRI"), c64("UI"), c64("P7"), A.mult)
+            chain(phases(c64("P0"), "ZW1", R("WAB", 0, 1024), True, True), phases(R("P4", 256, 320), "ZW2", R("WAB", 0, 1024), True, True))
+            ts(R("UI", 64, 128), c64("P0"), 32.0, A.add)
+            cp(c64("UI"), c64("P0"))
+            tt(c64("PRI"), R("UI", 64, 128), R("P4", 256, 320), A.mult)
             ts(c64("UMI"), c64("UI"), 127, A.bitwise_and)
             ts(c64("SHI"), c64("PRI"), 5, A.arith_shift_right, 1023, A.bitwise_and)
-            ts(c64("U2M"), R("UI", 64, 128), 1023, A.bitwise_and)
-            tt(c64("UA"), c64("SHI"), c64("U2M"), A.add)
-            ts(R("UA", 64, 128), c64("UMI"), 2.0, A.mult, 1.0, A.add)
+            ts(part("XH", 2), c32("SHI", 1), 1025.0, A.add)
+            ts(part("XH", 3), c32("SHI"), -1.0, A.mult, -1.0, A.add)
+            ts(c64("UA"), c64("UMI"), 2.0, A.mult, 2.0, A.add)
+            ts(c64("UN"), c64("UMI"), -2.0, A.mult, -2.0, A.add)
+            offer("XH", c32("UA"), c32("UA", 1), 1, (c32("UN"), c32("UN", 1)))
             for k in range(2):
-                tt(c32("UD", k), c32("UA", 2 * k + 1), c32("UA", 2 * k), A.subtract)
-                tt(c32("UM", k), c32("UD", k), c32(TOB), A.mult)
-                tt(c32("H16", k), c32("UM", k), c32("UA", 2 * k), A.add)
+                choose("OH", "XH", k)
+            ts(c32("CU"), part("OH", 3), -1.0, A.mult, -1.0, A.add)
+            ts(c64("H16"), R("OH", 2, 192, 3), -1.0, A.mult, -1.0, A.add)
         if st < 2:
-            tt(c32("S2"), c32(TOB), dk, A.mult)
-            tt(c32("CH%d" % st), c32("S2"), na, A.add)
-            cp(c32("NL"), c32("CH%d" % st))
-        tt(c32("S1"), c32(TOB), c32("LQ"), A.add)
-        ts(c32("SEL"), c32("S1"), 512.0, A.mult)
+            choose("ON", "XN")
+            ts(c32("NL"), part("ON", 3), -1.0, A.mult, -1.0, A.add)
+            ts(c32("CH%d" % st), part("ON", 3), -1.0, A.mult, -1.0, A.add)
+        choose("OS", "XS")
+        ts(c32("SEL"), part("OS", 3), -1.0, A.mult, -1.0, A.add)
         for c in HALF:
             act(R("DB" if st == 1 else "DA", *c), IND(R("WAB", 0, 1024), R("SEL", c[0] // 16, c[1] // 16)))
         was = c32("CH%d" % ((st + 2) % 3))
-        ts(c32("T2"), c32("P6"), 0.0, A.is_gt, float(SIDE), A.mult)
+        ts(c32("T2"), dif, 0.0, A.is_gt, float(SIDE), A.mult)
         if st == 0:
             tt(c32("ST"), c32("T2"), was, A.add)
-            tt(c32("ST", 1), c32(ES), c32("P4"), A.add)
         else:
-            ts(c32("LV"), was, 1.0, A.is_ge)
-            ts(c32("LV", 1), was, 1.0, A.is_lt)
-            for k in range(2):
-                tt(c32("DS", k), c32("ST", k), c32("LV", 1), A.mult)
+            ts(c32("LV", st - 1), was, 1.0, A.is_lt)
+            tt(c32("DS"), c32("ST"), c32("LV", st - 1), A.mult)
             tt(c32("DT"), c32("DS"), was, A.add)
             tt(c32("ST"), c32("T2"), c32("DT"), A.add)
-            tt(c32("NS"), c32(ES), c32("P4"), A.add)
-            tt(c32("NS", 1), c32("NS"), c32("LV"), A.mult)
-            tt(c32("ST", 1), c32("NS", 1), c32("DS", 1), A.add)
+            if st == 2:
+                cp(c32("KEYU"), c32("ST"))
+                ts(c32("KI"), c32("ST"), -1.0, A.add)
+        if st == 2:
+            cp(c32("LW"), c32("LV"))
+            tt(c32("LW", 1), c32("LV", 1), c32("LV"), A.subtract)
+            ts(c32("LW", 2), was, 1.0, A.is_ge)
+            mm(c32("P3"), a128("I4"), c32("ONE"), True, False)
+            phases(c32("P3"), "ZM8", R("AB", 1536, 2048), False, True, 4)
+            tt(c32("NS", 2), c32("ES", 2), c32("P3"), A.add)
+            tt(a96("NW"), a96("NS"), a96("LW"), A.mult)
+            tt(c32("DS", 1), c32("NW"), c32("NW", 1), A.add)
+            tt(c32("ST", 1), c32("DS", 1), c32("NW", 2), A.add)
 
     BY_S, RELU = (1, 2, 3), (4, 5, 6, 7)
+
+    LISTS = (("P4", (1, 2, 3)), ("P1", (4, 5, 6, 7)))
 
     def send(k, to, what, late):
         dst = T.cores[(rank + 1) % n_ranks]
@@ -536,47 +631,43 @@ def rank_program(g, core, T, topo):
         for k in range(4):
             dma("Y", ap(R("LT4", LIB * k, LIB * k + n)), ap(R("YT", H, H + n)), [R("YT", H, H + n)], [R("LT4", LIB * k, LIB * k + n)])
         D = a512("DA")
-        SL = "SL%d" % t
-        cp(c32("KEYU"), c32("ST"))
+        SL, SLOT = "SL%d" % t, "SLOT%d" % t
         yc = act(a512("YC%d" % t), IND(R("ZAB", 0, SIDE + 2049), c32("KEYU")), F.Abs)
-        send(2 * t, a512("YIN%d" % t), a512("YC%d" % t), 8000.0)
-        ts(c32("KI"), c32("ST"), -1.0, A.add)
+        send(2 * t, a512("YIN%d" % t), a512("YC%d" % t), 6500.0 if t else 13500.0)
         ts(c32("QCI"), c32("KI"), 15, A.bitwise_and)
         ts(c32("QCI", 1), c32("KI"), 4, A.arith_shift_right)
         cp(c64("QCH"), c64("QCI"))
         hh, stride = c32("H16"), c32("H16", 1)
-        for P, some in (("P4", (0, 1)), ("P1", (2, 3, 4, 5, 6, 7))):
-            steps = [(m, W) for j, W in enumerate(("IB", "I2", "I4")) for m in some if m >> j & 1]
-            mms([(c32(P, m - some[0]), a128(W), stride, k == 0, False) for k, (m, W) in enumerate(steps)])
+        for P, some in LISTS:
+            mms([(c32(P, m - some[0]), I if m == 1 else a128("I%d" % m), stride, m == some[0], False) for m in some])
             mms([(c32(P, m - some[0]), I, hh, False, m == some[-1]) for m in some])
             cp(R("CU", 32 * some[0], 32 * some[-1] + 32), R(P, 0, 32 * len(some)))
         ts(a128(SL), a128("LLO"), col("Q2"), A.mult, col("QI"), A.add)
         LW = R("LT4", 0, 4 * LIB)
         df = lambda m, b="DF", n=1: R(b, 512 * m, 512 * (m + n))
         banks = {1: "P0", 2: "P1", 3: "P4"}
-        mms([(a512("P5"), a128("E2"), a512("LLO"), True, False), (a512("P5"), a128("E3"), a512("LHI"), False, False)])
-        to_row("P5", 0, c32("QCH"), False, False)
-        to_row("P5", 1, c32("QCH", 1), False, True)
-        act(a512("PAY"), a512("P5"), scale=1.0 / 256)
-        cut = {}
+        to_row("P7", 0, c32("QCH"), False, False)
+        to_row("P7", 1, c32("QCH", 1), False, True)
+        act(a512("PAY"), a512("P7"), scale=1.0 / 256)
+        got, size = {0: yc}, {}
         for m in range(8):
             if m in BY_S:
                 k = BY_S.index(m)
-                got = act(df(k, "GV"), IND(LW, c32("CU", m)))
-                if k == 1:
-                    chain(yc, got)
+                got[m] = act(df(k, "GV"), IND(LW, c32("CU", m)))
                 mm(a512(banks[m]), NI, D, True, False)
                 mm(a512(banks[m]), I, df(k, "GV"), False, True)
-                act(df(m), a512(banks[m]), F.Abs, scale=0.5)
+                size[m] = act(df(m), a512(banks[m]), F.Abs, scale=0.5)
             elif m in RELU:
-                got = tt(df(RELU.index(m), "DD"), IND(LW, c32("CU", m)), D, A.subtract)
-                if m - 2 in RELU:
-                    chain(cut[m - 2], got)
-                cut[m] = ts(df(m), df(RELU.index(m), "DD"), 0.0, A.max)
+                got[m] = tt(df(RELU.index(m), "DD"), IND(LW, c32("CU", m)), D, A.subtract)
+                size[m] = ts(df(m), df(RELU.index(m), "DD"), 0.0, A.max)
             else:
-                tt(df(m), IND(LW, c32("CU", m)), D, A.subtract)
-                act(df(m), df(m), F.Abs, scale=0.5)
-        for P, m, n in (("P2", 0, 2), ("P3", 4, 2), ("P7", 6, 2), ("P6", 2, 2)):
+                for c in HALF:
+                    tt(sub(df(m), *c), IND(LW, R("CU", c[0] // 16, c[1] // 16)), sub(D, *c), A.subtract)
+                size[m] = act(df(m), df(m), F.Abs, scale=0.5)
+        chain(yc, got[2])
+        chain(size[4], got[6])
+        chain(size[5], got[7])
+        for P, m, n in (("P2", 0, 2), ("P3", 4, 2), ("P5", 6, 2), ("P6", 2, 2)):
             mm(R(P, 0, 32 * n), I, R("MC", 32 * m, 32 * (m + n)), True, False)
             for k in range(0, n, 2):
                 if m + k in RELU:
@@ -584,18 +675,20 @@ def rank_program(g, core, T, topo):
                 mark["sums"] = phases(R(P, 32 * k, 32 * k + 64), "ZM16", df(m + k, "DF", 2), False, k == n - 2)
         act(c64("B1"), c64("P3"))
         tt(c64("B2"), c64("B1"), c64("P2"), A.min)
-        tt(c64("B3"), c64("B2"), c64("P7"), A.min)
+        tt(c64("B3"), c64("B2"), c64("P5"), A.min)
         tt(c64("B4"), c64("B3"), c64("P6"), A.min)
         tt(c32("BEST"), c32("B4"), c32("B4", 1), A.min)
         tt(c32("HIT"), c32("BEST"), c32("ST", 1), A.is_lt)
         emit("V", lambda: g.vector.tensor_tensor_scan(ap(c32("INC")), ap(c32("ONE")), ap(c32("HIT")), 0.0, A.mult, A.add),
-             [c32("ONE"), c32("HIT")], [c32("INC")], 64)
+             [c32("ONE"), c32("HIT")], [c32("INC")], vcost(c32("INC")))
         tt(c32("HL"), c32("HIT"), c32("NL512"), A.mult)
         mm(c32("P6"), I, c32("L512"), True, False)
         mm(c32("P6"), a128("LB"), c32("HIT"), False, False)
         mm(c32("P6"), a128("BD"), c32("INC"), False, False)
         mm(c32("P6"), I, c32("HL"), False, True)
-        cp(c32("SLOT"), c32("P6"))
+        cp(c32(SLOT), c32("P6"))
+        if t in BY_SLOT:
+            send(2 * t + 1, c32("LIN%d" % t), c32(SLOT), 3600.0)
         ts(c32("MI"), c32("BEST"), 7, A.bitwise_and)
         tt(c32("MTT"), c32("MI"), stride, A.mult)
         tt(c32("HD"), c32("MTT"), hh, A.add)
@@ -603,38 +696,39 @@ def rank_program(g, core, T, topo):
         dn = cp(c32("DNH"), c32("DNI"))
         to_row("P4", 0, c32("DNH"), True, True)
         act(a512("DR"), a512("P4"), scale=1.0 / 256)
-        chain(dn, cp(IND(R(SL, 0, 1536), c32("SLOT")), a512("PAY")))
+        chain(dn, cp(IND(R(SL, 0, 1536), c32(SLOT)), a512("PAY")))
 
     def grafts(t):
         at = lambda gr, w=128: (w * gr, w * gr + w)
         XH, LL = a128("SL%d" % t), R("LL%d" % t, 0, 8)
         for h in range(2):
             chain(mark["sums"], mms([(R("P%d" % h, *at(k)), a128("N256"), a128("TRI"), k == 0, False) for k in range(4)]))
-            mm(a128("P%d" % (2 + h)), I, a128("IQN"), True, False)
+        mm(a128("P2"), I, a128("IQN"), True, False)
         diff = lambda h: mms([(a512("P%d" % h), XH, R("NBC", *at(h, 512)), False, False)]
                              + [(R("P%d" % h, *at(k)), R("BC", *at(4 * h + k)), XH, False, k == 3) for k in range(4)])
-        chain(mm(R("P6", 0, 8), XH, R("SEL1", 0, 8), True, True),
-              phases(R("P7", 0, 8), "ZR2", XH, True, True),
-              diff(0),
-              diff(1))
+        lanes = lambda: phases(R("P7", 0, 8), "ZR2", XH, True, True)
+        column = lambda: mm(R("P6", 0, 8), XH, R("SEL1", 0, 8), True, True)
+        if t in BY_SLOT:
+            chain(column(), diff(0), lanes(), diff(1))
+        else:
+            chain(lanes(), column(), diff(0), diff(1))
+        cp(LL, R("P7", 0, 8))
+        if t not in BY_SLOT:
+            send(2 * t + 1, R("LIN%d" % t, 0, 8), LL, 3600.0)
         ts(R("XF", 0, 8), R("P6", 0, 8), -MID, A.add)
-        ll = cp(LL, R("P7", 0, 8))
-        send(2 * t + 1, R("LIN%d" % t, 0, 8), LL, 2500.0)
-        act(a128("DG"), IND(R("DR", 0, 640), LL), scale=-1.0, bias=col("CMID"))
+        mark["donors"] = act(a128("DG"), IND(R("DR", 0, 640), LL), scale=-1.0, bias=col("CMID"))
         mm(a128("P4"), a128("DG"), a128("RQ"), True, True)
         mms([(R("P6", *at(k)), I, a128("ONE"), k == 0, False) for k in range(2)])
-        for h in range(2):
-            P, Q, z = "P%d" % h, "P%d" % (2 + h), 896 + 1024 * h
-            mm(a128(Q), XH, a128("RQ"), False, False)
-            chain(ll, ts(R("EQ", *at(h, 512)), a512(P), 0.0, A.is_equal))
-            mms([(R(Q, gr, 128, 8), R("EQ", *at(gr)), R("S16", 0, 16), False, gr % 4 == 3) for gr in range(4 * h, 4 * h + 4)])
-            ts(R("WN", z, z + 128), a128(Q), 0.0, A.is_equal, -1.0, A.mult)
-            tt(R("WZ", z, z + 128), R("WN", z, z + 128), a128("P4"), A.mult)
-            for gr in range(4 * h, 4 * h + 4):
-                ts(R("CHM", *at(gr, 256)), a256("IOC"), col("XF", gr), A.is_equal)
-                o = z - 127 * gr
-                mm(a256("P6"), R("WN", o, o + 1017, 8), R("CHM", *at(gr, 256)), False, gr == 7)
-                mm(a256("P5"), R("WZ", o, o + 1017, 8), R("CHM", *at(gr, 256)), gr == 0, gr == 7)
+        mm(a128("P2"), XH, a128("RQ"), False, True)
+        ts(R("WN", 896, 1024), a128("P2"), 0.0, A.is_equal, -1.0, A.mult)
+        tt(R("WZ", 896, 1024), R("WN", 896, 1024), a128("P4"), A.mult)
+        for gr in range(8):
+            P, near = R("P%d" % (gr // 4), *at(gr % 4)), col("XF", 8 + gr)
+            emit("V", lambda P=P, near=near: g.vector.tensor_reduce(ap(near), ap(P), AX.X, A.min, apply_absolute_value=True), [P], [near], vcost(P, P))
+            ts(R("CHM", *at(gr, 256)), a256("IOC"), col("XF", gr), A.is_equal, near, A.min)
+            o = 896 - 127 * gr
+            mm(a256("P6"), R("WN", o, o + 1017, 8), R("CHM", *at(gr, 256)), False, gr == 7)
+            mm(a256("P5"), R("WZ", o, o + 1017, 8), R("CHM", *at(gr, 256)), gr == 0, gr == 7)
         for c in ((0, 160), (160, 256)):
             tt(R("ZT", *c), R("WF", *c), R("P6", *c), A.mult)
             tt(R("WF", *c), R("ZT", *c), R("P5", *c), A.add)
@@ -642,10 +736,21 @@ def rank_program(g, core, T, topo):
 
     def receive(t):
         n = len(topo.engines(T.cores[(rank - 1) % n_ranks], core))
-        Y, L = R("YIN%d" % t, 0, 640), R("LIN%d" % t, 0, 8)
-        for k, r in ((2 * t, a512(Y[0])), (2 * t + 1, L)):
-            emit("S", lambda k=k: g.scalar.wait_ge(T.sem["arr%d" % k], n), [R("sent", k, k + 1), a128("DG")], [r], 1.0, False)
-        act(R("YT", H + 128 * t, H + 128 * t + 128), IND(Y, L))
+        Y, L, W, lib = a512("YIN%d" % t), c32("LIN%d" % t), R("YW", 0, 1536), R("YT", H + 128 * t, H + 128 * t + 128)
+        if t not in BY_SLOT:
+            L = R("LIN%d" % t, 0, 8)
+            act(R(Y[0], 512, 640), lib, also=[a512("PAY")])
+            for k, r in ((2 * t, Y), (2 * t + 1, L)):
+                emit("S", lambda k=k: g.scalar.wait_ge(T.sem["arr%d" % k], n), [R("sent", k, k + 1), a128("DG")], [r], 1.0, False)
+            return act(lib, IND(R(Y[0], 0, 640), L))
+        act(a128("YL"), lib, bias=col("CUP"))
+        calls[act(a128("YW"), a128("YL"), F.Silu, also=[R("LL0", 0, 8)])]["cost"] += TABLE
+        for k, r in ((2 * t, Y), (2 * t + 1, L)):
+            emit("S", lambda k=k: g.scalar.wait_ge(T.sem["arr%d" % k], n), [R("sent", k, k + 1), a128("DG") if r == L else a512("PAY")], [r], 1.0, False)
+            if r == Y:
+                chain(act(a512("YF"), Y, bias=col("CUP")), mark["donors"])
+        emit("S", lambda: g.scalar.activation(ap(IND(W, L)), ap(a512("YF")), F.Silu), [a512("YF"), L], [W], 65 + SCATTER * 512)
+        ts(lib, a128("YW"), ROUND, A.add, -ROUND - UP, A.add)
 
     def out(lo, hi, src):
         dma("Y", T.yo[:, lo:hi], ap(src), [src], [])
@@ -661,8 +766,7 @@ def rank_program(g, core, T, topo):
         dma("Y", T.ko[:, :], ap(a256("KOT")), [a256("KOT")], [])
         for l in range(3):
             level(l, yt(l), False)
-            act(a512("YR"), yt(l), F.Relu, scale=-1.0, bias=col("C255"))
-            act(yo(l), a512("YR"), scale=-1.0, bias=col("C255"))
+            ts(yo(l), yt(l), 255.0, A.min)
             out(1536 + 512 * l, 2048 + 512 * l, yo(l))
         level(3, yo(3), True)
         for a, b in HALF:

from concourse.mybir import AluOpType as A, ActivationFunctionType as F, AxisListType as AX

H = 16
LIB = 1024
BY_SLOT = (1,)
UP = 32.0
ROUND = 1.5 * 2 ** 23
MID = 1792.0
BIG = 2.0 ** 23
SIDE = 2064

SCRATCH, PLACE = {}, {}


def declare(dtype, text, packed=False):
    o = 0
    for item in text.split():
        name, w = item.split(":")
        if packed:
            PLACE[name] = ("SM" + dtype, o)
            o += (int(w) + 15) // 16 * 16
        else:
            SCRATCH[name] = ("sbuf", [128, int(w)], dtype)
    if packed:
        SCRATCH["SM" + dtype] = ("sbuf", [128, o], dtype)


declare("bfloat16", "YT:3616 ZAB:4128 SG:2064 NT:2064 TG:512 WAB:1024 DA:512 DB:512 Y2:1024 ZB:512 MN:1024 UU:512 CB:512 SA:512 AB:2048 DF:4096 DD:2048 "
        "GV:2048 RAW:2048 LT4:4096 YO:2048 YR:512 YC0:512 YC1:512 YIN0:640 YIN1:512 PAY:512 SL0:1536 SL1:1536 LLO:512 LHI:512 "
        "O256:512 BQ:2048 KQ:2064 BC:1024 NBC:1024")
declare("bfloat16", "HIT:32 INC:32 ONE:160 JB:160 NI:128 N256:128 I2:128 I3:128 I4:128 I255:128 I5:128 I6:128 I7:128 BD:128 BD1:128 L00:128 L01:128 L10:128 L11:128 "
        "SGB:128 LB:128 LT:128 TRI:128 MC:256 ZM:144 ZM8:144 ZN8:144 ZM16:144 ZMN:144 ZW1:144 ZW2:144 ZAD:144 ZR2:144 SEL1:16 RQ:128 "
        "IQN:128 E2:128 E3:128 ZMK:144 C4:128 KQ1:128", True)
declare("float16", "KLF:256 KLH:256 WF:256 NXF:256 KTG:1024 CHM:2048 WZ:1920 WN:1920 ZT:256")
declare("float16", "QCH:64 DNH:32 IOC:256 L512:32 HL:32 DG:128 H16:64", True)
declare("uint16", "UL:256 SEL:32 NK:64 NL:32 KEYU:32 CU:256 SLOT0:32 SLOT1:32 LL0:8 LL1:8 LIN0:32 LIN1:32")
declare("int32", "KLD:256 MLD:128 WTI:2")
declare("float32", "YF:512 YL:128 YW:1536 KT:1552 DR:640 KOF:256 KOT:256 WTF:2")
declare("float32", "XN:128 XH:256 XS:128 ON:128 OH:256 OS:128 T2:32 UA:64 UN:64 ES:96 Q0:32 Q1:32 Q2:32 Q3:32 QD:8 QL:8 QE:8 QI:8 UH:8 S1:32 CH0:32 CH1:32 CH2:32 ST:64 NS:96 NW:96 LW:96 "
        "DS:64 DT:64 LV:64 B1:64 B2:64 B3:64 B4:64 XF:16 LANE:32 NL512:32 IOF:256 C255:8 CNX:8 "
        "CMID:8 CUP:8", True)
declare("int32", "U16:8 KA:96 UI:128 PRI:64 SHI:64 UMI:64 BEST:32 MI:32 MTT:32 HD:32 DNI:32 KI:32 QCI:64 LI0:32 LI1:32 LI2:32", True)
for _k in range(8):
    SCRATCH["P%d" % _k] = ("psum", [128, 512], "float32")

SEMAPHORES = ["cV", "cS", "cP", "cG", "arr0", "arr1", "arr2", "arr3", "snt0", "snt1", "snt2", "snt3"] + ["d%d" % k for k in range(27)]

GATHER, SCATTER, PE, CYCLE, WAKE, WAKE_SAME = 1.1, 2.5, 0.42, 0.83, 215.0, 240.0
TABLE = 1400.0
PASSES, SHORT, LEAD = 4, 72, 1000.0
SWEEPS, TRIES = ((100, 400.0), (70, 300.0), (50, 250.0), (80, 300.0), (60, 200.0), (90, 200.0), (56, 150.0)), 2500
PACES = ((1.0, 1.0, 1.0, 0.8), (1.45, 2.1, 0.9, 1.0), (1.2, 1.3, 1.5, 1.2))
ORDER = []


def arrange(calls):
    n = len(calls)
    cost = [c["cost"] for c in calls]
    after, before = [[] for _ in range(n)], [[] for _ in range(n)]
    for k, c in enumerate(calls):
        for d, by_sem in c["deps"].items():
            gap = calls[d]["late"] * (by_sem is not None) + ((WAKE_SAME if calls[d]["q"] == c["q"] else WAKE) if by_sem else 0.0)
            after[d].append((k, gap))
            before[k].append((d, gap))

    def run(users, makers, way, ready):
        left = [len(m) for m in makers]
        pool, free, order, end = {}, {}, [], [0.0] * n
        for k in range(n):
            free[calls[k]["q"]] = 0.0
            if not left[k]:
                pool.setdefault(calls[k]["q"], []).append(k)
        while len(order) < n:
            now, q = min((max(free[q], min(ready[k] for k in p)), q) for q, p in pool.items() if p)
            for k in sorted((k for k in pool[q] if ready[k] <= now), key=lambda k: (-way[k], k)):
                if not any(now < ready[y] < now + cost[k] and max(ready[y] + way[y], ready[y] + cost[y] + way[k]) < max(now + way[k], now + cost[k] + way[y])
                           for y in pool[q]):
                    break
            else:
                k = min((y for y in pool[q] if ready[y] > now), key=lambda y: (ready[y], -way[y]))
                now = ready[k]
            pool[q].remove(k)
            order.append(k)
            end[k] = free[q] = now + cost[k]
            for u, gap in users[k]:
                ready[u] = max(ready[u], end[k] + gap)
                left[u] -= 1
                if not left[u]:
                    pool.setdefault(calls[u]["q"], []).append(u)
        return order, end

    way = [0.0] * n
    for k in reversed(range(n)):
        way[k] = cost[k] + max([gap + way[u] for u, gap in after[k]], default=calls[k]["late"])
    lead = [LEAD if c["cost"] <= SHORT and c["q"] in "PV" and any(calls[u]["q"] != c["q"] for u, gap in after[k]) else 0.0 for k, c in enumerate(calls)]
    best = None
    for _ in range(PASSES):
        order, end = run(after, before, [w + x for w, x in zip(way, lead)], [0.0] * n)
        total = max(e + c["late"] for e, c in zip(end, calls))
        if best is None or total < best[0]:
            best = (total, order)
        way = run(before, after, end, [c["late"] for c in calls])[1]
    return polish(calls, best[1])


def polish(calls, order):
    n = len(calls)
    qof = ["VSPGY".index(c["q"]) for c in calls]
    paces = []
    for plain, indexed, wake, far in PACES:
        late = [c["late"] * far for c in calls]
        before, after = [[] for _ in range(n)], [[] for _ in range(n)]
        for k, c in enumerate(calls):
            for d, by_sem in c["deps"].items():
                gap = late[d] * (by_sem is not None) + ((WAKE_SAME if qof[d] == qof[k] else WAKE) * wake if by_sem else 0.0)
                before[k].append((d, gap))
                after[d].append((k, gap))
        paces.append(([c["cost"] * (indexed if c["indexed"] else plain) for c in calls], late, before, after, [0.0] * n))
    links = [[[u for u, gap in x] for x in paces[0][j]] for j in (2, 3)]
    seq, x = list(order), [1]

    def draw(m):
        x[0] = (x[0] * 1103515245 + 12345) % 2147483648
        return (x[0] >> 8) % m

    def times(ks, free, cost, before, end):
        for k in ks:
            s = free[qof[k]]
            for d, gap in before[k]:
                if end[d] + gap > s:
                    s = end[d] + gap
            end[k] = free[qof[k]] = s + cost[k]

    for lo, size, heat in [(lo, size, heat) for size, heat in SWEEPS for lo in range(0, n - 1, size // 2)]:
        given = []
        for j, (cost, late, before, after, end) in enumerate(paces):
            times(seq, [0.0] * 5, cost, before, end)
            if j == 0:
                seq.sort(key=lambda k: end[k] - cost[k])
                win = seq[lo:lo + size]
            tail, head, free = {}, [0.0] * 5, [0.0] * 5
            for k in reversed(seq[lo + size:]):
                tail[k] = head[qof[k]] = cost[k] + max([late[k], head[qof[k]]] + [gap + tail[u] for u, gap in after[k]])
            for k in seq[:lo]:
                free[qof[k]] = end[k]
            out = {k: max([late[k]] + [gap + tail[u] for u, gap in after[k] if u in tail]) for k in win}
            given.append((cost, before, end, head, out, free, 1e5 / max(end)))

        def score(ks, a):
            total = 0.0
            for cost, before, end, head, out, free, w in given:
                free = free[:]
                for k in ks[:a]:
                    free[qof[k]] = end[k]
                times(ks[a:], free, cost, before, end)
                far = [end[k] + out[k] for k in ks]
                total += w * (max(max(far), max(f + h for f, h in zip(free, head))) + 5e-4 * sum(far))
            return total

        def longest(ks):
            path = []
            for cost, before, end, head, out, free, w in given:
                prev, last = {}, {}
                for k in ks:
                    prev[k], last[qof[k]] = last.get(qof[k]), k
                k = max([(end[k] + out[k], k) for k in ks] + [(end[k] + head[q], k) for q, k in last.items()])[1]
                while k in prev:
                    path.append(k)
                    k = max([(end[d] + gap, d) for d, gap in before[k]] + [(end[prev[k]] if prev[k] is not None else free[qof[k]], prev[k])],
                            key=lambda e: e[0])[1]
            return path

        now, clean = score(win, 0), len(win)
        best, path = (now, win), longest(win)
        for it in range(TRIES):
            y = path[draw(len(path))]
            i = win.index(y)
            way = -1 if draw(2) else 1
            if way > 0:
                while i > 0 and (win[i] == y or qof[win[i]] != qof[y]):
                    i -= 1
                y = win[i]
            j, m = i, 1 + draw(2 << draw(4))
            while 0 <= j + way < len(win) and m:
                j += way
                m -= qof[win[j]] == qof[y]
            a, b = min(i, j), max(i, j) + 1
            need = {y}
            for k in win[a:b][::way]:
                if k in need:
                    need.update(links[way > 0][k])
            new = win[:a] + sorted(win[a:b], key=lambda k: (k in need) != (way < 0)) + win[b:]
            if new != win:
                s, clean = score(new, min(a, clean)), a
                if s < now + heat * (1 - it / TRIES) * (draw(1024) / 1024) ** 2:
                    win, now, path, clean = new, s, longest(new), len(win)
                    best = min(best, (s, new))
        seq[lo:lo + size] = best[1]
    return seq


def rank_program(g, core, T, topo):
    rank = T.rank_of(core)
    if rank is None:
        return
    n_ranks = len(T.cores)
    ENG = {"V": g.vector, "S": g.scalar, "P": g.tensor, "G": g, "Y": g.sync}
    calls = []
    acc = {}
    dmas = [0]
    mark = {}

    def ap(r):
        if r[0] == "ind":
            return ap(r[1]).indirect(ap(r[2]))
        b, lo, hi, st = r
        if b in PLACE:
            b, o = PLACE[b]
            lo, hi = lo + o, hi + o
        return T[b][:, lo:hi] if st == 1 else T[b][:, lo:hi:st]

    def R(b, lo, hi, st=1):
        return (b, lo, hi, st)

    def sub(r, a, b):
        return R(r[0], r[1] + a, r[1] + b)

    def is_psum(b):
        return b[0] == "P" and len(b) == 2

    def emit(q, fn, reads, writes, cost, sem=None, late=0.0):
        me, deps = len(calls), {}
        for rs, w in ((reads, False), (writes, True)):
            for (b, lo, hi, st) in rs:
                ps = is_psum(b)
                if ps:
                    lo, hi = 0, 512
                for (k, lo2, hi2, w2, st2) in acc.get(b, ()):
                    same = calls[k]["q"] == q
                    if lo2 >= hi or hi2 <= lo or not (w or w2 or (ps and not same)):
                        continue
                    if same and not ps and st == st2 and (lo - lo2) % st:
                        continue
                    deps[k] = calls[k]["sem"] is not None and not (same and q == "P")
        for rs, w in ((writes, True), (reads, False)):
            for (b, lo, hi, st) in rs:
                ps = is_psum(b)
                if ps:
                    lo, hi = 0, 512
                L = acc.setdefault(b, [])
                if w and (st == 1 or ps):
                    L[:] = [e for e in L if not (lo <= e[1] and e[2] <= hi)]
                elif ps:
                    L[:] = [e for e in L if e[3] or e[0] == me or calls[e[0]]["q"] == q]
                L.append((me, lo, hi, w, st))
        calls.append(dict(q=q, fns=fn if isinstance(fn, list) else [fn], deps=deps, cost=cost, late=late,
                          indexed=q in "VS" and any(SCRATCH.get(r[0], "...")[2] == "uint16" for r in reads), sem="c" + q if sem is None else sem or None))
        return me

    def chain(*ks):
        for a, b in zip(ks, ks[1:]):
            calls[b]["deps"].setdefault(a, None)

    def dma(q, out, in_, reads, writes):
        dmas[0] += 1
        r = (writes or reads)[0]
        size = width(r) * (2 if narrow(r) else 4)
        emit(q, lambda: ENG[q].dma_start(out, in_), reads, writes, 60.0, "d%d" % (dmas[0] - 1), 1600.0 + 0.6 * size)

    def width(r):
        return 16 * width(r[2]) if r[0] == "ind" else -(-(r[2] - r[1]) // r[3])

    def narrow(*rs):
        return all(not is_psum(r[0]) and SCRATCH[PLACE.get(r[0], r)[0]][2][-2:] == "16" for r in rs)

    def vcost(out, *ins):
        if out[0] == "ind":
            return 50 + SCATTER * width(out)
        if any(r[0] == "ind" for r in ins):
            return 50 + GATHER * width(out)
        if len(ins) == 2 and not any(is_psum(r[0]) for r in ins):
            return 10 + CYCLE * max(64, 2 * width(out))
        return 10 + CYCLE * max(64, width(out) * (0.5 if narrow(out, *ins) else 1.0))

    def IND(win, off):
        return ("ind", win, off)

    def rd(*xs):
        r = []
        for x in xs:
            if isinstance(x, tuple):
                r += [x[1], x[2]] if x[0] == "ind" else [x]
        return r

    def num(x):
        return ap(x) if isinstance(x, tuple) else x

    def tt(out, a, b, op):
        return emit("V", lambda: g.vector.tensor_tensor(ap(out), ap(a), ap(b), op), rd(a, b), [out], vcost(out, a, b))

    def ts(out, a, s1, op0, s2=None, op1=None):
        if op1 is None:
            return emit("V", lambda: g.vector.tensor_scalar(ap(out), ap(a), num(s1), None, op0), rd(a, s1), [out], vcost(out, a))
        return emit("V", lambda: g.vector.tensor_scalar(ap(out), ap(a), num(s1), num(s2), op0, op1), rd(a, s1, s2), [out], vcost(out, a))

    def cp(out, a):
        if out[0] == "ind":
            return emit("V", lambda: g.vector.tensor_copy(ap(out), ap(a)), rd(a) + [out[2]], [out[1]], vcost(out, a))
        return emit("V", lambda: g.vector.tensor_copy(ap(out), ap(a)), rd(a), [out], vcost(out, a))

    def ms(out, v):
        emit("V", lambda: g.vector.memset(ap(out), v), [], [out], vcost(out))

    def vtr(out, a):
        emit("V", lambda: g.vector.transpose(ap(out), ap(a)), [a], [out], vcost(out, a))

    def act(out, a, func=F.Identity, scale=1.0, bias=0.0, also=()):
        return emit("S", lambda: g.scalar.activation(ap(out), ap(a), func, bias=num(bias), scale=num(scale)), rd(a, scale, bias, *also), [out],
                    65 + width(out) * GATHER if a[0] == "ind" else 90 + width(out) * CYCLE)

    def mms(items):
        return emit("P", [lambda x=x: g.tensor.matmul(ap(x[0]), ap(x[1]), ap(x[2]), x[3], x[4]) for x in items], [r for x in items for r in x[1:3]],
                    [x[0] for x in items], sum(PE * max(min(64, width(x[1])), width(x[2])) for x in items))

    def mm(*x):
        return mms([x])

    def iota(out, pat, base, chm, small=True):
        if small:
            emit("G", lambda: g.iota(ap(out), pat, base, chm, allow_small_or_imprecise_dtypes=True), [], [out], 170 + 2.2 * width(out))
        else:
            emit("G", lambda: g.iota(ap(out), pat, base, chm), [], [out], 170 + 2.2 * width(out))

    def asel(out, in_, pat, op, base, chm):
        emit("G", lambda: g.affine_select(ap(out), ap(in_), pat, op, 0.0, base, chm), [in_], [out], 220 + 2.2 * width(out))

    def phases(out, Z, src, first, last, by=16):
        for j in range(0, 16, by):
            k = mms([(out, R(Z, 15 - q, 143 - q), R(src[0], src[1] + q, src[2], 16), first and q == 0, last and q == 15) for q in range(j, j + by)])
        return k

    def to_row(P, r, src, first, last):
        for j in range(0, 16, 4):
            mms([(R(P, q, 512, 16), R("KQ", 16 + 128 * q - r, 144 + 128 * q - r), src, first and q == 0, last and q == 15) for q in range(j, j + 4)])

    a128 = lambda b: R(b, 0, 128)
    a256 = lambda b: R(b, 0, 256)
    a512 = lambda b: R(b, 0, 512)
    c32 = lambda b, k=0: R(b, 32 * k, 32 * k + 32)
    c64 = lambda b: R(b, 0, 64)
    col = lambda b, k=0: R(b, k, k + 1)
    HALF = ((0, 256), (256, 512))
    I, NI = R("JB", 16, 144), a128("NI")

    dma("S", ap(a256("KLD")), T.kid[:, :], [], [a256("KLD")])
    dma("Y", ap(a128("MLD")), T.mx[:, :], [], [a128("MLD")])
    dma("Y", ap(R("YT", H, H + 1536)), T.lv[:, :], [], [R("YT", H, H + 1536)])
    dma("Y", ap(a512("TG")), T.tg[:, :], [], [a512("TG")])
    dma("Y", ap(R("WTI", 0, 2)), T.wt[:, :], [], [R("WTI", 0, 2)])
    chain(1, 2, 3, 4)

    O256 = a512("O256")
    ms(R("ONE", 0, 160), 1.0)
    ms(O256, 256.0)
    for r in (R("YT", 0, H), R("KQ", 0, 1024), R("KQ", 1024, 2064), R("ZM", 0, 144), R("ZAB", 0, 1), R("ZAB", 2049, SIDE + 1), R("NT", 0, 1),
              R("DR", 512, 640)):
        ms(r, 0.0)
    ms(R("KT", 0, 513), 1.0)
    for b, v in (("C255", 255.0), ("CMID", MID), ("CUP", UP)):
        iota(R(b, 0, 8), [[0, 8]], int(v), 0)
    asel(R("JB", 0, 160), R("ONE", 0, 160), [[-1, 160]], A.is_equal, 16, 1)
    iota(c32("LI1"), [[0, 32]], 0, 1, False)
    ts(col("U16"), col("LI1"), 16, A.bitwise_and)
    for u in range(2):
        ts(col("UH", u), col("U16"), 16.0 * u, A.is_equal)
        for v in range(2):
            ts(a128("L%d%d" % (u, v)), R("JB", 16 * (1 + u - v), 16 * (9 + u - v)), col("UH", u), A.mult)
    for j in range(4):
        asel(R("BQ", 512 * j, 512 * j + 512), O256, [[-1, 4], [-16, 8], [0, 16]], A.is_equal, -4 * j, 1)
    asel(a128("KQ1"), a128("O256"), [[-1, 16], [-16, 8]], A.is_equal, 0, 1)
    cp(R("KQ", 16, 2064, 16), a128("KQ1"))
    asel(a128("BD1"), a128("ONE"), [[-16, 8], [0, 16]], A.is_ge, 0, 1)
    asel(a128("BD"), a128("BD1"), [[16, 8], [0, 16]], A.is_ge, 15, -1)
    iota(c32("LI0"), [[16, 32]], 0, 0, False)
    asel(a128("LT"), a128("BD"), [[1, 128]], A.is_gt, 0, -1)
    iota(a256("MC"), [[1, 8], [0, 32]], 0, 0)
    iota(a128("IQN"), [[-1, 16], [0, 8]], 0, 0)
    iota(a512("LLO"), [[0, 4], [1, 128]], 0, 0)
    iota(a512("LHI"), [[1, 4], [0, 128]], 0, 0)
    iota(a256("IOF"), [[SIDE // 16, 2], [1, 128]], -int(MID), 0)
    asel(a128("TRI"), a128("O256"), [[1, 128]], A.is_ge, 0, -1)
    asel(R("SEL1", 0, 8), R("ONE", 0, 8), [[-16, 8]], A.is_equal, -1, 1)
    asel(a128("RQ"), a128("ONE"), [[0, 16], [-16, 8]], A.is_equal, 0, 1)
    iota(R("NBC", 0, 1024), [[-240, 8], [0, 128]], 1, 15)
    asel(R("BC", 0, 1024), R("NBC", 0, 1024), [[16, 8], [0, 128]], A.is_ge, 1, -1)
    for j in range(2):
        act(R("BC", 512 * j, 512 * j + 512), R("BC", 512 * j, 512 * j + 512), F.Relu)
        act(R("NBC", 512 * j, 512 * j + 512), R("BC", 512 * j, 512 * j + 512), scale=-1.0)
    for lo in (0, 448):
        act(R("WZ", lo, lo + 448), R("O256", 0, 448), scale=0.0)
    for b, lo in (("WZ", 1024), ("WN", 0), ("WN", 1024)):
        dma("Y", ap(R(b, lo, lo + 896)), ap(R("WZ", 0, 896)), [R("WZ", 0, 896), R("YT", H, H + 1)], [R(b, lo, lo + 896)])
    for b, w in (("NI", -1.0), ("N256", -256.0), ("I255", 255.0 / 256), *[("I%d" % m, float(m)) for m in range(2, 8)]):
        ts(a128(b), I, w, A.mult)
    ts(c32("LI2"), c32("LI1"), 15, A.bitwise_and)
    for k in range(4):
        ts(c32("Q%d" % k), c32("LI2"), float(k), A.is_equal)
    ts(col("QD"), col("Q1"), 2048.0, A.mult, col("Q0"), A.add)
    for k in (2, 3):
        ts(a128("E%d" % k), I, col("Q%d" % k), A.mult, 256.0, A.mult)
    ts(col("QL"), col("Q3"), 128.0, A.mult, col("Q2"), A.add)
    ts(col("QE"), col("LI2"), 2.0, A.is_lt, -4096.0, A.mult)
    ts(col("QI"), col("Q3"), 4.0, A.mult, col("QE"), A.add)
    cp(R("WTF", 0, 2), R("WTI", 0, 2))
    cp(R("ZM", 15, 128, 16), R("BD", 0, 128, 16))
    for Z, w in (("ZAD", col("QD")), ("ZR2", col("QL")), ("ZMN", -BIG), ("ZMK", BIG), ("ZM8", 8.0), ("ZN8", -8.0), ("ZM16", 16.0),
                 ("ZW1", col("WTF", 0)), ("ZW2", col("WTF", 1))):
        ts(R(Z, 0, 144), R("ZM", 0, 144), w, A.mult)
    tt(c32("LANE"), c32("LI2"), c32("LI0"), A.add)
    ts(c32("CH2"), c32("LANE"), 1537.0, A.add)
    ts(c32("L512"), c32("LANE"), 512.0, A.add)
    ts(c32("NL512"), c32("LANE"), -1.0, A.mult, -512.0, A.add)
    for b in ("XH", "XS"):
        iota(R(b, 0, 96), [[0, 96]], 1, 0)
    ts(R("XS", 1, 96, 3), c32("LANE"), 513.0, A.add)
    ts(R("XS", 2, 96, 3), c32("LANE"), -1.0, A.mult, -1.0, A.add)
    iota(R("C4", 0, 96), [[0, 96]], -1, 0)
    ms(R("C4", 1, 96, 3), -BIG / 2)
    tt(a128("LB"), a128("LT"), a128("BD"), A.subtract)
    act(a256("IOC"), a256("IOF"))

    def load_lists():
        for j in range(2):
            c = (128 * j, 128 * j + 128)
            ts(R("KLF", *c), R("KLD", *c), -MID, A.add)
            vtr(R("KLH", *c), R("KLF", *c))
        for j in range(2):
            mms([(R("P%d" % j, 16 * i + c2, 16 * i + 16, 2), a128("L%d%d" % (c2, x)), R("KLH", 16 * x + 8 * j + i, 256, 32), x == 0, x == 1)
                 for i in range(2) for c2 in range(2) for x in range(2)])
            ts(R("UL", 128 * j, 128 * j + 32), c32("P%d" % j), MID + H, A.add)
        for j in range(2):
            mms([(R("P7", 2 * k + c2, 256, 16), a128("L%d%d" % (c2, x)), R("KLH", 32 * k + 16 * x, 32 * k + 16 * x + 16), x == 0, x == 1)
                 for k in range(4 * j, 4 * j + 4) for c2 in range(2) for x in range(2)])
        for c in ((32, 128), (160, 256)):
            ts(R("UL", *c), R("P7", *c), MID + H, A.add)
        act(a256("WF"), a256("P7"))
        ts(a128("SGB"), a128("MLD"), 2.0, A.mult, -1.0, A.add)
        for l in range(4):
            P = "P%d" % (2 + l)
            for r in range(4):
                mm(R(P, 128 * r, 128 * r + 128), R("BQ", 512 * l + 128 * r, 512 * l + 128 * r + 128), a128("SGB"), True, True)
            act(R("SG", 1 + 512 * l, 513 + 512 * l), a512(P), scale=1.0 / 256)
            ts(R("NT", 1 + 512 * l, 513 + 512 * l), R("SG", 1 + 512 * l, 513 + 512 * l), 0.0, A.is_lt)

    def lists():
        ts(a256("NXF"), a256("WF"), MID - 1534.0, A.add, 1.0, A.max)
        for l in (1, 2):
            P = "P%d" % (5 + l)
            for k in range(2):
                to_row(P, k, R("NXF", 128 * k + 32 * l, 128 * k + 32 * l + 32), k == 0, k == 1)
            act(R("KT", 1 + 512 * l, 513 + 512 * l), a512(P), scale=1.0 / 256)

    ul = lambda k, l, a, b: R("UL", 128 * k + 32 * l + a // 16, 128 * k + 32 * l + b // 16)
    below = lambda l: R("YT", 0, H + 1536 + 512 * l)
    tab = lambda b, o, l: R(b, o + 1 + 512 * l, o + 513 + 512 * l)
    yt = lambda l: R("YT", H + 1536 + 512 * l, H + 2048 + 512 * l)

    def level(l, out, cut, tables=False):
        za, yb, mn = tab("ZAB", 0, l), tab("ZAB", SIDE, l), R("MN", 512 * (l % 2), 0)
        if tables and l:
            za, yb = R("RAW", 1024 * (l % 2), 1024 * (l % 2) + 512), R("RAW", 1024 * (l % 2) + 512, 1024 * (l % 2) + 1024)
        for h, c in enumerate(HALF if out else HALF):
            tt(sub(za, *c), IND(below(l), ul(0, l, *c)), sub(tab("SG", 0, l), *c), A.mult)
            if tables and l:
                act(sub(yb, *c), IND(below(l), ul(1, l, *c)), F.Relu, scale=-1.0, bias=col("C255"))
                if l == 3:
                    act(sub(tab("ZAB", SIDE, l), *c), sub(yb, *c), scale=-1.0, bias=col("C255"))
            else:
                act(sub(yb, *c), IND(below(l), ul(1, l, *c)))
            ts(sub(mn, *c), sub(za, *c), 0.0, A.min, -255.0, A.max)
            if out:
                P = R("P%d" % (2 * (l % 2) + h), 0, c[1] - c[0])
                if tables and l:
                    mm(P, a128("I255"), R("O256", *c), True, False)
                mm(P, NI if tables and l else I, sub(yb, *c), not (tables and l), False)
                mm(P, NI, sub(mn, *c), False, True)
                tt(R("UU", *c) if cut else sub(out, *c), P, sub(za, *c), A.max)
                if cut:
                    ts(sub(out, *c), R("UU", *c), 255.0, A.min)
        if tables and l:
            for c in HALF if l == 3 else ((0, 512),):
                ts(sub(tab("ZAB", 0, l), *c), sub(za, *c), 255.0, A.min, -255.0, A.max)
                if l < 3:
                    act(sub(tab("ZAB", SIDE, l), *c), sub(yb, *c), scale=-1.0, bias=col("C255"))

    def levels():
        lists()
        for l in range(4):
            level(l, yt(l) if l < 3 else None, False, True)

    part = lambda b, j, k=0: R(b, 96 * k + j - 1, 96 * k + 96, 3)
    a96 = lambda b: R(b, 0, 96)

    def offer(X, a, b, k=0, neg=None):
        tt(part(X, 1, k), b, a, A.subtract)
        tt(part(X, 2, k), b, a, A.max)
        if neg:
            return tt(part(X, 3, k), neg[0], neg[1], A.max)
        tt(c32("S1"), b, a, A.min)
        ts(part(X, 3, k), c32("S1"), -1.0, A.mult)

    def choose(out, X, k=0):
        o, x = R(out, 96 * k, 96 * k + 96), R(X, 96 * k, 96 * k + 96)
        emit("V", lambda: g.vector.tensor_tensor_scan(ap(o), ap(a96("P6")), ap(x), -1.0, A.mult, A.min), [a96("P6"), x], [o], vcost(o, a96("P6")))

    def step(st):
        ab, zb = R("AB", 512 * (st + 1), 0), a512("ZB")
        if st == 0:
            D, mn, za, yb = a512("TG"), R("MN", 512, 1024), tab("ZAB", 0, 3), tab("ZAB", SIDE, 3)
            mm(a512("P6"), I, tab("NT", 0, 3), True, True)
            for c in HALF:
                tt(sub(zb, *c), sub(yb, *c), R("P6", *c), A.mult)
        else:
            D, mn, za, yb = a512("DA" if st == 1 else "DB"), a512("MN"), a512("Y2"), R("Y2", 512, 1024)
            for c in HALF:
                nl = R("NL", c[0] // 16, c[1] // 16)
                cp(sub(za, *c), IND(R("ZAB", 0, 1537), nl))
                act(sub(yb, *c), IND(R("ZAB", SIDE, SIDE + 1537), nl))
                tt(sub(zb, *c), IND(R("NT", 0, 1537), nl), sub(yb, *c), A.mult)
                ts(sub(mn, *c), sub(za, *c), 0.0, A.min)
        if st == 0:
            offer("XN", R("NXF", 96, 128), R("NXF", 224, 256))
        if st == 1:
            act(a512("KTG"), IND(R("KT", 0, 1537), c32("NL")))
            phases(c32("P7"), "ZAD", a512("KTG"), True, True, 4)
            cp(c32("KA"), c32("P7"))
        if st == 2:
            mm(c64("P7"), a128("I4"), c64("ONE"), True, False)
            phases(c64("P7"), "ZM8", R("AB", 512, 1536), False, True, 4)
            tt(c64("NS"), c64("ES"), c64("P7"), A.add)
            mms([(a512("P7"), a128("E2"), a512("LLO"), True, False), (a512("P7"), a128("E3"), a512("LHI"), False, False)])
        for h, c in enumerate(HALF):
            PD, EA, PA = a256("P%d" % h), R("P%d" % h, 256, 512), a256("P%d" % (4 + h))
            PB, EB = a256("P%d" % (2 + h)), R("P%d" % (2 + h), 256, 512)
            d, wa, wb = sub(D, *c), R("WAB", *c), sub(R("WAB", 512, 0), *c)
            mm(PD, I, d, True, True)
            tt(R("CB", *c), sub(za, *c), PD, A.is_gt)
            mm(PB, I, d, True, False)
            mm(PB, I, sub(mn, *c), False, False)
            mm(PB, a128("N256"), R("CB", *c), False, True)
            act(wb, PB, F.Relu)
            mm(EB, NI, sub(yb, *c), True, False)
            mm(EB, I, wb, False, True)
            act(sub(ab, *c), EB, F.Abs)
            tt(R("SA", *c), sub(yb, *c), PD, A.is_le)
            mm(PA, I, d, True, False)
            mm(PA, NI, sub(zb, *c), False, True)
            tt(wa, R("SA", *c), PA, A.mult)
            mm(EA, NI, sub(za, *c), True, False)
            mm(EA, a128("I2"), sub(mn, *c), False, False)
            mm(EA, I, wa, False, True)
            act(R("AB", *c), EA, F.Abs)
        if st == 1:
            ts(c32("KA", 1), c32("KA"), 2047, A.bitwise_and)
            ts(c32("KA", 2), c32("KA"), 11, A.arith_shift_right)
            offer("XN", c32("KA", 1), c32("KA", 2))
        dif = part("P6", 2)
        mm(a96("P6"), I, a96("C4"), True, False)
        phases(dif, "ZMN", sub(ab, 0, 512), False, False)
        phases(dif, "ZMK", a512("AB"), False, True)
        ts(c32("ES", st), dif, 8.0 / BIG, A.mult, -4.0, A.min)
        if st == 2:
            chain(phases(c64("P0"), "ZW1", R("WAB", 0, 1024), True, True), phases(R("P4", 256, 320), "ZW2", R("WAB", 0, 1024), True, True))
            ts(R("UI", 64, 128), c64("P0"), 32.0, A.add)
            cp(c64("UI"), c64("P0"))
            tt(c64("PRI"), R("UI", 64, 128), R("P4", 256, 320), A.mult)
            ts(c64("UMI"), c64("UI"), 127, A.bitwise_and)
            ts(c64("SHI"), c64("PRI"), 5, A.arith_shift_right, 1023, A.bitwise_and)
            ts(part("XH", 2), c32("SHI", 1), 1025.0, A.add)
            ts(part("XH", 3), c32("SHI"), -1.0, A.mult, -1.0, A.add)
            ts(c64("UA"), c64("UMI"), 2.0, A.mult, 2.0, A.add)
            ts(c64("UN"), c64("UMI"), -2.0, A.mult, -2.0, A.add)
            offer("XH", c32("UA"), c32("UA", 1), 1, (c32("UN"), c32("UN", 1)))
            for k in range(2):
                choose("OH", "XH", k)
            ts(c32("CU"), part("OH", 3), -1.0, A.mult, -1.0, A.add)
            ts(c64("H16"), R("OH", 2, 192, 3), -1.0, A.mult, -1.0, A.add)
        if st < 2:
            choose("ON", "XN")
            ts(c32("NL"), part("ON", 3), -1.0, A.mult, -1.0, A.add)
            ts(c32("CH%d" % st), part("ON", 3), -1.0, A.mult, -1.0, A.add)
        choose("OS", "XS")
        ts(c32("SEL"), part("OS", 3), -1.0, A.mult, -1.0, A.add)
        for c in HALF:
            act(R("DB" if st == 1 else "DA", *c), IND(R("WAB", 0, 1024), R("SEL", c[0] // 16, c[1] // 16)))
        was = c32("CH%d" % ((st + 2) % 3))
        ts(c32("T2"), dif, 0.0, A.is_gt, float(SIDE), A.mult)
        if st == 0:
            tt(c32("ST"), c32("T2"), was, A.add)
        else:
            ts(c32("LV", st - 1), was, 1.0, A.is_lt)
            tt(c32("DS"), c32("ST"), c32("LV", st - 1), A.mult)
            tt(c32("DT"), c32("DS"), was, A.add)
            tt(c32("ST"), c32("T2"), c32("DT"), A.add)
            if st == 2:
                cp(c32("KEYU"), c32("ST"))
                ts(c32("KI"), c32("ST"), -1.0, A.add)
        if st == 2:
            cp(c32("LW"), c32("LV"))
            tt(c32("LW", 1), c32("LV", 1), c32("LV"), A.subtract)
            ts(c32("LW", 2), was, 1.0, A.is_ge)
            mm(c32("P3"), a128("I4"), c32("ONE"), True, False)
            phases(c32("P3"), "ZM8", R("AB", 1536, 2048), False, True, 4)
            tt(c32("NS", 2), c32("ES", 2), c32("P3"), A.add)
            tt(a96("NW"), a96("NS"), a96("LW"), A.mult)
            tt(c32("DS", 1), c32("NW"), c32("NW", 1), A.add)
            tt(c32("ST", 1), c32("DS", 1), c32("NW", 2), A.add)

    BY_S, RELU = (1, 2, 3), (4, 5, 6, 7)

    LISTS = (("P4", (1, 2, 3)), ("P1", (4, 5, 6, 7)))

    def send(k, to, what, late):
        dst = T.cores[(rank + 1) % n_ranks]
        rid, pid, _ = topo.addr(dst)
        emit("G", lambda: g.remote_dma(ap(to), ap(what), T.sem["arr%d" % k], T.sem["snt%d" % k], pid, rid, topo.mask(core, dst)),
             [what], [R("sent", k, k + 1)], 500.0, False, late)

    def donors(t):
        n = LIB if t == 0 else 128
        for k in range(4):
            dma("Y", ap(R("LT4", LIB * k, LIB * k + n)), ap(R("YT", H, H + n)), [R("YT", H, H + n)], [R("LT4", LIB * k, LIB * k + n)])
        D = a512("DA")
        SL, SLOT = "SL%d" % t, "SLOT%d" % t
        yc = act(a512("YC%d" % t), IND(R("ZAB", 0, SIDE + 2049), c32("KEYU")), F.Abs)
        send(2 * t, a512("YIN%d" % t), a512("YC%d" % t), 6500.0 if t else 13500.0)
        ts(c32("QCI"), c32("KI"), 15, A.bitwise_and)
        ts(c32("QCI", 1), c32("KI"), 4, A.arith_shift_right)
        cp(c64("QCH"), c64("QCI"))
        hh, stride = c32("H16"), c32("H16", 1)
        for P, some in LISTS:
            mms([(c32(P, m - some[0]), I if m == 1 else a128("I%d" % m), stride, m == some[0], False) for m in some])
            mms([(c32(P, m - some[0]), I, hh, False, m == some[-1]) for m in some])
            cp(R("CU", 32 * some[0], 32 * some[-1] + 32), R(P, 0, 32 * len(some)))
        ts(a128(SL), a128("LLO"), col("Q2"), A.mult, col("QI"), A.add)
        LW = R("LT4", 0, 4 * LIB)
        df = lambda m, b="DF", n=1: R(b, 512 * m, 512 * (m + n))
        banks = {1: "P0", 2: "P1", 3: "P4"}
        to_row("P7", 0, c32("QCH"), False, False)
        to_row("P7", 1, c32("QCH", 1), False, True)
        act(a512("PAY"), a512("P7"), scale=1.0 / 256)
        got, size = {0: yc}, {}
        for m in range(8):
            if m in BY_S:
                k = BY_S.index(m)
                got[m] = act(df(k, "GV"), IND(LW, c32("CU", m)))
                mm(a512(banks[m]), NI, D, True, False)
                mm(a512(banks[m]), I, df(k, "GV"), False, True)
                size[m] = act(df(m), a512(banks[m]), F.Abs, scale=0.5)
            elif m in RELU:
                got[m] = tt(df(RELU.index(m), "DD"), IND(LW, c32("CU", m)), D, A.subtract)
                size[m] = ts(df(m), df(RELU.index(m), "DD"), 0.0, A.max)
            else:
                for c in HALF:
                    tt(sub(df(m), *c), IND(LW, R("CU", c[0] // 16, c[1] // 16)), sub(D, *c), A.subtract)
                size[m] = act(df(m), df(m), F.Abs, scale=0.5)
        chain(yc, got[2])
        chain(size[4], got[6])
        chain(size[5], got[7])
        for P, m, n in (("P2", 0, 2), ("P3", 4, 2), ("P5", 6, 2), ("P6", 2, 2)):
            mm(R(P, 0, 32 * n), I, R("MC", 32 * m, 32 * (m + n)), True, False)
            for k in range(0, n, 2):
                if m + k in RELU:
                    phases(R(P, 32 * k, 32 * k + 64), "ZN8", df(RELU.index(m + k), "DD", 2), False, False)
                mark["sums"] = phases(R(P, 32 * k, 32 * k + 64), "ZM16", df(m + k, "DF", 2), False, k == n - 2)
        act(c64("B1"), c64("P3"))
        tt(c64("B2"), c64("B1"), c64("P2"), A.min)
        tt(c64("B3"), c64("B2"), c64("P5"), A.min)
        tt(c64("B4"), c64("B3"), c64("P6"), A.min)
        tt(c32("BEST"), c32("B4"), c32("B4", 1), A.min)
        tt(c32("HIT"), c32("BEST"), c32("ST", 1), A.is_lt)
        emit("V", lambda: g.vector.tensor_tensor_scan(ap(c32("INC")), ap(c32("ONE")), ap(c32("HIT")), 0.0, A.mult, A.add),
             [c32("ONE"), c32("HIT")], [c32("INC")], vcost(c32("INC")))
        tt(c32("HL"), c32("HIT"), c32("NL512"), A.mult)
        mm(c32("P6"), I, c32("L512"), True, False)
        mm(c32("P6"), a128("LB"), c32("HIT"), False, False)
        mm(c32("P6"), a128("BD"), c32("INC"), False, False)
        mm(c32("P6"), I, c32("HL"), False, True)
        cp(c32(SLOT), c32("P6"))
        if t in BY_SLOT:
            send(2 * t + 1, c32("LIN%d" % t), c32(SLOT), 3600.0)
        ts(c32("MI"), c32("BEST"), 7, A.bitwise_and)
        tt(c32("MTT"), c32("MI"), stride, A.mult)
        tt(c32("HD"), c32("MTT"), hh, A.add)
        ts(c32("DNI"), c32("HD"), 1023, A.bitwise_and)
        dn = cp(c32("DNH"), c32("DNI"))
        to_row("P4", 0, c32("DNH"), True, True)
        act(a512("DR"), a512("P4"), scale=1.0 / 256)
        chain(dn, cp(IND(R(SL, 0, 1536), c32(SLOT)), a512("PAY")))

    def grafts(t):
        at = lambda gr, w=128: (w * gr, w * gr + w)
        XH, LL = a128("SL%d" % t), R("LL%d" % t, 0, 8)
        for h in range(2):
            chain(mark["sums"], mms([(R("P%d" % h, *at(k)), a128("N256"), a128("TRI"), k == 0, False) for k in range(4)]))
        mm(a128("P2"), I, a128("IQN"), True, False)
        diff = lambda h: mms([(a512("P%d" % h), XH, R("NBC", *at(h, 512)), False, False)]
                             + [(R("P%d" % h, *at(k)), R("BC", *at(4 * h + k)), XH, False, k == 3) for k in range(4)])
        lanes = lambda: phases(R("P7", 0, 8), "ZR2", XH, True, True)
        column = lambda: mm(R("P6", 0, 8), XH, R("SEL1", 0, 8), True, True)
        if t in BY_SLOT:
            chain(column(), diff(0), lanes(), diff(1))
        else:
            chain(lanes(), column(), diff(0), diff(1))
        cp(LL, R("P7", 0, 8))
        if t not in BY_SLOT:
            send(2 * t + 1, R("LIN%d" % t, 0, 8), LL, 3600.0)
        ts(R("XF", 0, 8), R("P6", 0, 8), -MID, A.add)
        mark["donors"] = act(a128("DG"), IND(R("DR", 0, 640), LL), scale=-1.0, bias=col("CMID"))
        mm(a128("P4"), a128("DG"), a128("RQ"), True, True)
        mms([(R("P6", *at(k)), I, a128("ONE"), k == 0, False) for k in range(2)])
        mm(a128("P2"), XH, a128("RQ"), False, True)
        ts(R("WN", 896, 1024), a128("P2"), 0.0, A.is_equal, -1.0, A.mult)
        tt(R("WZ", 896, 1024), R("WN", 896, 1024), a128("P4"), A.mult)
        for gr in range(8):
            P, near = R("P%d" % (gr // 4), *at(gr % 4)), col("XF", 8 + gr)
            emit("V", lambda P=P, near=near: g.vector.tensor_reduce(ap(near), ap(P), AX.X, A.min, apply_absolute_value=True), [P], [near], vcost(P, P))
            ts(R("CHM", *at(gr, 256)), a256("IOC"), col("XF", gr), A.is_equal, near, A.min)
            o = 896 - 127 * gr
            mm(a256("P6"), R("WN", o, o + 1017, 8), R("CHM", *at(gr, 256)), False, gr == 7)
            mm(a256("P5"), R("WZ", o, o + 1017, 8), R("CHM", *at(gr, 256)), gr == 0, gr == 7)
        for c in ((0, 160), (160, 256)):
            tt(R("ZT", *c), R("WF", *c), R("P6", *c), A.mult)
            tt(R("WF", *c), R("ZT", *c), R("P5", *c), A.add)
            ts(R("UL", *c), R("WF", *c), MID + H, A.add)

    def receive(t):
        n = len(topo.engines(T.cores[(rank - 1) % n_ranks], core))
        Y, L, W, lib = a512("YIN%d" % t), c32("LIN%d" % t), R("YW", 0, 1536), R("YT", H + 128 * t, H + 128 * t + 128)
        if t not in BY_SLOT:
            L = R("LIN%d" % t, 0, 8)
            act(R(Y[0], 512, 640), lib, also=[a512("PAY")])
            for k, r in ((2 * t, Y), (2 * t + 1, L)):
                emit("S", lambda k=k: g.scalar.wait_ge(T.sem["arr%d" % k], n), [R("sent", k, k + 1), a128("DG")], [r], 1.0, False)
            return act(lib, IND(R(Y[0], 0, 640), L))
        act(a128("YL"), lib, bias=col("CUP"))
        calls[act(a128("YW"), a128("YL"), F.Silu, also=[R("LL0", 0, 8)])]["cost"] += TABLE
        for k, r in ((2 * t, Y), (2 * t + 1, L)):
            emit("S", lambda k=k: g.scalar.wait_ge(T.sem["arr%d" % k], n), [R("sent", k, k + 1), a128("DG") if r == L else a512("PAY")], [r], 1.0, False)
            if r == Y:
                chain(act(a512("YF"), Y, bias=col("CUP")), mark["donors"])
        emit("S", lambda: g.scalar.activation(ap(IND(W, L)), ap(a512("YF")), F.Silu), [a512("YF"), L], [W], 65 + SCATTER * 512)
        ts(lib, a128("YW"), ROUND, A.add, -ROUND - UP, A.add)

    def out(lo, hi, src):
        dma("Y", T.yo[:, lo:hi], ap(src), [src], [])

    def last_levels():
        yo = lambda l: R("YO", 512 * l, 512 * l + 512)
        out(0, 1536, R("YT", H, H + 1536))
        for k in range(8):
            mms([(R("P4", 32 * k + 16 * x, 32 * k + 16 * x + 16), a128("L%d%d" % (x, c2)), R("WF", 2 * k + c2, 256, 16), c2 == 0, c2 == 1)
                 for x in range(2) for c2 in range(2)])
        act(a256("KOF"), a256("P4"), bias=col("CMID"))
        vtr(a256("KOT"), a256("KOF"))
        dma("Y", T.ko[:, :], ap(a256("KOT")), [a256("KOT")], [])
        for l in range(3):
            level(l, yt(l), False)
            ts(yo(l), yt(l), 255.0, A.min)
            out(1536 + 512 * l, 2048 + 512 * l, yo(l))
        level(3, yo(3), True)
        for a, b in HALF:
            out(3072 + a, 3072 + b, sub(yo(3), a, b))

    load_lists()
    for t in range(2):
        levels()
        for st in range(3):
            step(st)
        donors(t)
        grafts(t)
        receive(t)
    last_levels()

    if not ORDER:
        ORDER.extend(arrange(calls))
    cnt = {}
    seen = {q: {} for q in ENG}
    clocks = {}

    def wait(q, sem, n):
        if seen[q].get(sem, 0) < n:
            ENG[q].wait_ge(T.sem[sem], n)
            for k, v in clocks[(sem, n)].items():
                seen[q][k] = max(seen[q].get(k, 0), v)

    for k in ORDER:
        c = calls[k]
        need = {}
        for d, by_sem in c["deps"].items():
            if by_sem:
                sem, n = calls[d]["done"]
                need[sem] = max(need.get(sem, 0), n)
        for sem in sorted(need, key=lambda s: -sum(clocks[(s, need[s])].values())):
            wait(c["q"], sem, need[sem])
        sem = c["sem"]
        for fn in c["fns"]:
            ins = fn()
            if sem:
                inc = 16 if sem[0] == "d" else 1
                ins.then_inc(T.sem[sem], inc)
                cnt[sem] = cnt.get(sem, 0) + inc
        if sem:
            c["done"] = (sem, cnt[sem])
            clocks[c["done"]] = dict(seen[c["q"]], **{sem: cnt[sem]})

    for s in sorted(cnt, key=lambda s: (s[0] == "d", len(s), s)):
        wait("G", s, cnt[s])
    dst = T.cores[(rank + 1) % n_ranks]
    for t in range(4):
        g.wait_ge(T.sem["snt%d" % t], len(topo.engines(core, dst)))
